import numpy as np, ml_dtypes
CORES = [16,17,18,19,32,33,34,35]
N = 8
BF = ml_dtypes.bfloat16
def gentries(a):
    return np.ascontiguousarray(a.reshape(8, 16, -1).transpose(0, 2, 1)).reshape(8, -1)
def gtable(e):
    e = np.asarray(e); return np.ascontiguousarray(e.reshape(8, -1, 16).transpose(0, 2, 1)).reshape(128, -1).astype(np.int32)
V, H, K, P, D, ST, E, TH, CL = 1024, 256, 3, 2, 2, 5, 3, 9, 2
M = V + 2 * H
KV = K * V
def parts(rng):
    src = np.argsort(rng.random((N, 8, KV)), axis=-1); snd = np.argsort(rng.random((N, 8, V)), axis=-1)[..., :2 * H]
    dl = rng.integers(1, D + 1, (N, 8, KV)); wi = rng.integers(0, 65, (N, 8, 16, KV))
    dr = np.clip(rng.integers(-32, 81, (N, 8, 1, V)) + rng.integers(-32, 33, (N, 8, 16, V)), -128, 128)
    lo = 0.125 + 0.875 * rng.random((N, 8, 16, V))
    return wi, dr, lo, src, dl, np.ascontiguousarray(snd)
def pack(wi, dr, lo, src, dl, snd):
    return {"w": (wi * 0.015625).reshape(N, 128, KV).astype(BF), "src": np.stack([gtable(a) for a in src]), "dly": np.stack([gtable(a) for a in dl]),
            "snd": np.stack([gtable(a) for a in snd]), "drive": (dr * 0.015625).reshape(N, 128, V).astype(BF), "loss": lo.reshape(N, 128, V).astype(BF)}
def put(row, slots, ports):
    for s, p in zip(slots, ports):
        a = int(np.flatnonzero(row == p)[0]); row[a], row[s] = row[s], row[a]
def setup_inputs(rng):
    return pack(*parts(rng))
def setup_inputs_spread(rng):
    wi, dr, lo, src, dl, snd = parts(rng)
    wi = np.rint(wi * np.exp2(-1.0 * rng.integers(0, 3, (N, 8, 1, KV)))).astype(np.int64)
    dr = np.clip(rng.integers(-64, 113, (N, 8, 1, V)) + rng.integers(-24, 25, (N, 8, 16, V)), -128, 128)
    lo = (0.25 + 0.75 * rng.random(lo.shape)) * np.exp2(1.0 * rng.integers(-1, 2, (N, 8, 1, V)))
    return pack(wi, dr, lo, src, dl, snd)
def setup_inputs_ends(rng):
    wi, dr, lo, src, dl, snd = parts(rng)
    kind = rng.integers(0, 8, (N, 8, V)); kind[..., :4] = 0; kind[..., V - 4:] = 0; kind[..., V // 2] = 2
    kk = kind[:, :, None, :]; wk = np.tile(kk, (1, 1, 1, K)); pm = np.where(rng.random(wi.shape) < 0.5, 0, 64)
    wi = np.where((wk < 2) | (wk == 5), 64, np.where(wk == 2, 0, np.where(wk < 5, pm, wi)))
    dr = np.where((kk < 2) | (kk == 3) | (kk == 4), 128, np.where((kk == 2) | (kk == 5), -128, dr))
    lo = np.where(rng.random(lo.shape) < 0.85, np.where(rng.random(lo.shape) < 0.4, 2.0, 0.125), lo)
    dl = np.where(rng.random(dl.shape) < 0.5, 1, D)
    low = np.concatenate([np.arange(H), np.arange(V - H, V)]); snd = low[np.argsort(rng.random(snd.shape), axis=-1)]
    on = [0, V - 1, 1, V - 2][:K]; last = [k * V + V - 1 for k in range(K)]; mid = [k * V + V // 2 for k in range(K)]
    on2 = [2, V - 3, 3, V - 4][:K]; near = [k * V + V // 4 for k in range(K)]
    for q in range(N):
        for g in range(8):
            put(src[q, g], last, on); put(src[q, g], mid, [c + M for c in on]); dl[q, g, last] = 1; dl[q, g, mid] = 1
            put(src[q, g], near, on2); dl[q, g, near] = 1
            dd = np.where(rng.random(16) < 0.5, -128, rng.integers(-127, -64, 16)); dd[15] = -128; dr[q, g, :, V // 4] = dd
            for k in range(K): wi[q, g, :, near[k]] = (63 - dd + k) // K
    return pack(wi, dr, lo, src, dl, snd)
def setup_inputs_corners(rng):
    wi, dr, lo, src, dl, snd = parts(rng)
    for q in range(N):
        for g in range(8):
            c = (g + q) % 8
            if c == 0: src[q, g] = np.arange(KV); dr[q, g, :, 0] = 128; dr[q, g, :, V - 1] = 128
            if c == 1: src[q, g] = np.arange(KV)[::-1]; dl[q, g] = np.where(np.arange(KV) % 2 == 0, 1, D)
            if c == 2: dl[q, g] = 1
            if c == 3: dl[q, g] = D
            if c == 4: wi[q, g] = 0; dr[q, g] = rng.choice(np.array([32, 36, 40, 44, 48, 64, 80]), (16, V))
            if c == 5: dr[q, g] = 128
            if c == 6:
                half = rng.random((1, V)) < 0.5; dr[q, g] = np.where(half, -128, np.minimum(dr[q, g] + 48, 128)); wi[q, g] = np.minimum(wi[q, g], np.where(np.tile(half, (1, K)), 32, 16))
            if c == 7:
                place = rng.permutation(16)[:, None]; m = np.where(rng.random((1, V)) < 0.5, TH, TH - 1)
                dr[q, g] = np.where(place < m, 128, -64); wi[q, g] = np.minimum(wi[q, g], 16); src[q, g] = np.roll(np.arange(KV), 1)
                snd[q, g] = np.arange(2 * H) if q % 2 == 0 else V - 1 - np.arange(2 * H)
    return pack(wi, dr, lo, src, dl, snd)
def setup_inputs_calm(rng):
    wi, dr, lo, src, dl, snd = parts(rng)
    place = rng.permutation(16)[:, None]; wi = np.rint(wi * 0.25).astype(np.int64)
    m = rng.choice(np.array([7, 8, 8, 9, 9, 10, 16]), (N, 8, 1, V)); m[:, 1::2] = rng.choice(np.array([0, 1, 2, 3, 16, 16]), (N, 4, 1, V))
    for q, g in ((0, 0), (N - 1, 7)):
        a, b, c = (q - 1) % N, (g - 1) % 8, (q + 1) % N
        m[q, g] = 16; m[a, b, 0, snd[a, b, :H]] = 16; m[c, g, 0, snd[c, g, H:]] = 16
    lo = np.where(rng.random(lo.shape) < 0.125, 0.125, 0.125 + 0.125 * rng.random(lo.shape))
    return pack(wi, np.where(place < m, 128, -64), lo, src, dl, snd)
def check_ranges(d):
    bad = []
    for k, lo, hi in (("w", 0, 1), ("drive", -2, 2), ("loss", 0.125, 2), ("src", 0, KV - 1), ("dly", 1, D), ("snd", 0, V - 1)):
        a = np.asarray(d[k], np.float64)
        if not (np.min(a) >= lo and np.max(a) <= hi): bad.append("range of " + k)
    for k in ("w", "drive"):
        a = np.asarray(d[k], np.float64) * 64
        if not np.all(a == np.rint(a)): bad.append("steps of " + k)
    if any(np.any(np.sort(gentries(a), axis=1) != np.arange(KV)) for a in d["src"]): bad.append("src is no permutation")
    if any(np.any(np.diff(np.sort(gentries(a), axis=1), axis=1) == 0) for a in d["snd"]): bad.append("snd repeats a neuron")
    return bad
def turned(a, n):
    return np.ascontiguousarray(np.asarray(a, np.float64).reshape(N, 8, 16, n).transpose(0, 1, 3, 2))
def rows(a, n):
    return np.ascontiguousarray(a.transpose(0, 1, 3, 2)).reshape(N, 128, n).astype(np.float32)
def reference(w, src, dly, snd, drive, loss):
    wt = turned(w, KV); dr = turned(drive, V); ls = turned(loss, V)
    port = np.stack([gentries(a) for a in src]).astype(np.int64); dl = np.stack([gentries(a) for a in dly]).astype(np.int64); sn = np.stack([gentries(a) for a in snd]).astype(np.int64)
    units = [(q, g) for q in range(N) for g in range(8)]; slot = np.arange(KV)
    gam = np.zeros((N, 8, KV, 16)); cnt = np.zeros((N, 8, V, 16))
    for e in range(E):
        ix = (D - dl) * M + port % M
        inv = np.argsort(port, axis=-1)
        jx = np.take_along_axis((dl - 1) * V + slot % V, inv, axis=-1)
        wp = np.take_along_axis(wt, inv[..., None], axis=2)
        spk = np.zeros((N, 8, ST + D, M, 16), np.float32)
        slope = np.zeros((N, 8, ST, V, 16), np.float32); u = np.zeros((N, 8, V, 16)); gain = np.zeros((N, 8, KV, 16), np.float32)
        for t in range(ST):
            for q, g in units:
                x = spk[q, g, t:t + D].reshape(D * M, 16)[ix[q, g]]
                cur = dr[q, g] + np.add.reduce((wt[q, g] * x).reshape(K, V, 16), axis=0)
                v = 0.5 * u[q, g] + cur; s = (v >= 1).astype(np.float32)
                u[q, g] = np.where(v >= 1, 0.0, v); spk[q, g, t + D, :V] = s; cnt[q, g] += s
                slope[q, g, t] = np.where(cur < 0.75, 2.0, np.where(cur < 1.25, 1.0, 0.5))
                gain[q, g] += (x.reshape(K, V, 16) * (2 * s - 1)).reshape(KV, 16)
            for q, g in units:
                spk[(q + 1) % N, (g + 1) % 8, t + D, V:V + H] = spk[q, g, t + D, sn[q, g, :H]]
                spk[(q - 1) % N, g, t + D, V + H:] = spk[q, g, t + D, sn[q, g, H:]]
        lam = np.zeros((N, 8, ST + D, V, 16)); part = np.zeros((N, 8, M, 16))
        for t in range(ST - 1, -1, -1):
            for q, g in units:
                z = wp[q, g] * lam[q, g, t + 1:t + 1 + D].reshape(D * V, 16)[jx[q, g]]
                part[q, g] = np.add.reduce(z.reshape(P, M, 16), axis=0)
            for q, g in units:
                j = part[q, g, :V] + ls[q, g]
                j[sn[q, g, :H]] += part[(q + 1) % N, (g + 1) % 8, V:V + H]; j[sn[q, g, H:]] += part[(q - 1) % N, g, V + H:]
                s = spk[q, g, t + D, :V]
                y = np.minimum((1 - s) * (0.5 * lam[q, g, t + 1]) + s * (slope[q, g, t] * j), CL); lam[q, g, t] = y
                x = spk[q, g, t:t + D].reshape(D * M, 16)[ix[q, g]]
                gam[q, g] += (x.reshape(K, V, 16) * y).reshape(KV, 16)
        if e < E - 1:
            eager = np.add.reduce((gain > 0).astype(np.int64), axis=3) >= TH
            mate = slot ^ (1 << e)
            port = np.where(eager & eager[..., mate], port[..., mate], port)
    return {"lam": rows(lam[:, :, 0], V), "gam": rows(gam, KV), "cnt": rows(cnt, V)}

def check_inputs(d):
    bad = list(check_ranges(d))
    if not bad:
        for name, y in reference(**d).items():
            for q in range(N):
                v = np.abs(np.asarray(y[q], np.float64)); s = np.sqrt(np.mean(v * v))
                if v.max() > 13 * s or s < 2.0 ** -5: bad.append('%s of rank %d is uneven or too small' % (name, q))
    return bad

@@ -1,0 +1,784 @@
+import math
+from concourse.bass import DstId, RemoteDMATransfer
+from concourse.mybir import AluOpType as ALU, ActivationFunctionType as ACT
+
+V, H, KV, M = 1024, 256, 3072, 1536
+SW = M + 16
+SO = SW - V
+ZW = KV + 8
+RW = 64 + 2 * H
+EPS = 2.0 ** -30
+SC = [8.0, 4.0, 2.0, 1.0, -1 / 64, -1 / 32, -1 / 16, -1 / 8, -1 / 4, -1 / 2, 1 / 2, 1 / 4, 1 / 8, 1 / 16]
+RA = False
+
+F32, BF, I32, U16, F16 = "float32", "bfloat16", "int32", "uint16", "float16"
+_SB = {
+    "wt": (4 * KV, BF), "yb": (10 * KV, BF), "zz": (2 * ZW, F32), "acc": (KV, F32), "rc": (KV, F32),
+    "sp": (9 * SW - 2 * SO, BF), "aa": (9 * V, BF), "zg": (KV, F32), "rg": (V, F32), "rl": (2 * RW, F32),
+    "sb": (H, F32), "sg": (2 * H, BF), "sf": (H, BF), "cap": (V, F32), "mm": (V, F32 if RA else F16), "qq": (V, BF),
+    "dr": (V, BF), "ls": (V, BF), "cn": (V, BF), "one16": (512, BF),
+    "ii32": (256, F32), "ii16": (256, BF), "ids": (128 * len(SC), BF), "hf16": (128, F32 if RA else F16),
+    "h32": (144, F32), "h16": (144, BF), "pd32": (256, F32), "pp16": (256, BF), "pd16": (256, BF),
+    "srci": (192, I32), "dlyi": (192, I32), "sndi": (32, I32), "ioi": (192, I32), "mki": (16, I32), "cli": (4, I32),
+    "mk": (16, F32), "clf": (4, F32), "srcf": (192, F32), "fd": (192, F32), "fa": (192, F32), "t1": (192, F32),
+    "t2": (192, F32), "t3": (192, F32), "t4": (224, F32), "slot": (192, F32), "e1": (192, F32),
+    "swp": (192, F32), "eag": (192, BF), "x8": (192, BF), "cod": (192, BF),
+    "lt1": (192, U16), "lg": (192, U16), "lp": (192, U16), "lsn": (32, U16), "lr": (64, U16), "lbs": (192, U16),
+    "lba": (384, U16), "lbb": (384, U16), "lb3": (384, U16),
+}
+_PS = {"pv": 1024, "pk": 1024, "pl": 1024, "px0": 512, "px1": 512}
+SCRATCH = {k: ("sbuf", [128, n], d) for k, (n, d) in _SB.items()}
+SCRATCH.update({k: ("psum", [128, n], F32) for k, n in _PS.items()})
+NDMA, NREM = 60, 20
+SEMAPHORES = ["cv", "ca", "cp", "cg"] + ["d%d" % i for i in range(NDMA)] + ["ar%d" % i for i in range(NREM)] + ["lo%d" % i for i in range(NREM)]
+SEMAPHORES += ["ha%d" % i for i in range(8)] + ["hl%d" % i for i in range(8)]
+_HBM = ("w", "drive", "loss", "src", "dly", "snd", "lam", "gam", "cnt")
+
+COST = dict(cyc=1.0, gat=1.56, sca=3.5, pe=0.52, vfix=60, afix=90, pfix=25, wake=120, same=50, c16=1.0,
+            dissue=900, hissue=60, dlat=2000, dbw=550.0, rissue=400, rlat=2400, slack=120)
+OPT = dict(nt=1, tail="vvv", seed=0, iters=5000, split=3, own="ppp", s_mode=["v", "aa", "v"], wt_eng="vvaa", fold=[(), ()],
+           sig="p", ysplit=[0, 0, 0], afix="vvv", rps=True,
+           sc_eng="aaaaava")
+
+
+def A(name, lo=0, hi=None, step=1):
+    if hi is None:
+        hi = _SB[name][0] if name in _SB else _PS[name]
+    return (name, lo, hi, step)
+
+
+def IND(win, off):
+    return ("@", win, off)
+
+
+def _n(a):
+    if a[0] == "@":
+        return 16 * _n(a[2])
+    return (a[2] - a[1] + a[3] - 1) // a[3]
+
+
+def _dt(a):
+    if a[0] == "@":
+        return _dt(a[1])
+    return _SB[a[0]][1] if a[0] in _SB else F32
+
+
+def _isap(a):
+    return isinstance(a, tuple)
+
+
+def _parts(a):
+    return [a[1], a[2]] if a[0] == "@" else [a]
+
+
+def _ap(T, a):
+    if not _isap(a):
+        return a
+    if a[0] == "@":
+        return _ap(T, a[1]).indirect(_ap(T, a[2]))
+    return T[a[0]][:, a[1]:a[2]] if a[3] == 1 else T[a[0]][:, a[1]:a[2]:a[3]]
+
+
+def build_ops(C, O):
+    ops = []
+
+    def add(eng, kind, args, outs, ins, dur, lat=0.0, dby=0.0):
+        rd, wr = [], []
+        for a in ins:
+            if _isap(a):
+                rd += _parts(a)
+        for a in outs:
+            if a[0] == "@":
+                wr.append(a[1]); rd.append(a[2])
+            else:
+                wr.append(a)
+        ops.append(dict(eng=eng, kind=kind, args=args, rd=rd, wr=wr, dur=dur, lat=lat, dby=dby))
+
+    def vdur(out, ins, two):
+        n = _n(out)
+        if out[0] == "@":
+            return C["vfix"] + n * C["sca"] * C["cyc"]
+        if any(a[0] == "@" for a in ins):
+            return C["vfix"] + n * C["gat"] * C["cyc"]
+        narrow = all(_dt(a) in (BF, F16, U16) for a in [out] + ins)
+        f = (2.0 if two and all(a[0] in _SB for a in ins) else 1.0) * (0.5 if narrow else 1.0)
+        if two and narrow:
+            f = C["c16"]
+        return C["vfix"] + max(64, n * f) * C["cyc"]
+
+    def tt(out, a, b, op):
+        add("v", "tt", (out, a, b, op), [out], [a, b], vdur(out, [a, b], True))
+
+    def ts(out, a, s1, op0, s2=None, op1=None):
+        add("v", "ts", (out, a, s1, s2, op0, op1), [out], [a, s1, s2], vdur(out, [a], False))
+
+    def cp(out, a):
+        add("v", "cp", (out, a), [out], [a], vdur(out, [a], False))
+
+    def ms(out, c):
+        add("v", "ms", (out, c), [out], [], vdur(out, [], False))
+
+    def act(out, a, func, bias=0.0, scale=1.0, extra=0.0):
+        n = _n(out)
+        f = C["sca"] if out[0] == "@" else C["gat"] if a[0] == "@" else 1.0
+        add("a", "act", (out, a, func, bias, scale), [out], [a, bias, scale], C["afix"] + max(64, n * f) * C["cyc"] + extra)
+
+    def gat(eng, out, win, off):
+        if eng == "a":
+            act(out, IND(win, off), ACT.Copy)
+        else:
+            cp(out, IND(win, off))
+
+    def mm(out, lhs, rhs, start, stop):
+        f = 4 if _dt(rhs) == F32 else 1
+        add("p", "mm", (out, lhs, rhs, start, stop), [out], [lhs, rhs], C["pfix"] + max(64, _n(rhs)) * f * C["pe"])
+
+    def group(out, terms, first=True, last=True):
+        for i, (l, r) in enumerate(terms):
+            mm(out, l, r, first and i == 0, last and i == len(terms) - 1)
+
+    def dma(eng, out, a, acc=False):
+        by = _n(out) * 128 * (2 if _dt(out) == BF else 4)
+        add(eng, "dma", (out, a, acc), [out], [a, out] if acc else [a], C["dissue"] if eng == "g" else C["hissue"],
+            C["dlat"], by * (2 if acc else 1) / C["dbw"])
+
+    def rem(tr):
+        add("g", "rem", tr, [t[2] for t in tr], [s for t in tr for s in t[1]], C["rissue"], C["rlat"] - 600.0, 600.0)
+
+    def gp(kind, out, ins, args):
+        add("g", kind, args, [out], ins, 170 + 2 * _n(out) * C["cyc"])
+
+    def sel(out, a, pattern, op, base, cm):
+        gp("sel", out, [a], (out, a, pattern, op, 0.0, base, cm))
+
+    def iota(out, pattern, base, cm):
+        gp("iota", out, [], (out, pattern, base, cm))
+
+    def fill(out, c):
+        iota(out, [[0, _n(out)]], c, 0)
+
+    def ID(s):
+        i = SC.index(s)
+        return A("ids", 128 * i, 128 * i + 128)
+
+    def half(name, base, h):
+        return A(name, base + 512 * h, base + 512 * h + 512)
+
+    spos = lambda e, s: max(0, (4 + s if e % 2 == 0 else 4 - s) * SW - SO)
+    apos = lambda e, t: (0 if t == 0 else 4 * (e % 2) + t) * V
+    YB = [[0, 1, 2, 3], [4, 5, 6, 7], [2, 1, 0, 8]]
+    PB = [[4, 5, 6, 7], [8, 9, 3, 2]]
+    ypos = lambda e, t: YB[e][t - 1] * KV
+    I32F, SH32 = A("ii32", 0, 128), A("ii32", 16, 144)
+    SH16 = A("ii16", 112, 240)
+
+    def wrap(out, hbuf, src, base, n):
+        for i in range(16):
+            mm(out, A(hbuf, 15 - i, 143 - i), A(src, base + i, base + n, 16), i == 0, i == 15)
+
+    def send_spikes(e, s):
+        p = spos(e, s)
+        gat("a", A("sg"), A("sp", p, p + V), A("lsn"))
+        mm(A("px0", 0, H), SH16, A("sg", 0, H), True, True)
+        act(A("sf"), A("px0", 0, H), ACT.Copy)
+        rem([(1, [A("sf")], A("sp", p + V, p + V + H)), (-1, [A("sg", H, 2 * H)], A("sp", p + V + H, p + M))])
+
+    dma("s", A("dr"), A("drive", 0, V)); dma("a", A("sndi"), A("snd", 0, 32))
+    dma("s", A("srci"), A("src", 0, 192)); dma("a", A("dlyi"), A("dly", 0, 192))
+    for k in range(3):
+        dma("s", A("wt", 3 * KV + k * V, 3 * KV + k * V + V), A("w", k * V, k * V + V))
+    dma("a", A("ls"), A("loss", 0, V))
+    ms(A("pd32"), 1.0)
+    sel(A("ii32"), A("pd32"), [[0, 2], [-1, 128]], ALU.is_equal, 0, 1)
+    cp(A("ii16"), A("ii32"))
+    for s in SC:
+        act(ID(s), A("ii32", 0, 128), ACT.Identity, 0.0, s)
+    ts(A("hf16"), A("ii16", 0, 128), -0.5 if RA else 0.5, ALU.mult)
+    fill(A("one16"), 1)
+    for b in (4, 5, 6, 7, 3, 2, 1):
+        fill(A("sp", b * SW + M - SO, b * SW + SW - SO), 0)
+    cp(A("lsn"), A("sndi"))
+    p0 = spos(0, 0)
+    ts(A("sp", p0, p0 + V), A("dr"), 1.0, ALU.is_ge, 32.0, ALU.mult)
+    send_spikes(0, 0)
+    cp(A("lp"), A("srci"))
+    ts(A("t1"), A("srci"), 1536.0, ALU.is_ge, -1536.0, ALU.mult)
+    tt(A("srcf"), A("srci"), A("t1"), ALU.add)
+    ts(A("t2"), A("dlyi"), 1.0, ALU.subtract, float(SW), ALU.mult)
+    tt(A("fd"), A("srcf"), A("t2"), ALU.add)
+    ts(A("lt1"), A("fd"), float(M), ALU.min)
+    tt(A("fa"), A("srcf"), A("t2"), ALU.subtract)
+    ts(A("lg"), A("fa"), float(SW), ALU.add)
+    for t in (1, 2, 3, 4):
+        for k in range(3):
+            lo, hi = k * V, k * V + V
+            o, a, s = A("wt", (t - 1) * KV + lo, (t - 1) * KV + hi), A("wt", 3 * KV + lo, 3 * KV + hi), 2.0 ** (t - 4)
+            if O["wt_eng"][t - 1] == "v":
+                ts(o, a, EPS, ALU.max, s, ALU.mult)
+            elif O["wt_eng"][t - 1] == "d":
+                if k == 0:
+                    o, a = A("wt", (t - 1) * KV, t * KV), A("wt", (t - 2) * KV, (t - 1) * KV)
+                    dma("s", o, a)
+                    dma("g", o, a, True)
+            else:
+                act(o, a, ACT.Identity, EPS * s, s)
+    fill(A("h32"), 0)
+    sel(A("h32", 15, 144, 16), A("pd32", 0, 9), [[-16, 9]], ALU.is_ge, 0, 1)
+    sel(A("h32", 15, 144, 16), A("h32", 15, 144, 16), [[16, 9]], ALU.is_ge, 15, -1)
+    cp(A("h16"), A("h32"))
+    sel(A("pd32", 0, 128), A("pd32", 0, 128), [[-2, 64], [1, 2]], ALU.is_equal, -1, 1)
+    sel(A("pd32", 128, 256), A("pd32", 128, 256), [[-4, 32], [2, 2], [-1, 2]], ALU.is_equal, -2, 1)
+    tt(A("pp16"), A("pd32"), A("ii32"), ALU.add)
+    tt(A("pd32"), A("pd32"), A("ii32"), ALU.subtract)
+    cp(A("pd16"), A("pd32"))
+    iota(A("ioi"), [[16, 192]], 0, 1)
+    iota(A("mki"), [[-1, 16]], 16, 1)
+    ts(A("mki"), A("mki"), 15, ALU.bitwise_and)
+    ts(A("mk"), A("mki"), 0.0, ALU.is_equal)
+    ts(A("cli", 0, 1), A("ioi", 0, 1), 112, ALU.bitwise_and)
+    ts(A("cli", 1, 2), A("ioi", 0, 1), 15, ALU.bitwise_and)
+    cp(A("clf", 0, 2), A("cli", 0, 2))
+    ts(A("x8"), A("dlyi"), 8.0, ALU.mult, A("clf", 1, 2), ALU.add)
+    act(A("aa", 0, V), A("dr"), ACT.Identity, 16.0 * (195 - 1 / 64), -32.0)
+    ts(A("aa", 0, V), A("aa", 0, V), 192.0 * 16, ALU.subtract, 8.0, ALU.max)
+
+    def forward(e):
+        sm, th = O["s_mode"][e], 0.5 if RA else 1.0
+        if RA:
+            act(A("mm"), A("dr"), ACT.Relu, 1.0, -1.0)
+        else:
+            ts(A("mm"), A("dr"), 1.0, ALU.min)
+        for t in range(1, 5):
+            s = 2.0 ** (4 - t)
+            y, w = ypos(e, t), (t - 1) * KV
+            if t == 1:
+                win, lst = A("sp", p0, p0 + SW), "lt1"
+            else:
+                lo = min(spos(e, t - 1), spos(e, t - 2))
+                win, lst = A("sp", lo, lo + 2 * SW), "lg"
+            for h in range(2):
+                group(half("pv", 0, h), [(ID(1.0), half("dr", 0, h)), (ID(-2.0 ** (t - 7)), half("sp", spos(e, t - 1), h)),
+                                         (A("hf16"), half("mm", 0, h))], True, False)
+            for k in range(3):
+                yk, wk, lk = A("yb", y + k * V, y + k * V + V), A("wt", w + k * V, w + k * V + V), A(lst, 64 * k, 64 * k + 64)
+                if k < O["ysplit"][e]:
+                    gat("a", yk, win, lk)
+                    tt(yk, yk, wk, ALU.min)
+                else:
+                    tt(yk, IND(win, lk), wk, ALU.min)
+                for h in range(2):
+                    mm(half("pv", 0, h), ID(s), half("yb", y + k * V, h), False, k == 2)
+            p = spos(e, t)
+            a = apos(e, t)
+            for h in range(2):
+                if sm == "v":
+                    ts(half("sp", p, h), half("pv", 0, h), th, ALU.is_ge, 2.0 * s, ALU.mult)
+                else:
+                    act(half("qq", 0, h), half("pv", 0, h), ACT.Sign, 2.0 ** -12 - th)
+                    if sm == "av":
+                        ts(half("sp", p, h), half("qq", 0, h), s, ALU.mult, s, ALU.add)
+                    else:
+                        act(half("sp", p, h), half("qq", 0, h), ACT.Identity, s, s)
+            if t < 4:
+                send_spikes(e, t)
+                if RA:
+                    act(A("mm"), A("pv"), ACT.Relu, 0.5, -1.0)
+                else:
+                    ts(A("mm"), A("pv"), 1.0, ALU.min)
+            for h in range(2):
+                bank = A("px0") if t < 4 else A("px1")
+                terms = [(ID(1.0), half("dr", 0, h))] + [(ID(s), half("yb", y + k * V, h)) for k in range(3)]
+                group(bank, terms + ([(ID(4.0 / s), half("sp", p, h))] if t < 4 else []))
+                act(half("aa", a, h), bank, ACT.Identity, s * ((211 if t < 4 else 195) - 1 / 64), -2.0 * s)
+            if O["afix"][e] == "v":
+                ts(A("aa", a, a + V), A("aa", a, a + V), 192.0 * s, ALU.subtract, 0.5 * s, ALU.max)
+            else:
+                act(A("aa", a, a + V), A("aa", a, a + V), ACT.Relu, -192.5 * s)
+                act(A("aa", a, a + V), A("aa", a, a + V), ACT.Identity, 0.5 * s)
+            if e < 2 and t in O["fold"][e]:
+                b = PB[e][t - 1] * KV
+                add("g", "fold", (y, p, b), [A("yb", b, b + KV)], [A("yb", y, y + KV), A("sp", p, p + V)], C["rissue"],
+                    2 * C["rlat"] + 1.5e6 / C["dbw"], 2.4e6 / C["dbw"])
+            elif e < 2:
+                sig = A("pv") if O["sig"] == "p" else A("qq")
+                if sm == "v" or O["sig"] == "p":
+                    act(sig, A("pv"), ACT.Sign, 2.0 ** -12 - th)
+                b = PB[e][t - 1] * KV
+                for k in range(3):
+                    tt(A("yb", b + k * V, b + k * V + V), A("yb", y + k * V, y + k * V + V), sig, ALU.mult)
+
+    def diffs(e):
+        mm(A("px1", 0, 192), A("pd32", 128 * e, 128 * e + 128), A("srcf"), True, True)
+        mm(A("px1", 256, 448), A("pd16", 128 * e, 128 * e + 128), A("x8"), True, True)
+        act(A("t1"), A("px1", 0, 192), ACT.Copy)
+        act(A("t3"), A("px1", 256, 448), ACT.Copy)
+
+    def exchange(e):
+        vb = 8 * KV
+        banks = [A("px0"), half("pv", 0, 0), half("pv", 0, 1)] * 2
+        for c in range(6):
+            terms = []
+            for t in range(1, 5):
+                if t in O["fold"][e]:
+                    terms += [(ID(2.0 ** (1 - t)), half("yb", PB[e][t - 1] * KV, c)), (ID(-2.0 ** -t), half("yb", ypos(e, t), c))]
+                else:
+                    terms += [(ID(2.0 ** -t), half("yb", PB[e][t - 1] * KV, c))]
+            group(banks[c], terms)
+            act(half("yb", vb, c), banks[c], ACT.Sign, -EPS / 32)
+        wrap(A("pv", 0, 192), "h16", "yb", vb, KV)
+        ts(A("eag"), A("pv", 0, 192), 1.0, ALU.is_ge)
+        mm(A("pv", 512, 704), A("pp16", 128 * e, 128 * e + 128), A("eag"), True, True)
+        ts(A("swp"), A("pv", 512, 704), 1.5, ALU.is_ge)
+        tt(A("t1"), A("t1"), A("swp"), ALU.mult)
+        tt(A("fd"), A("fd"), A("t1"), ALU.add)
+        ts(A("lt1"), A("fd"), float(M), ALU.min)
+        tt(A("fa"), A("fa"), A("t1"), ALU.add)
+        if e == 0:
+            cp(A("lg"), A("fd"))
+            tt(A("srcf"), A("srcf"), A("t1"), ALU.add)
+        else:
+            ts(A("lg"), A("fa"), float(SW), ALU.add)
+        tt(A("cod"), A("t3"), A("swp"), ALU.mult)
+
+    def back_lists(e):
+        o = 192 * (e % 2)
+        tt(A("t2"), A("slot"), A("e1"), ALU.add)
+        cp(A("lba", o, o + 192), A("t2"))
+        ts(A("lb3", o, o + 192), A("t2"), float(KV), ALU.min)
+        tt(A("t4", 0, 192), A("slot"), A("e1"), ALU.subtract)
+        ts(A("lbb", o, o + 192), A("t4", 0, 192), float(ZW), ALU.add)
+        if e < 2:
+            cp(A("lbs"), A("slot"))
+
+    def invert():
+        ts(A("t2"), A("dlyi"), 4096.0, ALU.mult, A("clf", 0, 1), ALU.subtract)
+        tt(A("t4", 0, 192), A("ioi"), A("t2"), ALU.add)
+        ts(A("t4", 192, 224), A("ioi", 0, 32), A("clf", 0, 1), ALU.subtract, 64.0, ALU.add)
+        for i in range(16):
+            act(A("zz", i, 3584, 16), A("t4"), ACT.Identity, 0.0, A("mk", i, i + 1))
+        fill(A("rg"), 0)
+        for c in range(7):
+            dst = IND(A("zg"), A("lp", 32 * c, 32 * c + 32)) if c < 6 else IND(A("rg"), A("lsn"))
+            if O["sc_eng"][c] == "a":
+                act(dst, half("zz", 0, c), ACT.Silu, extra=1300 if "a" not in O["sc_eng"][:c] else 0)
+            else:
+                cp(dst, half("zz", 0, c))
+        wrap(A("px1", 0, 192), "h32", "zg", 0, KV)
+        cp(A("srci"), A("px1", 0, 192))
+        wrap(A("px1", 0, 64), "h32", "rg", 0, V)
+        cp(A("ioi", 0, 64), A("px1", 0, 64))
+        cp(A("lr"), A("ioi", 0, 64))
+        ts(A("ioi"), A("srci"), 4095, ALU.bitwise_and)
+        cp(A("slot"), A("ioi"))
+        ts(A("srci"), A("srci"), 12, ALU.logical_shift_right)
+        ts(A("e1"), A("srci"), 1.0, ALU.subtract, float(ZW), ALU.mult)
+        back_lists(0)
+        fill(A("zz", KV, ZW), 0); fill(A("zz", ZW + KV, 2 * ZW), 0)
+        fill(A("rl", 0, 64), 0); fill(A("rl", RW, RW + 64), 0)
+
+    def follow(e):
+        ab, gb = 9 * KV, (8 if e == 0 else 3) * KV
+        for i in range(16):
+            act(A("yb", ab + i, ab + KV, 16), A("cod"), ACT.Identity, 0.0, A("mk", i, i + 1))
+        for k in range(3):
+            gat("a", A("yb", gb + k * V, gb + k * V + V), A("yb", ab, ab + KV), A("lbs", 64 * k, 64 * k + 64))
+        wrap(A("px1", 0, 192), "h16", "yb", gb, KV)
+        ts(A("t2"), A("px1", 0, 192), 4.0, ALU.is_ge, 8.0, ALU.mult)
+        ts(A("t4", 0, 192), A("px1", 0, 192), -4.0, ALU.is_le, -8.0, ALU.mult)
+        tt(A("slot"), A("slot"), A("px1", 0, 192), ALU.add)
+        tt(A("t2"), A("t2"), A("t4", 0, 192), ALU.add)
+        tt(A("slot"), A("slot"), A("t2"), ALU.subtract)
+        ts(A("t2"), A("t2"), ZW / 8.0, ALU.mult)
+        tt(A("e1"), A("e1"), A("t2"), ALU.add)
+        back_lists(e + 1)
+        if e == 0:
+            diffs(1)
+
+    def count(e, bank):
+        for h in range(2):
+            terms = [(ID(-2.0 ** (s - 5)), half("sp", spos(e, s), h)) for s in range(5)]
+            if e > 0:
+                terms.append((ID(1.0), half("cn", 0, h)))
+            group(A(bank), terms)
+            act(half("cn", 0, h), A(bank), ACT.Identity, 0.0, -1.0 if e == 2 else 1.0)
+        if e == 2:
+            dma("g", A("cnt", 0, V), A("cn"))
+
+    def recip_a():
+        for k in range(3):
+            act(A("rc", k * V, k * V + V), A("wt", 3 * KV + k * V, 3 * KV + k * V + V), ACT.Ln, extra=0 if k else 1500)
+            ops[-1]["rd"].append(A("cn"))
+        for k in range(3):
+            act(A("rc", k * V, k * V + V), A("rc", k * V, k * V + V), ACT.Exp, 0.0, -1.0, extra=0 if k else 1500)
+
+    def recip_b():
+        for k in range(3):
+            r = A("rc", k * V, k * V + V)
+            for h in range(2):
+                mm(half("pv", 0, h), ID(1.0), half("wt", 3 * KV + k * V, h), True, True)
+            tt(A("pv"), A("pv"), r, ALU.mult)
+            act(A("pv"), A("pv"), ACT.Identity, 2.0, -1.0)
+            tt(r, A("pv"), r, ALU.mult)
+
+    nstep = [0]
+
+    def zprod(e, t):
+        z, y = (t % 2) * ZW, ypos(e, t)
+        for k in range(3):
+            tt(A("zz", z + k * V, z + k * V + V), A("yb", y + k * V, y + k * V + V), A("pl"), ALU.mult)
+        if e == 2 and t <= O["nt"]:
+            b = (9 if t == 1 else 3) * KV
+            ts(A("yb", b, b + KV), A("yb", y, y + KV), 2.0 ** 40, ALU.mult)
+            act(A("pv"), A("pl"), ACT.Identity, 0.0, 2.0 ** (t - 4))
+            for k in range(3):
+                r = A("rc", k * V, k * V + V)
+                tt(r, A("yb", b + k * V, b + k * V + V), A("pv"), ALU.min)
+                dma("g", A("gam", k * V, k * V + V), r, True)
+            return
+        if e == 0 and t == 4:
+            dma("s", A("acc"), A("zz", z, z + KV))
+        elif e == 2 and t == O["nt"] + 1:
+            for k in range(3):
+                a = A("acc", k * V, k * V + V)
+                dma("g", a, A("zz", z + k * V, z + k * V + V), True)
+                if O["rps"]:
+                    act(A("pv"), A("rc", k * V, k * V + V), ACT.Copy)
+                tt(a, a, A("pv") if O["rps"] else A("rc", k * V, k * V + V), ALU.mult)
+                dma("s", A("gam", k * V, k * V + V), a)
+        else:
+            c = KV // O["split"]
+            for k in range(O["split"]):
+                dma("g", A("acc", k * c, k * c + c), A("zz", z + k * c, z + k * c + c), True)
+
+    def backward(e):
+        o = 192 * (e % 2)
+        ew, e2, er = O["tail"] if e == 2 else "aaa"
+        a4, p4 = apos(e, 4), spos(e, 4)
+        for h in range(2):
+            mm(half("pk", 0, h), ID(1.0), half("ls", 0, h), True, True)
+        tt(A("pk"), A("pk"), A("aa", a4, a4 + V), ALU.mult)
+        tt(A("pl"), A("pk"), A("sp", p4, p4 + V), ALU.min)
+        zprod(e, 4)
+        for t in range(3, -1 if e == 2 else 0, -1):
+            win = A("zz", 0, ZW) if t == 3 else A("zz")
+            lst = "lb3" if t == 3 else "lbb" if t % 2 == 0 else "lba"
+            p, a = spos(e, t), apos(e, t)
+            r = (nstep[0] % 2) * RW
+            nstep[0] += 1
+            L = lambda c0, c1: A(lst, o + c0, o + c1)
+            gat("a", A("zg", V, M), win, L(64, 96))
+            gat(ew, A("zg", M + V, KV), win, L(160, 192))
+            group(A("px1", 0, H), [(SH32, A("zg", V, V + H)), (SH32, A("zg", M + V, M + V + H))])
+            act(A("sb"), A("px1", 0, H), ACT.Copy)
+            rem([(-1, [A("sb")], A("rl", r + 64, r + 64 + H)),
+                 (1, [A("zg", V + H, M), A("zg", M + V + H, KV)], A("rl", r + 64 + H, r + RW))])
+            for h in range(2):
+                lift = [(ID(2.0), A("one16")), (ID(-2.0 ** (t - 4)), half("sp", p, h))] if t == 0 else []
+                group(half("pk", 0, h), lift + [(ID(1.0), half("ls", 0, h))], True, False)
+            gat("a", A("zg", 0, V), win, L(0, 64))
+            mode = O["own"][e]
+            if mode == "v":
+                tt(A("zg", M, M + V), IND(win, L(96, 160)), A("zg", 0, V), ALU.add)
+            else:
+                gat(e2, A("zg", M, M + V), win, L(96, 160))
+            if mode == "d":
+                dma("g", A("zg", M, M + V), A("zg", 0, V), True)
+            if mode == "p":
+                for h in range(2):
+                    mm(half("pk", 0, h), I32F, half("zg", 0, h), False, False)
+            for h in range(2):
+                mm(half("pk", 0, h), I32F, half("zg", M, h), False, False)
+            tt(A("cap"), A("pl"), A("sp", p, p + V), ALU.max)
+            for h in range(2):
+                gat("a" if h == 0 else er, half("rg", 0, h), A("rl", r, r + RW), A("lr", 32 * h, 32 * h + 32))
+                mm(half("pk", 0, h), I32F, half("rg", 0, h), False, True)
+                tt(half("pk", 0, h), half("pk", 0, h), half("aa", a, h), ALU.mult)
+                tt(half("pl", 0, h), half("pk", 0, h), half("cap", 0, h), ALU.min)
+                if t == 0:
+                    act(half("cap", 0, h), half("pl", 0, h), ACT.Identity, 0.0, 1 / 16)
+                    dma("s", half("lam", 0, h), half("cap", 0, h))
+            if t > 0:
+                zprod(e, t)
+            if t == 3 and e < 2:
+                follow(e)
+            if t == 2 and e < 2:
+                count(e, "px1")
+
+    invert()
+    diffs(0)
+    forward(0); exchange(0); backward(0)
+    forward(1); exchange(1); backward(1)
+    recip_a()
+    forward(2); count(2, "px0"); recip_b(); backward(2)
+    return ops
+
+
+def link(ops):
+    hist = {}
+    for i, op in enumerate(ops):
+        dep = {}
+        acc = [(a, False) for a in op["rd"]] + [(a, True) for a in op["wr"]]
+        for a, w in acc:
+            ps = a[0] in _PS
+            lo, hi = (a[1] // 512 * 512, (a[2] + 511) // 512 * 512) if ps else (a[1], a[2])
+            for (j, l2, h2, w2, s2, o2) in hist.get(a[0], []):
+                if l2 >= hi or h2 <= lo:
+                    continue
+                if a[3] > 1 and s2 == a[3] and (o2 - a[1]) % s2 and not ps:
+                    continue
+                landing = op["kind"] == "rem" and w
+                if landing:
+                    continue
+                if w or w2 or (ps and ops[j]["eng"] != op["eng"]):
+                    kind = "lo" if (ops[j]["kind"] in ("rem", "fold") and not w2) else "ar"
+                    dep.setdefault(j, set()).add(kind)
+        op["dep"] = dep
+        for a, w in acc:
+            ps = a[0] in _PS
+            lo, hi = (a[1] // 512 * 512, (a[2] + 511) // 512 * 512) if ps else (a[1], a[2])
+            hl = hist.setdefault(a[0], [])
+            if (w or ps) and (a[3] == 1 or ps) and op["kind"] != "rem":
+                hl[:] = [x for x in hl if not (x[1] >= lo and x[2] <= hi and w and x[0] != i)]
+            if w and op["kind"] == "rem":
+                hl[:] = [x for x in hl if not (x[1] >= lo and x[2] <= hi)]
+            hl.append((i, lo, hi, w, a[3], a[1]))
+
+
+def gap(ops, j, i, C):
+    a, b = ops[j], ops[i]
+    if a["eng"] == b["eng"] and not a["lat"]:
+        return 0.0 if a["eng"] == "p" else C["same"]
+    return C["wake"]
+
+
+def graph(ops, C):
+    n = len(ops)
+    succ = [[] for _ in ops]
+    for i, op in enumerate(ops):
+        for j in op["dep"]:
+            succ[j].append((i, gap(ops, j, i, C)))
+    pr = [0.0] * n
+    for i in range(n - 1, -1, -1):
+        pr[i] = ops[i]["dur"] + ops[i]["lat"] + ops[i]["dby"] + max([x + pr[k] for k, x in succ[i]] + [0.0])
+    return (["vapgs".index(o["eng"]) for o in ops], [o["dur"] for o in ops], [o["lat"] for o in ops], [o["dby"] for o in ops],
+            succ, [len(o["dep"]) for o in ops], pr)
+
+
+def schedule(G, pr, slack):
+    eng, dur, lat, dby, succ, ndep, _ = G
+    n = len(eng)
+    left = list(ndep)
+    rdy = [0.0] * n
+    free = [0.0] * 6
+    ready = [[] for _ in range(5)]
+    for i in range(n):
+        if not left[i]:
+            ready[eng[i]].append(i)
+    order = []
+    last = 0.0
+    for _ in range(n):
+        e, t = -1, 1e30
+        for q in range(5):
+            if ready[q]:
+                x = max(free[q], min([rdy[i] for i in ready[q]]))
+                if x < t:
+                    e, t = q, x
+        i = max([k for k in ready[e] if rdy[k] <= t + slack], key=lambda k: pr[k])
+        ready[e].remove(i)
+        f = free[e] = max(free[e], rdy[i]) + dur[i]
+        if dby[i]:
+            free[5] = max(free[5], f + 500.0) + dby[i]
+            f = free[5] + lat[i] - 500.0
+        last = max(last, f)
+        order.append(i)
+        for k, x in succ[i]:
+            if f + x > rdy[k]:
+                rdy[k] = f + x
+            left[k] -= 1
+            if not left[k]:
+                ready[eng[k]].append(k)
+    return last, order
+
+
+def replay(G, order):
+    eng, dur, lat, dby, succ, ndep, _ = G
+    rdy, free, last = [0.0] * len(eng), [0.0] * 6, 0.0
+    end = [0.0] * len(eng)
+    for i in order:
+        e = eng[i]
+        f = end[i] = free[e] = max(free[e], rdy[i]) + dur[i]
+        if dby[i]:
+            free[5] = max(free[5], f + 500.0) + dby[i]
+            f = free[5] + lat[i] - 500.0
+        last = max(last, f)
+        for k, x in succ[i]:
+            if f + x > rdy[k]:
+                rdy[k] = f + x
+    return last, end
+
+
+VARIANTS = [{}, dict(gat=1.15, pe=0.6, rlat=3200, wake=200, dbw=400.0), dict(gat=1.95, sca=5.0, pe=0.45, rlat=1800, c16=1.3)]
+_PLAN = {}
+
+
+def plan():
+    if not _PLAN:
+        gs = []
+        for v in VARIANTS:
+            C = dict(COST, **v)
+            ops = build_ops(C, OPT)
+            link(ops)
+            gs.append(graph(ops, C))
+        n = len(ops)
+        state = [OPT["seed"] * 7919 + 12345]
+
+        def rnd(m):
+            state[0] = (state[0] * 6364136223846793005 + 1442695040888963407) % (1 << 64)
+            return (state[0] >> 33) % m
+
+        score = lambda order: sum(replay(G, order)[0] for G in gs) / len(gs)
+        pr = list(gs[0][6])
+        order = schedule(gs[0], pr, COST["slack"])[1]
+        best = score(order)
+        for it in range(OPT["iters"]):
+            p2 = list(pr)
+            for _ in range(1 + rnd(3)):
+                a = rnd(n)
+                b = min(n, a + [1, 3, 10, 30, 100][rnd(5)])
+                d = (rnd(2001) - 1000) * [0.8, 3.0, 12.0][rnd(3)]
+                en = rnd(5) - 2
+                for i in range(a, b):
+                    if en < 0 or gs[0][0][i] == en:
+                        p2[i] += d
+            o2 = schedule(gs[0], p2, COST["slack"])[1]
+            s2 = score(o2)
+            if s2 <= best:
+                best, pr, order = s2, p2, o2
+        _PLAN["ops"], _PLAN["order"], _PLAN["best"], _PLAN["gs"] = ops, order, best, gs
+    return _PLAN["ops"], _PLAN["order"]
+
+
+def _masks(core, nxt, prv, topo):
+    en, ep = topo.engines(core, nxt), topo.engines(core, prv)
+    first, second = (nxt, prv) if len(en) <= len(ep) else (prv, nxt)
+    e1, e2 = topo.engines(core, first), topo.engines(core, second)
+    k = len(set(e1) | set(e2)) // 2
+    k = 1 << int(math.log2(min(k, len(e1))))
+    s1 = e1[:k]
+    s2 = [x for x in e2 if x not in s1][:k]
+    return {first: s1, second: s2}
+
+
+def rank_program(g, core, T, topo):
+    rank = T.rank_of(core)
+    cores = list(T.cores)
+    helpers = {}
+    for c in cores:
+        helpers[c] = [x for x in topo.cores_of(c) if x not in cores and x not in helpers.values()][0]
+    if rank is None:
+        for c in cores:
+            if helpers[c] == core:
+                ops, order = plan()
+                folds = [ops[i]["args"][2] for i in order if ops[i]["kind"] == "fold"]
+                rid, pid, _ = topo.addr(c)
+                for f, b in enumerate(folds):
+                    g.wait_ge(T.sem["ha%d" % f], 3 * (len(topo.engines(c, core)) // 4))
+                    blk = _ap(T, A("yb", b, b + KV))
+                    g.remote_dma(blk, blk, T.sem["ha%d" % f], T.sem["hl%d" % f], pid, rid, topo.mask(core, c))
+                for f in range(len(folds)):
+                    g.wait_ge(T.sem["hl%d" % f], len(topo.engines(core, c)))
+        return
+    n = len(cores)
+    nb = {1: cores[(rank + 1) % n], -1: cores[(rank - 1) % n]}
+    eng_out = _masks(core, nb[1], nb[-1], topo)
+    arrive = len(_masks(nb[1], cores[(rank + 2) % n], core, topo)[core]) + len(_masks(nb[-1], core, cores[(rank - 2) % n], topo)[core])
+    leave = len(eng_out[nb[1]]) + len(eng_out[nb[-1]])
+    ops, order = plan()
+    Q = {"v": g.vector, "a": g.scalar, "p": g.tensor, "g": g, "s": g.sync}
+    cnt = {"cv": 0, "ca": 0, "cp": 0, "cg": 0}
+    done, seen, total = {}, {}, {}
+    nd, nr, nf = [0], [0], [0]
+    helper = helpers.get(core)
+    for i in order:
+        op = ops[i]
+        eng, kind, ar = op["eng"], op["kind"], op["args"]
+        q = Q[eng]
+        need = {}
+        for j, kinds in op["dep"].items():
+            if eng == "p" and ops[j]["eng"] == "p":
+                continue
+            for kd in kinds:
+                s, c = done[j][kd]
+                need[s] = max(need.get(s, 0), c)
+        for s, c in need.items():
+            if seen.get((eng, s), 0) < c:
+                q.wait_ge(T.sem[s], c)
+                seen[(eng, s)] = c
+        P = lambda a: _ap(T, a)
+        if kind == "rem":
+            sa, sl = "ar%d" % nr[0], "lo%d" % nr[0]
+            nr[0] += 1
+            trs = []
+            for to, srcs, dst in ar:
+                rid, pid, _ = topo.addr(nb[to])
+                mask = sum(1 << x for x in eng_out[nb[to]])
+                trs.append(RemoteDMATransfer(dst_ids=[DstId(rid=rid, pnc=pid)], dma_engine_mask=mask, remote_sem=T.sem[sa],
+                                             srcs=[P(s) for s in srcs], dsts=[P(dst)], alu_op=1 if len(srcs) > 1 else 0))
+            g.remote_dma_fused(trs, local_sem=T.sem[sl])
+            done[i] = {"ar": (sa, arrive), "lo": (sl, leave)}
+            total[sa], total[sl] = arrive, leave
+            continue
+        if kind == "fold":
+            sa, sl = "ha%d" % nf[0], "hl%d" % nf[0]
+            nf[0] += 1
+            y, p, b = ar
+            rid, pid, _ = topo.addr(helper)
+            en = topo.engines(core, helper)
+            w = len(en) // 4
+            g.remote_dma_fused([RemoteDMATransfer(dst_ids=[DstId(rid=rid, pnc=pid)], dma_engine_mask=sum(1 << x for x in en[(k + 1) * w:(k + 2) * w]),
+                                                  remote_sem=T.sem[sa], srcs=[P(A("yb", y + k * V, y + k * V + V)), P(A("sp", p, p + V))],
+                                                  dsts=[P(A("yb", b + k * V, b + k * V + V))], alu_op=3) for k in range(3)], local_sem=T.sem[sl])
+            back = len(topo.engines(helper, core))
+            done[i] = {"ar": (sa, back), "lo": (sl, 3 * w)}
+            total[sa], total[sl] = back, 3 * w
+            continue
+        if kind == "dma":
+            s = "d%d" % nd[0]
+            nd[0] += 1
+            if ar[2]:
+                q.dma_start(P(ar[0]), P(ar[1]), accum_op=ALU.add, max_dma_last_dim=4096 if _dt(ar[0]) == BF else 8192).then_inc(T.sem[s], 16)
+            else:
+                q.dma_start(P(ar[0]), P(ar[1])).then_inc(T.sem[s], 16)
+            done[i] = {"ar": (s, 16)}
+            total[s] = 16
+            continue
+        if kind == "tt":
+            ins = q.tensor_tensor(P(ar[0]), P(ar[1]), P(ar[2]), ar[3])
+        elif kind == "ts":
+            if ar[5] is None:
+                ins = q.tensor_scalar(P(ar[0]), P(ar[1]), P(ar[2]), None, ar[4])
+            else:
+                ins = q.tensor_scalar(P(ar[0]), P(ar[1]), P(ar[2]), P(ar[3]), ar[4], ar[5])
+        elif kind == "cp":
+            ins = q.tensor_copy(P(ar[0]), P(ar[1]))
+        elif kind == "ms":
+            ins = q.memset(P(ar[0]), ar[1])
+        elif kind == "act":
+            if ar[3] == 0.0 and ar[4] == 1.0:
+                ins = q.activation(P(ar[0]), P(ar[1]), ar[2])
+            else:
+                ins = q.activation(P(ar[0]), P(ar[1]), ar[2], bias=P(ar[3]), scale=P(ar[4]))
+        elif kind == "mm":
+            ins = q.matmul(P(ar[0]), P(ar[1]), P(ar[2]), ar[3], ar[4])
+        elif kind == "sel":
+            ins = q.affine_select(P(ar[0]), P(ar[1]), ar[2], ar[3], ar[4], ar[5], ar[6])
+        else:
+            ins = q.iota(P(ar[0]), ar[1], ar[2], ar[3], allow_small_or_imprecise_dtypes=_dt(ar[0]) != I32)
+        s = "c" + eng
+        cnt[s] += 1
+        ins.then_inc(T.sem[s], 1)
+        done[i] = {"ar": (s, cnt[s])}
+        total[s] = cnt[s]
+    for s, c in total.items():
+        if max(seen.get((e, s), 0) for e in Q) < c:
+            g.sync.wait_ge(T.sem[s], c)

@@ -36,8 +36,8 @@ _HBM = ("w", "drive", "loss", "src", "dly", "snd", "lam", "gam", "cnt")
 
 COST = dict(cyc=1.0, gat=1.56, sca=3.5, pe=0.52, vfix=60, afix=90, pfix=25, wake=120, same=50, c16=1.0,
             dissue=900, hissue=60, dlat=2000, dbw=550.0, rissue=400, rlat=2400, slack=120)
-OPT = dict(nt=1, tail="vvv", seed=0, iters=5000, split=3, own="ppp", s_mode=["v", "aa", "v"], wt_eng="vvaa", fold=[(), ()],
-           sig="p", ysplit=[0, 0, 0], afix="vvv", rps=True,
+OPT = dict(nt=1, tail="vvv", seed=0, iters=9000, fuse=False, split=3, own="ppv", s_mode=["av", "aa", "aa"], wt_eng="vvva", fold=[(), ()],
+           sig="s", ysplit=[0, 0, 0], afix="vvv", rps=True, fpos=[2, 2], cpos=[1, 1],
            sc_eng="aaaaava")
 
 
@@ -239,8 +239,8 @@ def build_ops(C, O):
     ts(A("cli", 1, 2), A("ioi", 0, 1), 15, ALU.bitwise_and)
     cp(A("clf", 0, 2), A("cli", 0, 2))
     ts(A("x8"), A("dlyi"), 8.0, ALU.mult, A("clf", 1, 2), ALU.add)
-    act(A("aa", 0, V), A("dr"), ACT.Identity, 16.0 * (195 - 1 / 64), -32.0)
-    ts(A("aa", 0, V), A("aa", 0, V), 192.0 * 16, ALU.subtract, 8.0, ALU.max)
+    act(A("aa", 0, V), A("dr"), ACT.Identity, 195 - 1 / 64, -2.0)
+    ts(A("aa", 0, V), A("aa", 0, V), 192.0, ALU.subtract, 0.5, ALU.max)
 
     def forward(e):
         sm, th = O["s_mode"][e], 0.5 if RA else 1.0
@@ -286,7 +286,7 @@ def build_ops(C, O):
                 else:
                     ts(A("mm"), A("pv"), 1.0, ALU.min)
             for h in range(2):
-                bank = A("px0") if t < 4 else A("px1")
+                bank = A("px0") if t < 4 or e == 2 else A("px1")
                 terms = [(ID(1.0), half("dr", 0, h))] + [(ID(s), half("yb", y + k * V, h)) for k in range(3)]
                 group(bank, terms + ([(ID(4.0 / s), half("sp", p, h))] if t < 4 else []))
                 act(half("aa", a, h), bank, ACT.Identity, s * ((211 if t < 4 else 195) - 1 / 64), -2.0 * s)
@@ -410,6 +410,8 @@ def build_ops(C, O):
             ops[-1]["rd"].append(A("cn"))
         for k in range(3):
             act(A("rc", k * V, k * V + V), A("rc", k * V, k * V + V), ACT.Exp, 0.0, -1.0, extra=0 if k else 1500)
+            if k == 0:
+                ops[-1]["rd"].append(A("rc"))
 
     def recip_b():
         for k in range(3):
@@ -421,11 +423,12 @@ def build_ops(C, O):
             tt(r, A("pv"), r, ALU.mult)
 
     nstep = [0]
+    lbuf = lambda e, t: A("pv" if (e, t) == (2, 4) else "pl")
 
     def zprod(e, t):
         z, y = (t % 2) * ZW, ypos(e, t)
         for k in range(3):
-            tt(A("zz", z + k * V, z + k * V + V), A("yb", y + k * V, y + k * V + V), A("pl"), ALU.mult)
+            tt(A("zz", z + k * V, z + k * V + V), A("yb", y + k * V, y + k * V + V), lbuf(e, t), ALU.mult)
         if e == 2 and t <= O["nt"]:
             b = (9 if t == 1 else 3) * KV
             ts(A("yb", b, b + KV), A("yb", y, y + KV), 2.0 ** 40, ALU.mult)
@@ -457,7 +460,7 @@ def build_ops(C, O):
         for h in range(2):
             mm(half("pk", 0, h), ID(1.0), half("ls", 0, h), True, True)
         tt(A("pk"), A("pk"), A("aa", a4, a4 + V), ALU.mult)
-        tt(A("pl"), A("pk"), A("sp", p4, p4 + V), ALU.min)
+        tt(lbuf(e, 4), A("pk"), A("sp", p4, p4 + V), ALU.min)
         zprod(e, 4)
         for t in range(3, -1 if e == 2 else 0, -1):
             win = A("zz", 0, ZW) if t == 3 else A("zz")
@@ -466,8 +469,14 @@ def build_ops(C, O):
             r = (nstep[0] % 2) * RW
             nstep[0] += 1
             L = lambda c0, c1: A(lst, o + c0, o + c1)
-            gat("a", A("zg", V, M), win, L(64, 96))
-            gat(ew, A("zg", M + V, KV), win, L(160, 192))
+            if e == 2:
+                gat("a", A("zg", V, V + H), win, L(64, 80))
+                gat(ew, A("zg", M + V, M + V + H), win, L(160, 176))
+                gat("a", A("zg", V + H, M), win, L(80, 96))
+                gat(ew, A("zg", M + V + H, KV), win, L(176, 192))
+            else:
+                gat("a", A("zg", V, M), win, L(64, 96))
+                gat(ew, A("zg", M + V, KV), win, L(160, 192))
             group(A("px1", 0, H), [(SH32, A("zg", V, V + H)), (SH32, A("zg", M + V, M + V + H))])
             act(A("sb"), A("px1", 0, H), ACT.Copy)
             rem([(-1, [A("sb")], A("rl", r + 64, r + 64 + H)),
@@ -477,6 +486,7 @@ def build_ops(C, O):
                 group(half("pk", 0, h), lift + [(ID(1.0), half("ls", 0, h))], True, False)
             gat("a", A("zg", 0, V), win, L(0, 64))
             mode = O["own"][e]
+            fuse = e == 2 and O["fuse"]
             if mode == "v":
                 tt(A("zg", M, M + V), IND(win, L(96, 160)), A("zg", 0, V), ALU.add)
             else:
@@ -487,21 +497,29 @@ def build_ops(C, O):
                 for h in range(2):
                     mm(half("pk", 0, h), I32F, half("zg", 0, h), False, False)
             for h in range(2):
-                mm(half("pk", 0, h), I32F, half("zg", M, h), False, False)
-            tt(A("cap"), A("pl"), A("sp", p, p + V), ALU.max)
+                mm(half("pk", 0, h), I32F, half("zg", M, h), False, fuse)
+            tt(A("cap"), lbuf(e, t + 1), A("sp", p, p + V), ALU.max)
+            if e == 2 and t == 3:
+                recip_b()
+            if t == 0:
+                act(A("cap"), A("cap"), ACT.Identity, 0.0, 1 / 16)
             for h in range(2):
-                gat("a" if h == 0 else er, half("rg", 0, h), A("rl", r, r + RW), A("lr", 32 * h, 32 * h + 32))
-                mm(half("pk", 0, h), I32F, half("rg", 0, h), False, True)
-                tt(half("pk", 0, h), half("pk", 0, h), half("aa", a, h), ALU.mult)
-                tt(half("pl", 0, h), half("pk", 0, h), half("cap", 0, h), ALU.min)
+                if fuse:
+                    tt(half("pk", 0, h), half("pk", 0, h), half("aa", a, h), ALU.mult)
+                    tt(half("rg", 0, h), IND(A("rl", r, r + RW), A("lr", 32 * h, 32 * h + 32)), half("aa", a, h), ALU.mult)
+                    tt(half("pk", 0, h), half("pk", 0, h), half("rg", 0, h), ALU.add)
+                else:
+                    gat("a" if h == 0 else er, half("rg", 0, h), A("rl", r, r + RW), A("lr", 32 * h, 32 * h + 32))
+                    mm(half("pk", 0, h), I32F, half("rg", 0, h), False, True)
+                    tt(half("pk", 0, h), half("pk", 0, h), half("aa", a, h), ALU.mult)
+                tt(half("pl" if t else "rg", 0, h), half("pk", 0, h), half("cap", 0, h), ALU.min)
                 if t == 0:
-                    act(half("cap", 0, h), half("pl", 0, h), ACT.Identity, 0.0, 1 / 16)
-                    dma("s", half("lam", 0, h), half("cap", 0, h))
+                    dma("s", half("lam", 0, h), half("rg", 0, h))
             if t > 0:
                 zprod(e, t)
-            if t == 3 and e < 2:
+            if e < 2 and t == O["fpos"][e]:
                 follow(e)
-            if t == 2 and e < 2:
+            if e < 2 and t == O["cpos"][e]:
                 count(e, "px1")
 
     invert()
@@ -509,7 +527,7 @@ def build_ops(C, O):
     forward(0); exchange(0); backward(0)
     forward(1); exchange(1); backward(1)
     recip_a()
-    forward(2); count(2, "px0"); recip_b(); backward(2)
+    forward(2); count(2, "px0"); backward(2)
     return ops
 
 
@@ -617,7 +635,7 @@ def replay(G, order):
     return last, end
 
 
-VARIANTS = [{}, dict(gat=1.15, pe=0.6, rlat=3200, wake=200, dbw=400.0), dict(gat=1.95, sca=5.0, pe=0.45, rlat=1800, c16=1.3)]
+VARIANTS = [{}, dict(gat=1.15, pe=0.6, rlat=3200, wake=200, dbw=400.0), dict(gat=1.95, sca=5.0, pe=0.45, rlat=1800)]
 _PLAN = {}
 
 
@@ -640,6 +658,7 @@ def plan():
         pr = list(gs[0][6])
         order = schedule(gs[0], pr, COST["slack"])[1]
         best = score(order)
+        cur, first = [best], [1e30]
         for it in range(OPT["iters"]):
             p2 = list(pr)
             for _ in range(1 + rnd(3)):
@@ -650,10 +669,14 @@ def plan():
                 for i in range(a, b):
                     if en < 0 or gs[0][0][i] == en:
                         p2[i] += d
-            o2 = schedule(gs[0], p2, COST["slack"])[1]
+            t2, o2 = schedule(gs[0], p2, COST["slack"])
+            if t2 > first[0] + 2000.0:
+                continue
             s2 = score(o2)
-            if s2 <= best:
-                best, pr, order = s2, p2, o2
+            if s2 <= cur[0]:
+                cur[0], first[0], pr = s2, t2, p2
+                if s2 <= best:
+                    best, order = s2, o2
         _PLAN["ops"], _PLAN["order"], _PLAN["best"], _PLAN["gs"] = ops, order, best, gs
     return _PLAN["ops"], _PLAN["order"]
 

@@ -8,37 +8,41 @@ SO = SW - V
 ZW = KV + 8
 RW = 64 + 2 * H
 EPS = 2.0 ** -30
-SC = [8.0, 4.0, 2.0, 1.0, -1 / 64, -1 / 32, -1 / 16, -1 / 8, -1 / 4, -1 / 2, 1 / 2, 1 / 4, 1 / 8, 1 / 16]
-RA = False
+SC = [1.0, 8.0, -1 / 64, 1 / 2, 4.0, -1 / 32, 1 / 32, -1 / 8, 1 / 8, 2.0, -1 / 16, 1 / 16, 1 / 4]
 
 F32, BF, I32, U16, F16 = "float32", "bfloat16", "int32", "uint16", "float16"
 _SB = {
     "wt": (4 * KV, BF), "yb": (10 * KV, BF), "zz": (2 * ZW, F32), "acc": (KV, F32), "rc": (KV, F32),
     "sp": (9 * SW - 2 * SO, BF), "aa": (9 * V, BF), "zg": (KV, F32), "rg": (V, F32), "rl": (2 * RW, F32),
-    "sb": (H, F32), "sg": (2 * H, BF), "sf": (H, BF), "cap": (V, F32), "mm": (V, F32 if RA else F16), "qq": (V, BF),
+    "sb": (H, F32), "sg": (2 * H, BF), "sf": (H, BF), "cap": (V, F32), "mm": (2 * V, F16), "qq": (2 * V, BF),
     "dr": (V, BF), "ls": (V, BF), "cn": (V, BF), "one16": (512, BF),
-    "ii32": (256, F32), "ii16": (256, BF), "ids": (128 * len(SC), BF), "hf16": (128, F32 if RA else F16),
-    "h32": (144, F32), "h16": (144, BF), "pd32": (256, F32), "pp16": (256, BF), "pd16": (256, BF),
-    "srci": (192, I32), "dlyi": (192, I32), "sndi": (32, I32), "ioi": (192, I32), "mki": (16, I32), "cli": (4, I32),
-    "mk": (16, F32), "clf": (4, F32), "srcf": (192, F32), "fd": (192, F32), "fa": (192, F32), "t1": (192, F32),
-    "t2": (192, F32), "t3": (192, F32), "t4": (224, F32), "slot": (192, F32), "e1": (192, F32),
-    "swp": (192, F32), "eag": (192, BF), "x8": (192, BF), "cod": (192, BF),
-    "lt1": (192, U16), "lg": (192, U16), "lp": (192, U16), "lsn": (32, U16), "lr": (64, U16), "lbs": (192, U16),
+    "ii32": (256, F32), "ii16": (256, BF), "ids": (128 * len(SC), BF), "hf16": (128, F16),
+    "h16": (144, BF), "k16": (144, BF), "pd32": (256, F32), "pp16": (256, BF), "pd16": (256, BF),
+    "srci": (192, I32), "dlyi": (192, I32), "sndi": (32, I32), "ioi": (192, I32), "cli": (4, I32),
+    "clf": (4, F32), "srcf": (192, F32), "fd": (192, F32), "fa": (192, F32), "t1": (192, F32),
+    "t2": (192, F32), "la": (192, F32), "lb": (192, F32),
+    "swp": (192, BF), "d8": (192, BF), "eag": (192, BF), "x8": (192, BF), "cod": (192, BF),
+    "lt1": (192, U16), "lg": (192, U16), "lp": (192, U16), "lsn": (32, U16), "lsp": (32, U16), "lr": (64, U16), "lbs": (192, U16),
     "lba": (384, U16), "lbb": (384, U16), "lb3": (384, U16),
 }
-_PS = {"pv": 1024, "pk": 1024, "pl": 1024, "px0": 512, "px1": 512}
+_PS = {"pv": 1024, "pk": 1024, "pq": 1024, "px0": 512, "px1": 512}
+_HW = {"w": BF, "drive": BF, "loss": BF}
 SCRATCH = {k: ("sbuf", [128, n], d) for k, (n, d) in _SB.items()}
 SCRATCH.update({k: ("psum", [128, n], F32) for k, n in _PS.items()})
-NDMA, NREM = 60, 20
+NDMA, NREM = 90, 20
 SEMAPHORES = ["cv", "ca", "cp", "cg"] + ["d%d" % i for i in range(NDMA)] + ["ar%d" % i for i in range(NREM)] + ["lo%d" % i for i in range(NREM)]
-SEMAPHORES += ["ha%d" % i for i in range(8)] + ["hl%d" % i for i in range(8)]
-_HBM = ("w", "drive", "loss", "src", "dly", "snd", "lam", "gam", "cnt")
 
-COST = dict(cyc=1.0, gat=1.56, sca=3.5, pe=0.52, vfix=60, afix=90, pfix=25, wake=120, same=50, c16=1.0,
-            dissue=900, hissue=60, dlat=2000, dbw=550.0, rissue=400, rlat=2400, slack=120)
-OPT = dict(nt=1, tail="vvv", seed=0, iters=9000, fuse=False, split=3, own="ppv", s_mode=["av", "aa", "aa"], wt_eng="vvva", fold=[(), ()],
-           sig="s", ysplit=[0, 0, 0], afix="vvv", rps=True, fpos=[2, 2], cpos=[1, 1],
-           sc_eng="aaaaava")
+COST = dict(cyc=0.83, gat=1.56, sca=3.5, pe=0.42, vfix=60, afix=90, pfix=25, wake=120, same=50, c16=1.0,
+            dissue=900, hissue=60, dlat=2000, dbw=550.0, rissue=400, rlat=2400)
+VARIANTS = [dict(cyc=0.9, gat=1.4, sca=3.0, pe=0.45, rlat=2800, wake=150), dict(cyc=1.2, gat=2.0, sca=5.5, pe=0.6, dbw=450.0)]
+OPT = dict(seed=0, tries=4, steps=22000, more=40000, heat=0.0015, pull=0.3, aim=[0, 1], passes=1,
+           tail="vaa", own="ppv", spike=["vvvv", "aaaa", "aaav"], wt_eng="vadd", vote=["bssm", "ssss"],
+           ysplit=[[0] * 4] * 3, afix="vvv", sc_eng="aaaaaaa", ids="g", xhalf=True, fin="m", whole=[False, False, False],
+           gaps=2, g4=8.0, sat=7.0, mat=5.3, big="a", late=[1, 2], cend=1, rps=False, rpos=3, cpos=[2, 5], fpos=[2, 2], wsplit=[True, True, True], fill=True, defer=True, rb={2: [0, 1, 2]}, parts=[1, 1, 2],
+           beat=[10.3, 14.7, 11.5], zbeat=[0, 13.5, 13.5],
+           send=[5.4, 6.4, 5.4], rat=[6.2, 5.0], x4=[(8.0, 13.1, 13.0), (8.0, 13.1, 13.0), (7.0, 12.0, 0)], xat=[10.3, 11.3, 13.2],
+           vat=[[(7.0, 8.0, 9.0), (5.3, 6.2, 7.1)], [(12.8, 13.7, 14.0), (5.3, 6.2, 7.1)]],
+           gam=[(-1.7, -0.8, 3.6), (2.4, 2.5, 2.6)], fat=[7.0, 12.9, 13.8], bat=[(1.6, 3.0, 1.6, 3.5, 0), (0.6, 1.7, 0.9, 1.7, 1.0)])
 
 
 def A(name, lo=0, hi=None, step=1):
@@ -60,7 +64,7 @@ def _n(a):
 def _dt(a):
     if a[0] == "@":
         return _dt(a[1])
-    return _SB[a[0]][1] if a[0] in _SB else F32
+    return _SB[a[0]][1] if a[0] in _SB else _HW.get(a[0], F32)
 
 
 def _isap(a):
@@ -80,7 +84,7 @@ def _ap(T, a):
 
 
 def build_ops(C, O):
-    ops = []
+    ops, clock = [], [0.0]
 
     def add(eng, kind, args, outs, ins, dur, lat=0.0, dby=0.0):
         rd, wr = [], []
@@ -92,7 +96,11 @@ def build_ops(C, O):
                 wr.append(a[1]); rd.append(a[2])
             else:
                 wr.append(a)
-        ops.append(dict(eng=eng, kind=kind, args=args, rd=rd, wr=wr, dur=dur, lat=lat, dby=dby))
+        clock[0] += 0.001
+        ops.append(dict(eng=eng, kind=kind, args=args, rd=rd, wr=wr, dur=dur, lat=lat, dby=dby, at=clock[0]))
+
+    def at(x):
+        clock[0] = x
 
     def vdur(out, ins, two):
         n = _n(out)
@@ -129,18 +137,27 @@ def build_ops(C, O):
         else:
             cp(out, IND(win, off))
 
-    def mm(out, lhs, rhs, start, stop):
-        f = 4 if _dt(rhs) == F32 else 1
-        add("p", "mm", (out, lhs, rhs, start, stop), [out], [lhs, rhs], C["pfix"] + max(64, _n(rhs)) * f * C["pe"])
-
     def group(out, terms, first=True, last=True):
-        for i, (l, r) in enumerate(terms):
-            mm(out, l, r, first and i == 0, last and i == len(terms) - 1)
+        dur = sum(C["pfix"] + max(64, _n(r)) * (4 if _dt(r) == F32 else 1) * C["pe"] for _, r in terms)
+        add("p", "mm", [(out, terms, first, last)], [out], [a for t in terms for a in t], dur)
+
+    def both(bank, terms, first=True, last=True):
+        for h in range(2):
+            group(half(bank, 0, h), [(l, half(n, b, h if n != "one16" else 0)) for l, n, b in terms], first, last)
+        o = ops.pop()
+        for k in ("args", "rd", "wr", "dur"):
+            ops[-1][k] += o[k]
+
+    def mm(out, lhs, rhs, start=True, stop=True):
+        group(out, [(lhs, rhs)], start, stop)
 
     def dma(eng, out, a, acc=False):
         by = _n(out) * 128 * (2 if _dt(out) == BF else 4)
         add(eng, "dma", (out, a, acc), [out], [a, out] if acc else [a], C["dissue"] if eng == "g" else C["hissue"],
             C["dlat"], by * (2 if acc else 1) / C["dbw"])
+
+    def cat(kind, out, a):
+        add("s", kind, (out, a), [out], [a], C["hissue"], C["dlat"], 1000.0 if _dt(a) == F32 else 600.0)
 
     def rem(tr):
         add("g", "rem", tr, [t[2] for t in tr], [s for t in tr for s in t[1]], C["rissue"], C["rlat"] - 600.0, 600.0)
@@ -148,8 +165,8 @@ def build_ops(C, O):
     def gp(kind, out, ins, args):
         add("g", kind, args, [out], ins, 170 + 2 * _n(out) * C["cyc"])
 
-    def sel(out, a, pattern, op, base, cm):
-        gp("sel", out, [a], (out, a, pattern, op, 0.0, base, cm))
+    def sel(out, a, pattern, op, base, cm, other=0.0):
+        gp("sel", out, [a], (out, a, pattern, op, other, base, cm))
 
     def iota(out, pattern, base, cm):
         gp("iota", out, [], (out, pattern, base, cm))
@@ -164,370 +181,584 @@ def build_ops(C, O):
     def half(name, base, h):
         return A(name, base + 512 * h, base + 512 * h + 512)
 
+    def third(name, base, k):
+        return A(name, base + V * k, base + V * k + V)
+
     spos = lambda e, s: max(0, (4 + s if e % 2 == 0 else 4 - s) * SW - SO)
     apos = lambda e, t: (0 if t == 0 else 4 * (e % 2) + t) * V
     YB = [[0, 1, 2, 3], [4, 5, 6, 7], [2, 1, 0, 8]]
-    PB = [[4, 5, 6, 7], [8, 9, 3, 2]]
+    PB = [[4, 5, 6, 7], [3, 2, 8, 9]]
     ypos = lambda e, t: YB[e][t - 1] * KV
+    mpos = lambda t: V if t else 0
     I32F, SH32 = A("ii32", 0, 128), A("ii32", 16, 144)
     SH16 = A("ii16", 112, 240)
+    p0 = spos(0, 0)
 
-    def wrap(out, hbuf, src, base, n):
-        for i in range(16):
-            mm(out, A(hbuf, 15 - i, 143 - i), A(src, base + i, base + n, 16), i == 0, i == 15)
+    def wrap(out, hbuf, src, base, n=KV):
+        group(out, [(A(hbuf, 15 - i, 143 - i), A(src, base + i, base + n, 16)) for i in range(16)])
+        ops[-1]["rd"] = [A(hbuf), A(src, base, base + n)]
 
-    def send_spikes(e, s):
+    def rowwise(out, idx, width, more, tmp):
+        lo, hi = A("ioi", 0, _n(idx)), A("dlyi", 0, _n(idx))
+        ts(lo, idx, 15, ALU.bitwise_and)
+        ts(hi, idx, 4, ALU.logical_shift_right)
+        ts(tmp, lo, float(width), ALU.mult)
+        tt(tmp, tmp, hi, ALU.add)
+        if more:
+            tt(tmp, tmp, more, ALU.add)
+        cp(out, tmp)
+
+    def send_spikes(e, s, T):
         p = spos(e, s)
-        gat("a", A("sg"), A("sp", p, p + V), A("lsn"))
-        mm(A("px0", 0, H), SH16, A("sg", 0, H), True, True)
+        at(T)
+        gat("a", A("sg", 0, H), A("sp", p, p + V), A("lsn", 0, 16))
+        gat("a", A("sg", H, 2 * H), A("sp", p, p + V), A("lsn", 16, 32))
+        mm(A("px0", 0, H), SH16, A("sg", 0, H))
         act(A("sf"), A("px0", 0, H), ACT.Copy)
         rem([(1, [A("sf")], A("sp", p + V, p + V + H)), (-1, [A("sg", H, 2 * H)], A("sp", p + V + H, p + M))])
 
-    dma("s", A("dr"), A("drive", 0, V)); dma("a", A("sndi"), A("snd", 0, 32))
-    dma("s", A("srci"), A("src", 0, 192)); dma("a", A("dlyi"), A("dly", 0, 192))
-    for k in range(3):
-        dma("s", A("wt", 3 * KV + k * V, 3 * KV + k * V + V), A("w", k * V, k * V + V))
-    dma("a", A("ls"), A("loss", 0, V))
-    ms(A("pd32"), 1.0)
-    sel(A("ii32"), A("pd32"), [[0, 2], [-1, 128]], ALU.is_equal, 0, 1)
-    cp(A("ii16"), A("ii32"))
-    for s in SC:
-        act(ID(s), A("ii32", 0, 128), ACT.Identity, 0.0, s)
-    ts(A("hf16"), A("ii16", 0, 128), -0.5 if RA else 0.5, ALU.mult)
-    fill(A("one16"), 1)
-    for b in (4, 5, 6, 7, 3, 2, 1):
-        fill(A("sp", b * SW + M - SO, b * SW + SW - SO), 0)
-    cp(A("lsn"), A("sndi"))
-    p0 = spos(0, 0)
-    ts(A("sp", p0, p0 + V), A("dr"), 1.0, ALU.is_ge, 32.0, ALU.mult)
-    send_spikes(0, 0)
-    cp(A("lp"), A("srci"))
-    ts(A("t1"), A("srci"), 1536.0, ALU.is_ge, -1536.0, ALU.mult)
-    tt(A("srcf"), A("srci"), A("t1"), ALU.add)
-    ts(A("t2"), A("dlyi"), 1.0, ALU.subtract, float(SW), ALU.mult)
-    tt(A("fd"), A("srcf"), A("t2"), ALU.add)
-    ts(A("lt1"), A("fd"), float(M), ALU.min)
-    tt(A("fa"), A("srcf"), A("t2"), ALU.subtract)
-    ts(A("lg"), A("fa"), float(SW), ALU.add)
-    for t in (1, 2, 3, 4):
+    def weights(t):
+        o, a, s = (t - 1) * KV, 3 * KV, 2.0 ** (t - 4)
+        if O["wt_eng"][t - 1] == "d":
+            dma("s", A("wt", o, o + KV), A("wt", o - KV, o))
+            dma("g", A("wt", o, o + KV), A("wt", o - KV, o), True)
+            return
         for k in range(3):
-            lo, hi = k * V, k * V + V
-            o, a, s = A("wt", (t - 1) * KV + lo, (t - 1) * KV + hi), A("wt", 3 * KV + lo, 3 * KV + hi), 2.0 ** (t - 4)
             if O["wt_eng"][t - 1] == "v":
-                ts(o, a, EPS, ALU.max, s, ALU.mult)
-            elif O["wt_eng"][t - 1] == "d":
-                if k == 0:
-                    o, a = A("wt", (t - 1) * KV, t * KV), A("wt", (t - 2) * KV, (t - 1) * KV)
-                    dma("s", o, a)
-                    dma("g", o, a, True)
+                ts(third("wt", o, k), third("wt", a, k), EPS, ALU.max, s, ALU.mult)
             else:
-                act(o, a, ACT.Identity, EPS * s, s)
-    fill(A("h32"), 0)
-    sel(A("h32", 15, 144, 16), A("pd32", 0, 9), [[-16, 9]], ALU.is_ge, 0, 1)
-    sel(A("h32", 15, 144, 16), A("h32", 15, 144, 16), [[16, 9]], ALU.is_ge, 15, -1)
-    cp(A("h16"), A("h32"))
-    sel(A("pd32", 0, 128), A("pd32", 0, 128), [[-2, 64], [1, 2]], ALU.is_equal, -1, 1)
-    sel(A("pd32", 128, 256), A("pd32", 128, 256), [[-4, 32], [2, 2], [-1, 2]], ALU.is_equal, -2, 1)
-    tt(A("pp16"), A("pd32"), A("ii32"), ALU.add)
-    tt(A("pd32"), A("pd32"), A("ii32"), ALU.subtract)
-    cp(A("pd16"), A("pd32"))
-    iota(A("ioi"), [[16, 192]], 0, 1)
-    iota(A("mki"), [[-1, 16]], 16, 1)
-    ts(A("mki"), A("mki"), 15, ALU.bitwise_and)
-    ts(A("mk"), A("mki"), 0.0, ALU.is_equal)
-    ts(A("cli", 0, 1), A("ioi", 0, 1), 112, ALU.bitwise_and)
-    ts(A("cli", 1, 2), A("ioi", 0, 1), 15, ALU.bitwise_and)
-    cp(A("clf", 0, 2), A("cli", 0, 2))
-    ts(A("x8"), A("dlyi"), 8.0, ALU.mult, A("clf", 1, 2), ALU.add)
-    act(A("aa", 0, V), A("dr"), ACT.Identity, 195 - 1 / 64, -2.0)
-    ts(A("aa", 0, V), A("aa", 0, V), 192.0, ALU.subtract, 0.5, ALU.max)
+                act(third("wt", o, k), third("wt", a, k), ACT.Identity, EPS * s, s)
 
-    def forward(e):
-        sm, th = O["s_mode"][e], 0.5 if RA else 1.0
-        if RA:
-            act(A("mm"), A("dr"), ACT.Relu, 1.0, -1.0)
-        else:
-            ts(A("mm"), A("dr"), 1.0, ALU.min)
-        for t in range(1, 5):
-            s = 2.0 ** (4 - t)
-            y, w = ypos(e, t), (t - 1) * KV
-            if t == 1:
-                win, lst = A("sp", p0, p0 + SW), "lt1"
+    def scaled(some):
+        for s in some:
+            if O["ids"] == "g":
+                sel(ID(s), A("k16", 0, 128), [[-1, 128]], ALU.not_equal, 0, 1, s)
             else:
-                lo = min(spos(e, t - 1), spos(e, t - 2))
-                win, lst = A("sp", lo, lo + 2 * SW), "lg"
-            for h in range(2):
-                group(half("pv", 0, h), [(ID(1.0), half("dr", 0, h)), (ID(-2.0 ** (t - 7)), half("sp", spos(e, t - 1), h)),
-                                         (A("hf16"), half("mm", 0, h))], True, False)
-            for k in range(3):
-                yk, wk, lk = A("yb", y + k * V, y + k * V + V), A("wt", w + k * V, w + k * V + V), A(lst, 64 * k, 64 * k + 64)
-                if k < O["ysplit"][e]:
-                    gat("a", yk, win, lk)
-                    tt(yk, yk, wk, ALU.min)
-                else:
-                    tt(yk, IND(win, lk), wk, ALU.min)
-                for h in range(2):
-                    mm(half("pv", 0, h), ID(s), half("yb", y + k * V, h), False, k == 2)
-            p = spos(e, t)
-            a = apos(e, t)
-            for h in range(2):
-                if sm == "v":
-                    ts(half("sp", p, h), half("pv", 0, h), th, ALU.is_ge, 2.0 * s, ALU.mult)
-                else:
-                    act(half("qq", 0, h), half("pv", 0, h), ACT.Sign, 2.0 ** -12 - th)
-                    if sm == "av":
-                        ts(half("sp", p, h), half("qq", 0, h), s, ALU.mult, s, ALU.add)
-                    else:
-                        act(half("sp", p, h), half("qq", 0, h), ACT.Identity, s, s)
-            if t < 4:
-                send_spikes(e, t)
-                if RA:
-                    act(A("mm"), A("pv"), ACT.Relu, 0.5, -1.0)
-                else:
-                    ts(A("mm"), A("pv"), 1.0, ALU.min)
-            for h in range(2):
-                bank = A("px0") if t < 4 or e == 2 else A("px1")
-                terms = [(ID(1.0), half("dr", 0, h))] + [(ID(s), half("yb", y + k * V, h)) for k in range(3)]
-                group(bank, terms + ([(ID(4.0 / s), half("sp", p, h))] if t < 4 else []))
-                act(half("aa", a, h), bank, ACT.Identity, s * ((211 if t < 4 else 195) - 1 / 64), -2.0 * s)
-            if O["afix"][e] == "v":
-                ts(A("aa", a, a + V), A("aa", a, a + V), 192.0 * s, ALU.subtract, 0.5 * s, ALU.max)
-            else:
-                act(A("aa", a, a + V), A("aa", a, a + V), ACT.Relu, -192.5 * s)
-                act(A("aa", a, a + V), A("aa", a, a + V), ACT.Identity, 0.5 * s)
-            if e < 2 and t in O["fold"][e]:
-                b = PB[e][t - 1] * KV
-                add("g", "fold", (y, p, b), [A("yb", b, b + KV)], [A("yb", y, y + KV), A("sp", p, p + V)], C["rissue"],
-                    2 * C["rlat"] + 1.5e6 / C["dbw"], 2.4e6 / C["dbw"])
-            elif e < 2:
-                sig = A("pv") if O["sig"] == "p" else A("qq")
-                if sm == "v" or O["sig"] == "p":
-                    act(sig, A("pv"), ACT.Sign, 2.0 ** -12 - th)
-                b = PB[e][t - 1] * KV
-                for k in range(3):
-                    tt(A("yb", b + k * V, b + k * V + V), A("yb", y + k * V, y + k * V + V), sig, ALU.mult)
+                act(ID(s), A("ii32", 0, 128), ACT.Identity, 0.0, s)
 
-    def diffs(e):
-        mm(A("px1", 0, 192), A("pd32", 128 * e, 128 * e + 128), A("srcf"), True, True)
-        mm(A("px1", 256, 448), A("pd16", 128 * e, 128 * e + 128), A("x8"), True, True)
-        act(A("t1"), A("px1", 0, 192), ACT.Copy)
-        act(A("t3"), A("px1", 256, 448), ACT.Copy)
-
-    def exchange(e):
-        vb = 8 * KV
-        banks = [A("px0"), half("pv", 0, 0), half("pv", 0, 1)] * 2
-        for c in range(6):
-            terms = []
-            for t in range(1, 5):
-                if t in O["fold"][e]:
-                    terms += [(ID(2.0 ** (1 - t)), half("yb", PB[e][t - 1] * KV, c)), (ID(-2.0 ** -t), half("yb", ypos(e, t), c))]
-                else:
-                    terms += [(ID(2.0 ** -t), half("yb", PB[e][t - 1] * KV, c))]
-            group(banks[c], terms)
-            act(half("yb", vb, c), banks[c], ACT.Sign, -EPS / 32)
-        wrap(A("pv", 0, 192), "h16", "yb", vb, KV)
-        ts(A("eag"), A("pv", 0, 192), 1.0, ALU.is_ge)
-        mm(A("pv", 512, 704), A("pp16", 128 * e, 128 * e + 128), A("eag"), True, True)
-        ts(A("swp"), A("pv", 512, 704), 1.5, ALU.is_ge)
-        tt(A("t1"), A("t1"), A("swp"), ALU.mult)
-        tt(A("fd"), A("fd"), A("t1"), ALU.add)
+    def start():
+        dma("s", A("dr"), A("drive", 0, V)); dma("a", A("sndi"), A("snd", 0, 32))
+        dma("s", A("srci"), A("src", 0, 192)); dma("a", A("dlyi"), A("dly", 0, 192))
+        for k in range(3):
+            dma("s", third("wt", 3 * KV, k), third("w", 0, k))
+        dma("a", A("ls"), A("loss", 0, V))
+        ms(A("pd32"), 1.0)
+        sel(A("ii32"), A("pd32"), [[0, 2], [-1, 128]], ALU.is_equal, 0, 1)
+        cp(A("ii16"), A("ii32"))
+        fill(A("k16"), 0)
+        fill(A("sp", p0 + M, p0 + SW), 0)
+        cp(A("lsn"), A("sndi"))
+        ts(A("sp", p0, p0 + V), A("dr"), 1.0, ALU.is_ge, 32.0, ALU.mult)
+        send_spikes(0, 0, 1.0)
+        scaled(SC[:4])
+        ts(A("t1"), A("srci"), 1536.0, ALU.is_ge, -1536.0, ALU.mult)
+        tt(A("srcf"), A("srci"), A("t1"), ALU.add)
+        ts(A("t2"), A("dlyi"), 1.0, ALU.subtract, float(SW), ALU.mult)
+        tt(A("fd"), A("srcf"), A("t2"), ALU.add)
         ts(A("lt1"), A("fd"), float(M), ALU.min)
-        tt(A("fa"), A("fa"), A("t1"), ALU.add)
+        weights(1)
+        ts(A("hf16"), A("ii16", 0, 128), 0.5, ALU.mult)
+        ts(third("mm", 0, 0), A("dr"), 1.0, ALU.min)
+        iota(A("cli", 0, 1), [[0, 1]], 0, 1)
+        for b in (5, 6, 7, 3, 2, 1):
+            fill(A("sp", b * SW + M - SO, b * SW + SW - SO), 0)
+
+    def more_lists():
+        tt(A("fa"), A("srcf"), A("t2"), ALU.subtract)
+        ts(A("lg"), A("fa"), float(SW), ALU.add)
+        ts(A("cli", 1, 2), A("cli", 0, 1), 15, ALU.bitwise_and)
+        ts(A("clf", 0, 1), A("cli", 1, 2), 128.0, ALU.subtract)
+        ts(A("x8"), A("dlyi"), 128.0, ALU.mult, A("clf", 0, 1), ALU.add)
+        ts(A("la"), A("dlyi"), 1.0, ALU.subtract, float(ZW), ALU.mult)
+        rowwise(A("lp"), A("srci"), 192, A("la"), A("px1", 0, 192))
+        rowwise(A("lsp"), A("sndi"), 64, None, A("px1", 256, 288))
+
+    def constants():
+        fill(A("one16"), 1)
+        fill(A("h16"), 0)
+        sel(A("h16", 15, 144, 16), A("one16", 0, 9), [[-16, 9]], ALU.is_ge, 0, 1)
+        sel(A("h16", 15, 144, 16), A("h16", 15, 144, 16), [[16, 9]], ALU.is_ge, 15, -1)
+        sel(A("k16", 15, 144, 16), A("one16", 0, 9), [[-16, 9]], ALU.is_equal, 0, 1)
+        sel(A("pd32", 0, 128), A("pd32", 0, 128), [[-2, 64], [1, 2]], ALU.is_equal, -1, 1)
+        sel(A("pd32", 128, 256), A("pd32", 128, 256), [[-4, 32], [2, 2], [-1, 2]], ALU.is_equal, -2, 1)
+        tt(A("pp16"), A("pd32"), A("ii32"), ALU.add)
+        tt(A("pd32"), A("pd32"), A("ii32"), ALU.subtract)
+        cp(A("pd16"), A("pd32"))
+        fill(A("rl", 0, 64), 0); fill(A("rl", RW, RW + 64), 0)
+
+    def f_open(e, t, T):
+        at(T - 1.5)
+        both("pv", [(ID(1.0), "dr", 0), (ID(-2.0 ** (t - 7)), "sp", spos(e, t - 1)), (A("hf16"), "mm", mpos(t - 1))], True, False)
+
+    def f_gather(e, t, T):
+        s, y, w = 2.0 ** (4 - t), ypos(e, t), (t - 1) * KV
+        if t == 1:
+            win, lst = A("sp", p0, p0 + SW), "lt1"
+        else:
+            lo = min(spos(e, t - 1), spos(e, t - 2))
+            win, lst = A("sp", lo, lo + 2 * SW), "lg"
+        for k in range(3):
+            yk, wk, lk = third("yb", y, k), third("wt", w, k), A(lst, 64 * k, 64 * k + 64)
+            at(T + 1.4 * k)
+            if k < O["ysplit"][e][t - 1]:
+                gat("a", yk, win, lk)
+                at(T + 3.0)
+                tt(yk, yk, wk, ALU.min)
+            else:
+                tt(yk, IND(win, lk), wk, ALU.min)
+            at(T + 1.4 * k + 1.5)
+            both("pv", [(ID(s), "yb", y + k * V)], False, k == 2)
+
+    def smode(e, t):
+        return "v" if O["spike"][e][t - 1] == "m" and t == 4 else O["spike"][e][t - 1]
+
+    def f_spike(e, t, T):
+        s, p, mode = 2.0 ** (4 - t), spos(e, t), smode(e, t)
+        at(T + 4.35)
+        for h in range(2):
+            if mode == "v":
+                ts(half("sp", p, h), half("pv", 0, h), 1.0, ALU.is_ge, 2.0 * s, ALU.mult)
+            elif mode == "m":
+                ts(half("mm", mpos(t), h), half("pv", 0, h), 1.0, ALU.min)
+                ts(half("sp", p, h), half("mm", mpos(t), h), 1.0, ALU.is_ge, 2.0 * s, ALU.mult)
+            else:
+                q = half("qq", t % 2 * V, h)
+                act(q, half("pv", 0, h), ACT.Sign, 2.0 ** -12 - 1.0)
+                if mode == "x":
+                    ts(half("sp", p, h), q, s, ALU.mult, s, ALU.add)
+                else:
+                    act(half("sp", p, h), q, ACT.Identity, s, s)
+        if t < 4:
+            send_spikes(e, t, T + O["send"][e])
+        if e < 2 and O["vote"][e][t - 1] in "sbc" and mode in "vm":
+            act(third("qq", 0, t % 2), A("pv"), ACT.Sign, 2.0 ** -12 - 1.0)
+
+    def f_keep(e, t, T):
+        at(T + 5.3)
+        if t < 4 and smode(e, t) != "m":
+            ts(third("mm", mpos(t), 0), A("pv"), 1.0, ALU.min)
+
+    def f_slope(e, t, T, T2):
+        s, y, a = 2.0 ** (4 - t), ypos(e, t), third("aa", apos(e, t), 0)
+        late = e == 2 and t < 4 and t in O["late"]
+        small = t == 4 and e < 2 or late
+        for h in range(2):
+            at(T + h)
+            bank = A("px%d" % (0 if late else h))
+            terms = [(ID(1.0), half("dr", 0, h))] + [(ID(s), half("yb", y + k * V, h)) for k in range(3)]
+            if t == 4:
+                at(T - 1.4 + 0.1 * h)
+                group(bank if small else half("pq", 0, h), terms[:3], True, False)
+                at(T - 0.05 + 0.1 * h)
+                group(bank if small else half("pq", 0, h), terms[3:], False, True)
+            else:
+                group(bank if small else half("pq", 0, h), terms + [(ID(4.0 / s), half("sp", spos(e, t), h))])
+            if small:
+                act(half("aa", a[1], h), bank, ACT.Identity, s * ((211 if t < 4 else 195) - 1 / 64), -2.0 * s)
+        at(T + 2.5)
+        if not small:
+            act(a, A("pq"), ACT.Identity, s * ((211 if t < 4 else 195) - 1 / 64), -2.0 * s)
+        at(T2)
+        if O["afix"][e] == "v":
+            ts(a, a, 192.0 * s, ALU.subtract, 0.5 * s, ALU.max)
+        else:
+            act(a, a, ACT.Relu, -192.5 * s)
+            act(a, a, ACT.Identity, 0.5 * s)
+
+    def f_vote(e, t, Ts):
+        y, p, b, vote = ypos(e, t), spos(e, t), PB[e][t - 1] * KV, O["vote"][e][t - 1]
+        for k in range(3):
+            at(Ts[k])
+            o, yk = third("yb", b, k), third("yb", y, k)
+            if vote == "s" or (vote == "b" and k > 0) or (vote == "c" and k > 1):
+                tt(o, yk, third("qq", 0, t % 2), ALU.mult)
+            elif vote == "m":
+                tt(o, yk, A("sp", p, p + V), ALU.min)
+            else:
+                bank = "pk" if e == 0 else "pq"
+                both(bank, [(ID(1 / 8), "yb", y + k * V), (ID(-1 / 8), "sp", p)])
+                act(o, A(bank), ACT.Relu, 0.0, 2.0 ** (7 - t))
+
+    def diffs(e, bank):
+        mm(A(bank, 0, 192), A("pd32", 128 * e, 128 * e + 128), A("srcf"))
+        mm(A(bank, 256, 448), A("pd16", 128 * e, 128 * e + 128), A("x8"))
+        act(A("t1"), A(bank, 0, 192), ACT.Copy)
+        act(A("d8"), A(bank, 256, 448), ACT.Copy)
+
+    def exchange(e, T):
+        vb = 8 * KV
+        for k in range(3):
+            bank = ("pq", "pk", "pv")[k]
+            for h in range(2):
+                terms = []
+                for t in range(1, 5):
+                    if t == 4:
+                        at(T + (0.2, 3.1, 6.5)[k] + 0.1 * h)
+                        group(half(bank, 0, h), terms, True, False)
+                        at(T + O["vat"][e][1][k] + 1.0 + 0.1 * h)
+                        terms = []
+                    b, y = half("yb", PB[e][t - 1] * KV + k * V, h), half("yb", ypos(e, t) + k * V, h)
+                    vote = O["vote"][e][t - 1]
+                    if vote == "s" or (vote == "b" and k > 0) or (vote == "c" and k > 1):
+                        terms += [(ID(2.0 ** -t), b)]
+                    elif vote == "m":
+                        terms += [(ID(-2.0 ** -t), y), (ID(2.0 ** (1 - t)), b)]
+                    else:
+                        terms += [(ID(2.0 ** -t), y), (ID(-1 / 8), b)]
+                group(half(bank, 0, h), terms, False, True)
+                if O["xhalf"]:
+                    act(half("yb", vb + k * V, h), half(bank, 0, h), ACT.Sign, -EPS / 32)
+            if not O["xhalf"]:
+                act(third("yb", vb, k), A(bank), ACT.Sign, -EPS / 32)
+            at(T + O["vat"][e][1][k] + 2.3)
+            wrap(A("px0", 64 * k, 64 * k + 64), "h16", "yb", vb + k * V, V)
+        X0, X1 = A("px0", 0, 192), A("px0", 256, 448)
+        at(T + O["xat"][0])
+        ts(A("eag"), X0, 1.0, ALU.is_ge)
+        mm(X1, A("pp16", 128 * e, 128 * e + 128), A("eag"))
+        at(T + O["xat"][1])
+        ts(X1, X1, 1.5, ALU.is_ge)
+        tt(X0, X1, A("t1"), ALU.mult)
+        tt(A("fd"), X0, A("fd"), ALU.add)
+        ts(A("lt1"), A("fd"), float(M), ALU.min)
+        at(T + O["xat"][2])
+        tt(A("cod"), X1, A("d8"), ALU.mult)
+        tt(A("fa"), X0, A("fa"), ALU.add)
         if e == 0:
+            tt(A("srcf"), X0, A("srcf"), ALU.add)
+            act(A("swp"), X1, ACT.Copy)
             cp(A("lg"), A("fd"))
-            tt(A("srcf"), A("srcf"), A("t1"), ALU.add)
         else:
             ts(A("lg"), A("fa"), float(SW), ALU.add)
-        tt(A("cod"), A("t3"), A("swp"), ALU.mult)
 
     def back_lists(e):
         o = 192 * (e % 2)
-        tt(A("t2"), A("slot"), A("e1"), ALU.add)
-        cp(A("lba", o, o + 192), A("t2"))
-        ts(A("lb3", o, o + 192), A("t2"), float(KV), ALU.min)
-        tt(A("t4", 0, 192), A("slot"), A("e1"), ALU.subtract)
-        ts(A("lbb", o, o + 192), A("t4", 0, 192), float(ZW), ALU.add)
-        if e < 2:
-            cp(A("lbs"), A("slot"))
+        ts(A("lb3", o, o + 192), A("la"), float(KV), ALU.min)
+        cp(A("lba", o, o + 192), A("la"))
+        cp(A("lbb", o, o + 192), A("lb"))
 
-    def invert():
-        ts(A("t2"), A("dlyi"), 4096.0, ALU.mult, A("clf", 0, 1), ALU.subtract)
-        tt(A("t4", 0, 192), A("ioi"), A("t2"), ALU.add)
-        ts(A("t4", 192, 224), A("ioi", 0, 32), A("clf", 0, 1), ALU.subtract, 64.0, ALU.add)
-        for i in range(16):
-            act(A("zz", i, 3584, 16), A("t4"), ACT.Identity, 0.0, A("mk", i, i + 1))
+    def invert_in():
         fill(A("rg"), 0)
-        for c in range(7):
-            dst = IND(A("zg"), A("lp", 32 * c, 32 * c + 32)) if c < 6 else IND(A("rg"), A("lsn"))
-            if O["sc_eng"][c] == "a":
-                act(dst, half("zz", 0, c), ACT.Silu, extra=1300 if "a" not in O["sc_eng"][:c] else 0)
-            else:
-                cp(dst, half("zz", 0, c))
-        wrap(A("px1", 0, 192), "h32", "zg", 0, KV)
-        cp(A("srci"), A("px1", 0, 192))
-        wrap(A("px1", 0, 64), "h32", "rg", 0, V)
-        cp(A("ioi", 0, 64), A("px1", 0, 64))
-        cp(A("lr"), A("ioi", 0, 64))
-        ts(A("ioi"), A("srci"), 4095, ALU.bitwise_and)
-        cp(A("slot"), A("ioi"))
-        ts(A("srci"), A("srci"), 12, ALU.logical_shift_right)
-        ts(A("e1"), A("srci"), 1.0, ALU.subtract, float(ZW), ALU.mult)
-        back_lists(0)
-        fill(A("zz", KV, ZW), 0); fill(A("zz", ZW + KV, 2 * ZW), 0)
-        fill(A("rl", 0, 64), 0); fill(A("rl", RW, RW + 64), 0)
+        for c in range(6):
+            dma("s", third("zz", 0, c), A("rg"))
+        fill(A("zz", 6 * V, 2 * ZW), 0)
+        for c in range(6):
+            iota(half("zg", 0, c), [[1, 512]], 64 + 512 * c, 0)
 
-    def follow(e):
+    def scatter(some):
+        for c in some:
+            dst = IND(A("zz"), A("lp", 32 * c, 32 * c + 32)) if c < 6 else IND(A("rg"), A("lsp"))
+            if O["sc_eng"][c] == "a":
+                act(dst, half("zg", 0, c % 6), ACT.Silu, extra=1300 if "a" not in O["sc_eng"][:c] else 0)
+            else:
+                cp(dst, half("zg", 0, c % 6))
+
+    def invert_out():
+        P0 = A("px1", 0, 192)
+        cat("uncat", A("la"), A("zz", 0, KV))
+        cat("uncat", A("lb"), A("zz", ZW, ZW + KV))
+        cat("uncat", A("t2", 0, 64), A("rg"))
+        act(P0, A("lb"), ACT.Identity, -64.0)
+        tt(P0, P0, A("la"), ALU.add)
+        cp(A("srci"), P0)
+        ts(P0, A("lb"), 8.0, ALU.is_ge, float(ZW), ALU.mult)
+        tt(A("la"), P0, A("srci"), ALU.add)
+        ts(P0, A("lb"), 8.0, ALU.is_lt, float(ZW), ALU.mult)
+        tt(A("lb"), P0, A("srci"), ALU.add)
+        back_lists(0)
+        cp(A("ioi", 0, 64), A("t2", 0, 64))
+        cp(A("lr"), A("ioi", 0, 64))
+        rowwise(A("lbs"), A("srci"), 192, None, P0)
+        dma("s", A("yb", 9 * KV, 10 * KV), A("w", 0, KV))
+
+    def follow_a(e, T, Ts):
         ab, gb = 9 * KV, (8 if e == 0 else 3) * KV
-        for i in range(16):
-            act(A("yb", ab + i, ab + KV, 16), A("cod"), ACT.Identity, 0.0, A("mk", i, i + 1))
+        at(T)
+        if e == 1:
+            mm(A("pq", 0, 192), A("pd16", 0, 128), A("cod"))
+            tt(A("swp"), A("pq", 0, 192), A("swp"), ALU.mult)
+            tt(A("cod"), A("cod"), A("swp"), ALU.add)
+        cat("cat", A("yb", ab, ab + KV), A("cod"))
         for k in range(3):
-            gat("a", A("yb", gb + k * V, gb + k * V + V), A("yb", ab, ab + KV), A("lbs", 64 * k, 64 * k + 64))
-        wrap(A("px1", 0, 192), "h16", "yb", gb, KV)
-        ts(A("t2"), A("px1", 0, 192), 4.0, ALU.is_ge, 8.0, ALU.mult)
-        ts(A("t4", 0, 192), A("px1", 0, 192), -4.0, ALU.is_le, -8.0, ALU.mult)
-        tt(A("slot"), A("slot"), A("px1", 0, 192), ALU.add)
-        tt(A("t2"), A("t2"), A("t4", 0, 192), ALU.add)
-        tt(A("slot"), A("slot"), A("t2"), ALU.subtract)
-        ts(A("t2"), A("t2"), ZW / 8.0, ALU.mult)
-        tt(A("e1"), A("e1"), A("t2"), ALU.add)
+            at(Ts[k])
+            gat("a", third("yb", gb, k), A("yb", ab, ab + KV), A("lbs", 64 * k, 64 * k + 64))
+
+    def follow_b(e, T):
+        bank, gb = "pq", (8 if e == 0 else 3) * KV
+        P0, P1 = A(bank, 0, 192), A(bank, 256, 448)
+        at(T - 2.0)
+        wrap(P0, "k16", "yb", gb)
+        at(T)
+        act(A("eag"), P0, ACT.Identity, 3072.0)
+        tt(A("la"), P0, A("la"), ALU.add)
+        tt(A("lb"), P0, A("lb"), ALU.add)
+        for n, c in (("la", ZW / 128 - 1), ("lb", -ZW / 128 - 1)):
+            act(P1, A("eag"), ACT.Identity, -3072.0 * c, c)
+            tt(A(n), P1, A(n), ALU.add)
         back_lists(e + 1)
         if e == 0:
-            diffs(1)
+            diffs(1, bank)
 
-    def count(e, bank):
+    def count(e, bank="pq"):
         for h in range(2):
-            terms = [(ID(-2.0 ** (s - 5)), half("sp", spos(e, s), h)) for s in range(5)]
-            if e > 0:
-                terms.append((ID(1.0), half("cn", 0, h)))
-            group(A(bank), terms)
-            act(half("cn", 0, h), A(bank), ACT.Identity, 0.0, -1.0 if e == 2 else 1.0)
+            terms = [(ID(2.0 ** (s - 5)), half("sp", spos(x, s), h)) for x in ([1, 2] if e == 2 and O["cpos"][1] > 4 else [e]) for s in range(5)]
+            group(half(bank, 0, h if bank == "pq" else 0), terms + ([(ID(1.0), half("cn", 0, h))] if e else []))
+            if bank != "pq":
+                act(half("cn", 0, h), A(bank), ACT.Copy)
+        if bank == "pq":
+            act(A("cn"), A("pq"), ACT.Copy)
         if e == 2:
             dma("g", A("cnt", 0, V), A("cn"))
 
     def recip_a():
         for k in range(3):
-            act(A("rc", k * V, k * V + V), A("wt", 3 * KV + k * V, 3 * KV + k * V + V), ACT.Ln, extra=0 if k else 1500)
-            ops[-1]["rd"].append(A("cn"))
+            act(third("rc", 0, k), third("wt", 3 * KV, k), ACT.Ln, extra=0 if k else 1500)
+            ops[-1]["rd"].append(A("lr"))
         for k in range(3):
-            act(A("rc", k * V, k * V + V), A("rc", k * V, k * V + V), ACT.Exp, 0.0, -1.0, extra=0 if k else 1500)
+            act(third("rc", 0, k), third("rc", 0, k), ACT.Exp, 0.0, -1.0, extra=0 if k else 1500)
             if k == 0:
                 ops[-1]["rd"].append(A("rc"))
 
-    def recip_b():
+    def recip_b(k, bank):
+        r = third("rc", 0, k)
+        both(bank, [(ID(1.0), "wt", 3 * KV + k * V)])
+        tt(A(bank), A(bank), r, ALU.mult)
+        act(A(bank), A(bank), ACT.Identity, 2.0, -1.0)
+        tt(r, A(bank), r, ALU.mult)
+
+    lbuf = lambda e, t: "pk" if e < 2 else ("pv", "pq")[t % 2]
+    land = lambda e, t: ((3 * e + 3 - t) % 2) * RW
+
+    def finish(z, add_z, Z):
         for k in range(3):
-            r = A("rc", k * V, k * V + V)
-            for h in range(2):
-                mm(half("pv", 0, h), ID(1.0), half("wt", 3 * KV + k * V, h), True, True)
-            tt(A("pv"), A("pv"), r, ALU.mult)
-            act(A("pv"), A("pv"), ACT.Identity, 2.0, -1.0)
-            tt(r, A("pv"), r, ALU.mult)
+            a, bank = third("acc", 0, k), "pk"
+            if add_z == "d":
+                at(Z + O["gam"][1][k])
+                dma("g", a, third("zz", z, k), True)
+            at(Z + O["fat"][k] - 2.0)
+            if O["rps"]:
+                act(A(bank), third("rc", 0, k), ACT.Copy)
+            else:
+                for h in range(2):
+                    mm(half(bank, 0, h), I32F, half("acc", k * V, h))
+            at(Z + O["fat"][k])
+            tt(a, A(bank), a if O["rps"] else third("rc", 0, k), ALU.mult)
+            dma("s", third("gam", 0, k), a)
 
-    nstep = [0]
-    lbuf = lambda e, t: A("pv" if (e, t) == (2, 4) else "pl")
-
-    def zprod(e, t):
+    def b_z(e, t, Z):
         z, y = (t % 2) * ZW, ypos(e, t)
         for k in range(3):
-            tt(A("zz", z + k * V, z + k * V + V), A("yb", y + k * V, y + k * V + V), lbuf(e, t), ALU.mult)
-        if e == 2 and t <= O["nt"]:
-            b = (9 if t == 1 else 3) * KV
-            ts(A("yb", b, b + KV), A("yb", y, y + KV), 2.0 ** 40, ALU.mult)
-            act(A("pv"), A("pl"), ACT.Identity, 0.0, 2.0 ** (t - 4))
-            for k in range(3):
-                r = A("rc", k * V, k * V + V)
-                tt(r, A("yb", b + k * V, b + k * V + V), A("pv"), ALU.min)
-                dma("g", A("gam", k * V, k * V + V), r, True)
-            return
-        if e == 0 and t == 4:
-            dma("s", A("acc"), A("zz", z, z + KV))
-        elif e == 2 and t == O["nt"] + 1:
-            for k in range(3):
-                a = A("acc", k * V, k * V + V)
-                dma("g", a, A("zz", z + k * V, z + k * V + V), True)
-                if O["rps"]:
-                    act(A("pv"), A("rc", k * V, k * V + V), ACT.Copy)
-                tt(a, a, A("pv") if O["rps"] else A("rc", k * V, k * V + V), ALU.mult)
-                dma("s", A("gam", k * V, k * V + V), a)
-        else:
-            c = KV // O["split"]
-            for k in range(O["split"]):
-                dma("g", A("acc", k * c, k * c + c), A("zz", z + k * c, z + k * c + c), True)
+            at(Z - 2.7 + 0.9 * k)
+            tt(third("zz", z, k), third("yb", y, k), A(lbuf(e, t)), ALU.mult)
 
-    def backward(e):
-        o = 192 * (e % 2)
-        ew, e2, er = O["tail"] if e == 2 else "aaa"
-        a4, p4 = apos(e, 4), spos(e, 4)
-        for h in range(2):
-            mm(half("pk", 0, h), ID(1.0), half("ls", 0, h), True, True)
-        tt(A("pk"), A("pk"), A("aa", a4, a4 + V), ALU.mult)
-        tt(lbuf(e, 4), A("pk"), A("sp", p4, p4 + V), ALU.min)
-        zprod(e, 4)
-        for t in range(3, -1 if e == 2 else 0, -1):
-            win = A("zz", 0, ZW) if t == 3 else A("zz")
-            lst = "lb3" if t == 3 else "lbb" if t % 2 == 0 else "lba"
-            p, a = spos(e, t), apos(e, t)
-            r = (nstep[0] % 2) * RW
-            nstep[0] += 1
-            L = lambda c0, c1: A(lst, o + c0, o + c1)
-            if e == 2:
-                gat("a", A("zg", V, V + H), win, L(64, 80))
-                gat(ew, A("zg", M + V, M + V + H), win, L(160, 176))
-                gat("a", A("zg", V + H, M), win, L(80, 96))
-                gat(ew, A("zg", M + V + H, KV), win, L(176, 192))
-            else:
-                gat("a", A("zg", V, M), win, L(64, 96))
-                gat(ew, A("zg", M + V, KV), win, L(160, 192))
-            group(A("px1", 0, H), [(SH32, A("zg", V, V + H)), (SH32, A("zg", M + V, M + V + H))])
-            act(A("sb"), A("px1", 0, H), ACT.Copy)
-            rem([(-1, [A("sb")], A("rl", r + 64, r + 64 + H)),
-                 (1, [A("zg", V + H, M), A("zg", M + V + H, KV)], A("rl", r + 64 + H, r + RW))])
-            for h in range(2):
-                lift = [(ID(2.0), A("one16")), (ID(-2.0 ** (t - 4)), half("sp", p, h))] if t == 0 else []
-                group(half("pk", 0, h), lift + [(ID(1.0), half("ls", 0, h))], True, False)
-            gat("a", A("zg", 0, V), win, L(0, 64))
-            mode = O["own"][e]
-            fuse = e == 2 and O["fuse"]
-            if mode == "v":
-                tt(A("zg", M, M + V), IND(win, L(96, 160)), A("zg", 0, V), ALU.add)
-            else:
-                gat(e2, A("zg", M, M + V), win, L(96, 160))
-            if mode == "d":
-                dma("g", A("zg", M, M + V), A("zg", 0, V), True)
-            if mode == "p":
-                for h in range(2):
-                    mm(half("pk", 0, h), I32F, half("zg", 0, h), False, False)
-            for h in range(2):
-                mm(half("pk", 0, h), I32F, half("zg", M, h), False, fuse)
-            tt(A("cap"), lbuf(e, t + 1), A("sp", p, p + V), ALU.max)
-            if e == 2 and t == 3:
-                recip_b()
-            if t == 0:
-                act(A("cap"), A("cap"), ACT.Identity, 0.0, 1 / 16)
-            for h in range(2):
-                if fuse:
-                    tt(half("pk", 0, h), half("pk", 0, h), half("aa", a, h), ALU.mult)
-                    tt(half("rg", 0, h), IND(A("rl", r, r + RW), A("lr", 32 * h, 32 * h + 32)), half("aa", a, h), ALU.mult)
-                    tt(half("pk", 0, h), half("pk", 0, h), half("rg", 0, h), ALU.add)
+    def b_gamma(e, t, Z):
+        z, y, fin = (t % 2) * ZW, ypos(e, t), O["fin"]
+        if e == 2 and t == 1 and fin == "m":
+            b = 9 * KV
+            at(Z - 8.0)
+            for k in range(3):
+                if O["big"] == "v":
+                    ts(third("yb", b, k), third("yb", y, k), 2.0 ** 40, ALU.mult)
                 else:
-                    gat("a" if h == 0 else er, half("rg", 0, h), A("rl", r, r + RW), A("lr", 32 * h, 32 * h + 32))
-                    mm(half("pk", 0, h), I32F, half("rg", 0, h), False, True)
-                    tt(half("pk", 0, h), half("pk", 0, h), half("aa", a, h), ALU.mult)
-                tt(half("pl" if t else "rg", 0, h), half("pk", 0, h), half("cap", 0, h), ALU.min)
-                if t == 0:
-                    dma("s", half("lam", 0, h), half("rg", 0, h))
-            if t > 0:
-                zprod(e, t)
-            if e < 2 and t == O["fpos"][e]:
-                follow(e)
-            if e < 2 and t == O["cpos"][e]:
-                count(e, "px1")
+                    act(third("yb", b, k), third("yb", y, k), ACT.Identity, 0.0, 2.0 ** 40)
+            at(Z + 0.05)
+            act(A("pk"), A(lbuf(e, t)), ACT.Identity, 0.0, 2.0 ** (t - 4))
+            at(Z + 1.5)
+            for k in range(3):
+                tt(third("rc", 0, k), third("yb", b, k), A("pk"), ALU.min)
+                dma("g", third("gam", 0, k), third("rc", 0, k), True)
+        elif e == 0 and t == 4:
+            at(Z + 3.6)
+            dma("s", A("acc"), A("zz", z, z + KV))
+        elif e == 2 and t == (2 if fin == "m" else 1):
+            finish(z, "d" if fin == "m" else fin, Z)
+        else:
+            for k in range(3):
+                at(Z + O["gam"][e == 2][k])
+                dma("g", third("acc", 0, k), third("zz", z, k), True)
 
-    invert()
-    diffs(0)
-    forward(0); exchange(0); backward(0)
-    forward(1); exchange(1); backward(1)
-    recip_a()
-    forward(2); count(2, "px0"); backward(2)
+    def b_first(e, Z):
+        x = lbuf(e, 4)
+        at(Z - 6.0)
+        both(x, [(ID(1.0), "ls", 0)])
+        at(Z - 4.5)
+        tt(A(x), A(x), third("aa", apos(e, 4), 0), ALU.mult)
+        tt(A(x), A(x), third("sp", spos(e, 4), 0), ALU.min)
+        b_z(e, 4, Z)
+
+    def b_lists(e, t):
+        o = 192 * (e % 2)
+        lst = "lb3" if t == 3 else "lbb" if t % 2 == 0 else "lba"
+        return (A("zz", 0, ZW) if t == 3 else A("zz")), lambda c0, c1: A(lst, o + c0, o + c1)
+
+    def b_wires(e, t, Z):
+        (win, L), r, ew = b_lists(e, t), land(e, t), O["tail"][0] if e == 2 else "a"
+        at(Z + 0.1)
+        if O["wsplit"][e]:
+            gat("a", A("zg", V, V + H), win, L(64, 80))
+            gat(ew, A("zg", M + V, M + V + H), win, L(160, 176))
+            gat("a", A("zg", V + H, M), win, L(80, 96))
+            gat(ew, A("zg", M + V + H, KV), win, L(176, 192))
+        else:
+            gat("a", A("zg", V, M), win, L(64, 96))
+            gat("a", A("zg", M + V, KV), win, L(160, 192))
+        at(Z + O["bat"][e == 2][0])
+        mm(A("px1", 0, H), SH32, A("zg", V, V + H), True, False)
+        mm(A("px1", 0, H), SH32, A("zg", M + V, M + V + H), False, True)
+        at(Z + O["bat"][e == 2][1])
+        act(A("sb"), A("px1", 0, H), ACT.Copy)
+        rem([(-1, [A("sb")], A("rl", r + 64, r + 64 + H)),
+             (1, [A("zg", V + H, M), A("zg", M + V + H, KV)], A("rl", r + 64 + H, r + RW))])
+        ops[-1]["rd"].append(A("rg"))
+
+    def b_cap(e, t, Z):
+        at(Z + (0.5 if e < 2 else 4.5))
+        cap = A("cap") if e < 2 else A(lbuf(e, t + 1))
+        tt(cap, A(lbuf(e, t + 1)), third("sp", spos(e, t), 0), ALU.max)
+        if t == 0:
+            act(cap, cap, ACT.Identity, 0.0, 1 / 16)
+
+    def b_own(e, t, Z):
+        (win, L), own, b, x = b_lists(e, t), O["own"][e], O["bat"][e == 2], lbuf(e, t)
+        at(Z + b[0] + 0.1)
+        lift = [(ID(2.0), "one16", 0), (ID(-2.0 ** (t - 4)), "sp", spos(e, t))] if t == 0 else []
+        both(x, lift + [(ID(1.0), "ls", 0)], True, False)
+        n = O["parts"][e]
+        for c in range(n):
+            w = V // n
+            a0, a1 = A("zg", c * w, c * w + w), A("zg", M + c * w, M + c * w + w)
+            at(Z + b[2] + c * b[4])
+            gat("a", a0, win, L(c * w // 16, (c * w + w) // 16))
+            at(Z + b[3] + c * b[4])
+            l1 = L(96 + c * w // 16, 96 + (c * w + w) // 16)
+            if own == "v":
+                tt(a1, IND(win, l1), a0, ALU.add)
+            else:
+                gat(O["tail"][1] if e == 2 else "a", a1, win, l1)
+        if own == "d":
+            dma("g", A("zg", M, M + V), A("zg", 0, V), True)
+        if own == "p":
+            at(Z + b[2] + 1.5)
+            for h in range(2):
+                mm(half(x, 0, h), I32F, half("zg", 0, h), False, False)
+        at(Z + b[3] + 1.5)
+        for h in range(2):
+            mm(half(x, 0, h), I32F, half("zg", M, h), False, False)
+
+    def b_back(e, t, R):
+        r = land(e, t)
+        for h in range(2):
+            both = e == 2 and O["tail"][2] == "v"
+            at(R + (0 if both else 0.8 * h))
+            gat("v" if both and h else "a", half("rg", 0, h), A("rl", r, r + RW), A("lr", 32 * h, 32 * h + 32))
+            at(R + 0.95 + 0.9 * h)
+            mm(half(lbuf(e, t), 0, h), I32F, half("rg", 0, h), False, True)
+
+    def b_lam(e, t, Z):
+        a = apos(e, t)
+        at(Z - 4.6)
+        if e < 2 and O["whole"][e]:
+            tt(A("pk"), A("pk"), third("aa", a, 0), ALU.mult)
+            tt(A("pk"), A("pk"), A("cap"), ALU.min)
+        elif e < 2:
+            for h in range(2):
+                tt(half("pk", 0, h), half("pk", 0, h), half("aa", a, h), ALU.mult)
+                tt(half("pk", 0, h), half("pk", 0, h), half("cap", 0, h), ALU.min)
+        else:
+            for h in range(2):
+                tt(half("rg", 0, h), half(lbuf(e, t), 0, h), half("aa", a, h), ALU.mult)
+                tt(half(lbuf(e, t) if t else "cap", 0, h), half(lbuf(e, t + 1), 0, h), half("rg", 0, h), ALU.min)
+                if t == 0:
+                    dma("s", half("lam", 0, h), half("cap", 0, h))
+        if t > 0:
+            b_z(e, t, Z)
+
+    def b_next(e, t, Z):
+        if t > (0 if e == 2 else 1):
+            b_wires(e, t - 1, Z)
+        if (e, t) == (2, 4) and O["defer"]:
+            b_lam(1, 1, Z + 5.6)
+            b_gamma(1, 1, Z + 5.6)
+            Z += O["g4"]
+        b_gamma(e, t, Z)
+        if (e, t) == (2, 4) and O["defer"]:
+            Z -= O["g4"]
+        if t > (0 if e == 2 else 1):
+            b_cap(e, t - 1, Z)
+            b_own(e, t - 1, Z)
+
+    def slope0():
+        act(A("aa", 0, V), A("dr"), ACT.Identity, 195 - 1 / 64, -2.0)
+        ts(A("aa", 0, V), A("aa", 0, V), 192.0, ALU.subtract, 0.5, ALU.max)
+
+    start()
+    at(2.0)
+    scaled(SC[4:])
+    invert_in()
+    extras = {1: [(O["mat"], more_lists), (6.4, lambda: weights(2)), (7.8, constants)] + [(O["sat"] + 1.6 * c, lambda c=c: scatter([c])) for c in range(7)],
+              2: [(6.3, lambda: weights(3)), (11.0, lambda: diffs(0, "px1"))],
+              3: [(6.3, lambda: weights(4)), (6.4, invert_out)]}
+    T, Z = 8.0, 0.0
+    for e in range(3):
+        for t in range(1, 5):
+            u, beat = 4 - t if e and t < 4 else 0, O["beat"][e]
+            f_open(e, t, T)
+            if u:
+                b_back(e - 1, u, Z + O["rat"][0])
+                Z += O["zbeat"][e]
+            f_gather(e, t, T)
+            if t == 4:
+                f_slope(e, t, T + 4.4, T + O["x4"][e][0])
+            f_spike(e, t, T)
+            f_keep(e, t, T)
+            if e and t == O["fpos"][e - 1]:
+                follow_b(e - 1, T + 6.2)
+            if t < 4 and not (e == 2 and t in O["late"]):
+                f_slope(e, t, T + 7.5, T + beat + 6.05)
+            if u and not (e == 2 and u == 1 and O["defer"]):
+                b_lam(e - 1, u, Z)
+                b_next(e - 1, u, Z)
+            if e and t == O["fpos"][e - 1] - 1:
+                follow_a(e - 1, T + 5.5, [T + 8.5, T + 10.1, T + 10.2])
+            for x, f in extras.get(t, []) if e == 0 else []:
+                at(T + x)
+                f()
+            if e < 2:
+                f_vote(e, t, [T + x for x in O["vat"][e][t == 4]])
+            if e and t == O["cpos"][e - 1]:
+                at(T + 11.0)
+                count(e - 1)
+            if 4 * e + t == O["rpos"] + 8:
+                at(T + 8.0)
+                recip_a()
+            for k in O["rb"].get(10 + t, []) if e == 2 else []:
+                at(T + 6.4)
+                recip_b(k, "pq")
+            if e == 2 and t == 1:
+                at(T + 6.3)
+                slope0()
+            if t < 4:
+                T += beat
+        if e < 2:
+            exchange(e, T)
+        Z = T + O["x4"][e][1]
+        b_first(e, Z)
+        b_next(e, 4, Z)
+        T += O["x4"][e][2]
+    for t in (3, 2, 1, 0):
+        if t in O["late"]:
+            f_slope(2, t, Z - 5.0, Z + 4.0)
+        if t == O["cend"]:
+            at(Z + 3.0)
+            count(2, "px0")
+        for k in O["rb"].get(t, []):
+            at(Z + 2.5 + k)
+            recip_b(k, "pk")
+        b_back(2, t, Z + O["rat"][1])
+        Z += 12.0
+        b_lam(2, t, Z)
+        if t:
+            b_next(2, t, Z)
     return ops
 
 
@@ -548,7 +779,7 @@ def link(ops):
                 if landing:
                     continue
                 if w or w2 or (ps and ops[j]["eng"] != op["eng"]):
-                    kind = "lo" if (ops[j]["kind"] in ("rem", "fold") and not w2) else "ar"
+                    kind = "lo" if (ops[j]["kind"] == "rem" and not w2) else "ar"
                     dep.setdefault(j, set()).add(kind)
         op["dep"] = dep
         for a, w in acc:
@@ -562,80 +793,265 @@ def link(ops):
             hl.append((i, lo, hi, w, a[3], a[1]))
 
 
-def gap(ops, j, i, C):
-    a, b = ops[j], ops[i]
-    if a["eng"] == b["eng"] and not a["lat"]:
-        return 0.0 if a["eng"] == "p" else C["same"]
-    return C["wake"]
-
-
 def graph(ops, C):
     n = len(ops)
-    succ = [[] for _ in ops]
+    succ, pred, above = [[] for _ in ops], [[] for _ in ops], [0] * n
     for i, op in enumerate(ops):
-        for j in op["dep"]:
-            succ[j].append((i, gap(ops, j, i, C)))
-    pr = [0.0] * n
-    for i in range(n - 1, -1, -1):
-        pr[i] = ops[i]["dur"] + ops[i]["lat"] + ops[i]["dby"] + max([x + pr[k] for k, x in succ[i]] + [0.0])
-    return (["vapgs".index(o["eng"]) for o in ops], [o["dur"] for o in ops], [o["lat"] for o in ops], [o["dby"] for o in ops],
-            succ, [len(o["dep"]) for o in ops], pr)
+        for j in sorted(op["dep"], reverse=True):
+            if not above[i] >> j & 1:
+                same = ops[j]["eng"] == op["eng"] and not ops[j]["lat"]
+                x = C["wake"] if not same else 0.0 if op["eng"] == "p" else C["same"]
+                succ[j].append((i, x)); pred[i].append((j, x))
+                above[i] |= above[j] | 1 << j
+    return (["vapgs".index(o["eng"]) for o in ops], [o["dur"] for o in ops], [o["lat"] for o in ops], [o["dby"] for o in ops], succ, pred)
 
 
-def schedule(G, pr, slack):
-    eng, dur, lat, dby, succ, ndep, _ = G
-    n = len(eng)
-    left = list(ndep)
-    rdy = [0.0] * n
-    free = [0.0] * 6
-    ready = [[] for _ in range(5)]
-    for i in range(n):
-        if not left[i]:
-            ready[eng[i]].append(i)
-    order = []
-    last = 0.0
-    for _ in range(n):
-        e, t = -1, 1e30
-        for q in range(5):
-            if ready[q]:
-                x = max(free[q], min([rdy[i] for i in ready[q]]))
-                if x < t:
-                    e, t = q, x
-        i = max([k for k in ready[e] if rdy[k] <= t + slack], key=lambda k: pr[k])
-        ready[e].remove(i)
-        f = free[e] = max(free[e], rdy[i]) + dur[i]
+def nodes(G):
+    eng, dur, lat, dby, succ, _ = G
+    eng, dur, fw, tail = list(eng), list(dur), [], [0.0] * len(eng)
+    extra, seq = [], []
+    for i in range(len(succ)):
+        seq.append(i)
         if dby[i]:
-            free[5] = max(free[5], f + 500.0) + dby[i]
-            f = free[5] + lat[i] - 500.0
-        last = max(last, f)
-        order.append(i)
-        for k, x in succ[i]:
-            if f + x > rdy[k]:
-                rdy[k] = f + x
-            left[k] -= 1
-            if not left[k]:
-                ready[eng[k]].append(k)
-    return last, order
+            seq.append(len(eng))
+            fw.append([(len(eng), 500.0)])
+            extra.append([(k, x + lat[i] - 500.0) for k, x in succ[i]])
+            eng.append(5); dur.append(dby[i]); tail.append(lat[i] - 500.0)
+        else:
+            fw.append(succ[i])
+    fw += extra
+    bw = [[] for _ in fw]
+    for i, s in enumerate(fw):
+        for k, x in s:
+            bw[k].append((i, x))
+    return eng, dur, fw, bw, tail, seq
 
 
-def replay(G, order):
-    eng, dur, lat, dby, succ, ndep, _ = G
-    rdy, free, last = [0.0] * len(eng), [0.0] * 6, 0.0
+def place(eng, dur, succ, seq, head):
+    rdy = list(head)
     end = [0.0] * len(eng)
-    for i in order:
-        e = eng[i]
-        f = end[i] = free[e] = max(free[e], rdy[i]) + dur[i]
-        if dby[i]:
-            free[5] = max(free[5], f + 500.0) + dby[i]
-            f = free[5] + lat[i] - 500.0
-        last = max(last, f)
+    st, en = [[] for _ in range(6)], [[] for _ in range(6)]
+    for i in seq:
+        s, e, t, d = st[eng[i]], en[eng[i]], rdy[i], dur[i]
+        lo = len(e)
+        while lo and e[lo - 1] > t:
+            lo -= 1
+        while lo < len(e) and s[lo] < t + d:
+            t = e[lo]
+            lo += 1
+        f = end[i] = t + d
+        s.insert(lo, t); e.insert(lo, f)
         for k, x in succ[i]:
             if f + x > rdy[k]:
                 rdy[k] = f + x
-    return last, end
+    return end
 
 
-VARIANTS = [{}, dict(gat=1.15, pe=0.6, rlat=3200, wake=200, dbw=400.0), dict(gat=1.95, sca=5.0, pe=0.45, rlat=1800)]
+def rerun(G, order, p, end, fin, why):
+    eng, dur, lat, dby, _, pred = G
+    free, who, left, q = [0.0] * 6, [-1] * 6, 6, p - 1
+    while left and q >= 0:
+        i = order[q]
+        q -= 1
+        if who[eng[i]] < 0:
+            free[eng[i]], who[eng[i]] = end[i], i
+            left -= 1
+        if dby[i] and who[5] < 0:
+            free[5], who[5] = fin[i] - lat[i] + 500.0, i
+            left -= 1
+    for q in range(p, len(order)):
+        i = order[q]
+        e = eng[i]
+        t, w = free[e], who[e]
+        for j, x in pred[i]:
+            if fin[j] + x > t:
+                t, w = fin[j] + x, j
+        f = end[i] = free[e] = t + dur[i]
+        who[e] = i
+        if dby[i]:
+            f += 500.0
+            if free[5] > f:
+                f, w = free[5], who[5]
+            free[5] = f = f + dby[i]
+            who[5] = i
+            f += lat[i] - 500.0
+        fin[i], why[i] = f, w
+    return max(fin)
+
+
+def behind(G, order, top, p, tail, moved):
+    eng, dur, lat, dby, succ, _ = G
+    nxt, td, left = [0.0] * 5, 0.0, set(range(6))
+    for i in order[top:]:
+        if eng[i] in left:
+            nxt[eng[i]] = dur[i] + tail[i]
+            left.discard(eng[i])
+        if dby[i] and 5 in left:
+            td = moved[i]
+            left.discard(5)
+        if not left:
+            break
+    for q in range(top - 1, p - 1, -1):
+        i = order[q]
+        t = 0.0
+        for k, x in succ[i]:
+            if x + dur[k] + tail[k] > t:
+                t = x + dur[k] + tail[k]
+        if dby[i]:
+            td = moved[i] = dby[i] + max(lat[i] - 500.0 + t, td)
+            t = 500.0 + td
+        if nxt[eng[i]] > t:
+            t = nxt[eng[i]]
+        tail[i] = t
+        nxt[eng[i]] = dur[i] + t
+
+
+def retry(G, order, p, hi, s, tail, limit, undo, last):
+    eng, dur, lat, dby, _, pred = G
+    end, fin, why = s
+    free, who, left, q = [0.0] * 6, [-1] * 6, 6, p - 1
+    while left and q >= 0:
+        i = order[q]
+        q -= 1
+        if who[eng[i]] < 0:
+            free[eng[i]], who[eng[i]] = end[i], i
+            left -= 1
+        if dby[i] and who[5] < 0:
+            free[5], who[5] = fin[i] - lat[i] + 500.0, i
+            left -= 1
+    reach, open_ = hi, set(eng[i] for i in order[p:hi + 1]) | {5}
+    for q in range(p, len(order)):
+        i = order[q]
+        e = eng[i]
+        t, w = free[e], who[e]
+        for j, x in pred[i]:
+            if fin[j] + x > t:
+                t, w = fin[j] + x, j
+        t = f = free[e] = t + dur[i]
+        who[e] = i
+        if dby[i]:
+            f += 500.0
+            if free[5] > f:
+                f, w = free[5], who[5]
+            free[5] = f = f + dby[i]
+            who[5] = i
+            f += lat[i] - 500.0
+            if q > hi:
+                if f == fin[i]:
+                    open_.discard(5)
+                else:
+                    open_.add(5)
+        if t != end[i] or f != fin[i]:
+            if q > hi and t + tail[i] > limit:
+                return None
+            open_.add(e)
+            if last[i] > reach:
+                reach = last[i]
+        elif q > hi:
+            open_.discard(e)
+        undo.append((i, end[i], fin[i], why[i]))
+        end[i], fin[i], why[i] = t, f, w
+        if q >= reach and not open_ - {4}:
+            break
+    return max(fin)
+
+
+def polish(gs, order, steps, temp, rnd, marks, pull, gaps):
+    n = len(order)
+    up, down = [set(j for j, _ in p) for p in gs[0][5]], [set(k for k, _ in s) for s in gs[0][4]]
+    st = [([0.0] * n, [0.0] * n, [-1] * n) for _ in gs]
+    base = [rerun(G, order, 0, *s) for G, s in zip(gs, st)]
+
+    tails = [([0.0] * n, [0.0] * n) for _ in gs]
+    value = lambda ends, w: sum((x + w * sum([s[1][i] for i in marks])) / b for x, s, b in zip(ends, st, base)) / len(gs)
+    cur, best, keep = 9.0, 1.0, list(order)
+    arcs, took, good = None, -1, n
+    for it in range(steps):
+        if arcs is None:
+            took += 1
+            if took % 24 == 0:
+                end, dur = st[0][0], gs[0][1]
+                order = sorted(order, key=lambda i: end[i] - dur[i])
+                w = pull / len(marks) * (1 - it / steps)
+                ends = [rerun(G, order, 0, *s) for G, s in zip(gs, st)]
+                cur, good, pos = value(ends, w), n, [0] * n
+                for q, i in enumerate(order):
+                    pos[i] = q
+                far_ = [max([pos[k] for k in d] + [0]) for d in down]
+            arcs = []
+            for end, fin, why in st:
+                for i in (fin.index(max(fin)), marks[rnd(len(marks))]):
+                    while why[i] >= 0:
+                        if why[i] not in up[i]:
+                            arcs.append((why[i], i))
+                        i = why[i]
+        u, v = arcs[rnd(len(arcs))]
+        far = rnd([0, 0, 3, 10, 40][rnd(5)] + 1)
+        side = rnd(2)
+        if rnd(3) < gaps:
+            (end, fin, _), G = st[it % len(gs)], gs[it % len(gs)]
+            one, holes = (v, []) if side else (u, [])
+            e, nb = G[0][one], u if side else v
+            stop = max([pos[j] for j in up[v]] + [-1]) if side else min([pos[k] for k in down[u]] + [n])
+            for q in (range(pos[u] - 1, stop - 8, -1) if side else range(pos[v] + 1, min(n, stop + 8))):
+                i = order[q]
+                if q >= 0 and G[0][i] == e:
+                    a, b = (i, nb) if side else (nb, i)
+                    if end[b] - G[1][b] - end[a] > 0.3 * G[1][one]:
+                        holes.append(pos[u] - pos[b] if side else pos[a] - pos[v])
+                    nb = i
+            if holes:
+                far = holes[rnd(len(holes))]
+        if side:
+            lo, hi = max(0, pos[u] - far), pos[v]
+            mark = {v}
+            for q in range(hi - 1, lo - 1, -1):
+                if not mark.isdisjoint(down[order[q]]):
+                    mark.add(order[q])
+            seg = order[lo:hi + 1]
+            seg = [i for i in seg if i in mark] + [i for i in seg if i not in mark]
+        else:
+            lo, hi = pos[u], min(n - 1, pos[v] + far)
+            mark = {u}
+            for q in range(lo + 1, hi + 1):
+                if not mark.isdisjoint(up[order[q]]):
+                    mark.add(order[q])
+            seg = order[lo:hi + 1]
+            seg = [i for i in seg if i not in mark] + [i for i in seg if i in mark]
+        was = order[lo:hi + 1]
+        if seg == was:
+            continue
+        if good > hi + 1:
+            for G, tl in zip(gs, tails):
+                behind(G, order, good, hi + 1, *tl)
+            good = hi + 1
+        room = temp * (1 - it / steps) * rnd(1000) / 500
+        order[lo:hi + 1] = seg
+        new, undo = [], []
+        for G, s, tl, x, b in zip(gs, st, tails, ends, base):
+            undo.append([])
+            new.append(retry(G, order, lo, hi, s, tl[0], x + (room * len(gs) + 0.002) * b, undo[-1], far_))
+            if new[-1] is None:
+                break
+        x = value(new, w) if new[-1] else 9.0
+        if x <= cur + room:
+            cur, ends, arcs, good = x, new, None, max(good, hi + 1)
+            for q in range(lo, hi + 1):
+                pos[order[q]] = q
+                for j in up[order[q]]:
+                    if far_[j] < q:
+                        far_[j] = q
+            last = sum(x / b for x, b in zip(ends, base)) / len(gs)
+            if last < best:
+                best, keep = last, list(order)
+        else:
+            order[lo:hi + 1] = was
+            for (end, fin, why), log in zip(st, undo):
+                for i, a, b, c in log:
+                    end[i], fin[i], why[i] = a, b, c
+    return keep
+
+
 _PLAN = {}
 
 
@@ -654,30 +1070,25 @@ def plan():
             state[0] = (state[0] * 6364136223846793005 + 1442695040888963407) % (1 << 64)
             return (state[0] >> 33) % m
 
-        score = lambda order: sum(replay(G, order)[0] for G in gs) / len(gs)
-        pr = list(gs[0][6])
-        order = schedule(gs[0], pr, COST["slack"])[1]
-        best = score(order)
-        cur, first = [best], [1e30]
-        for it in range(OPT["iters"]):
-            p2 = list(pr)
-            for _ in range(1 + rnd(3)):
-                a = rnd(n)
-                b = min(n, a + [1, 3, 10, 30, 100][rnd(5)])
-                d = (rnd(2001) - 1000) * [0.8, 3.0, 12.0][rnd(3)]
-                en = rnd(5) - 2
-                for i in range(a, b):
-                    if en < 0 or gs[0][0][i] == en:
-                        p2[i] += d
-            t2, o2 = schedule(gs[0], p2, COST["slack"])
-            if t2 > first[0] + 2000.0:
-                continue
-            s2 = score(o2)
-            if s2 <= cur[0]:
-                cur[0], first[0], pr = s2, t2, p2
-                if s2 <= best:
-                    best, order = s2, o2
-        _PLAN["ops"], _PLAN["order"], _PLAN["best"], _PLAN["gs"] = ops, order, best, gs
+        eng, dur, fw, bw, tail, seq = nodes(gs[OPT["aim"][0]])
+        zero = [0.0] * len(eng)
+        key = [o["at"] for o in ops] + [0.0] * (len(eng) - n)
+        for i in seq:
+            for k, _ in fw[i]:
+                key[k] = max(key[k], key[i] + 1e-6)
+        seq = sorted(seq, key=lambda i: key[i])
+        end = place(eng, dur, fw, seq, zero)
+        if not OPT["fill"]:
+            end = [key[i] + dur[i] for i in range(n)]
+        for _ in range(OPT["passes"] - 1):
+            back = place(eng, dur, bw, sorted(seq, key=lambda i: -end[i]), tail)
+            end = place(eng, dur, fw, sorted(seq, key=lambda i: -back[i]), zero)
+        order = sorted(range(n), key=lambda i: end[i] - dur[i])
+        aim, marks = [gs[k] for k in OPT["aim"]], [i for i in range(n) if ops[i]["kind"] == "rem"]
+        time = lambda o: math.prod(rerun(G, o, 0, [0.0] * n, [0.0] * n, [-1] * n) for G in aim)
+        order = min([polish(aim, order, OPT["steps"], OPT["heat"], rnd, marks, OPT["pull"], OPT["gaps"]) for _ in range(OPT["tries"])], key=time)
+        order = polish(aim, order, OPT["more"], OPT["heat"] / 2, rnd, marks, OPT["pull"] / 2, OPT["gaps"])
+        _PLAN["ops"], _PLAN["order"], _PLAN["gs"] = ops, order, gs
     return _PLAN["ops"], _PLAN["order"]
 
 
@@ -694,23 +1105,9 @@ def _masks(core, nxt, prv, topo):
 
 def rank_program(g, core, T, topo):
     rank = T.rank_of(core)
-    cores = list(T.cores)
-    helpers = {}
-    for c in cores:
-        helpers[c] = [x for x in topo.cores_of(c) if x not in cores and x not in helpers.values()][0]
     if rank is None:
-        for c in cores:
-            if helpers[c] == core:
-                ops, order = plan()
-                folds = [ops[i]["args"][2] for i in order if ops[i]["kind"] == "fold"]
-                rid, pid, _ = topo.addr(c)
-                for f, b in enumerate(folds):
-                    g.wait_ge(T.sem["ha%d" % f], 3 * (len(topo.engines(c, core)) // 4))
-                    blk = _ap(T, A("yb", b, b + KV))
-                    g.remote_dma(blk, blk, T.sem["ha%d" % f], T.sem["hl%d" % f], pid, rid, topo.mask(core, c))
-                for f in range(len(folds)):
-                    g.wait_ge(T.sem["hl%d" % f], len(topo.engines(core, c)))
         return
+    cores = list(T.cores)
     n = len(cores)
     nb = {1: cores[(rank + 1) % n], -1: cores[(rank - 1) % n]}
     eng_out = _masks(core, nb[1], nb[-1], topo)
@@ -720,8 +1117,9 @@ def rank_program(g, core, T, topo):
     Q = {"v": g.vector, "a": g.scalar, "p": g.tensor, "g": g, "s": g.sync}
     cnt = {"cv": 0, "ca": 0, "cp": 0, "cg": 0}
     done, seen, total = {}, {}, {}
-    nd, nr, nf = [0], [0], [0]
-    helper = helpers.get(core)
+    nd, nr = [0], [0]
+    P = lambda a: _ap(T, a)
+    heads = lambda a: T[a[0]][0:128:16, a[1]:a[2]]
     for i in order:
         op = ops[i]
         eng, kind, ar = op["eng"], op["kind"], op["args"]
@@ -737,7 +1135,6 @@ def rank_program(g, core, T, topo):
             if seen.get((eng, s), 0) < c:
                 q.wait_ge(T.sem[s], c)
                 seen[(eng, s)] = c
-        P = lambda a: _ap(T, a)
         if kind == "rem":
             sa, sl = "ar%d" % nr[0], "lo%d" % nr[0]
             nr[0] += 1
@@ -751,24 +1148,14 @@ def rank_program(g, core, T, topo):
             done[i] = {"ar": (sa, arrive), "lo": (sl, leave)}
             total[sa], total[sl] = arrive, leave
             continue
-        if kind == "fold":
-            sa, sl = "ha%d" % nf[0], "hl%d" % nf[0]
-            nf[0] += 1
-            y, p, b = ar
-            rid, pid, _ = topo.addr(helper)
-            en = topo.engines(core, helper)
-            w = len(en) // 4
-            g.remote_dma_fused([RemoteDMATransfer(dst_ids=[DstId(rid=rid, pnc=pid)], dma_engine_mask=sum(1 << x for x in en[(k + 1) * w:(k + 2) * w]),
-                                                  remote_sem=T.sem[sa], srcs=[P(A("yb", y + k * V, y + k * V + V)), P(A("sp", p, p + V))],
-                                                  dsts=[P(A("yb", b + k * V, b + k * V + V))], alu_op=3) for k in range(3)], local_sem=T.sem[sl])
-            back = len(topo.engines(helper, core))
-            done[i] = {"ar": (sa, back), "lo": (sl, 3 * w)}
-            total[sa], total[sl] = back, 3 * w
-            continue
-        if kind == "dma":
+        if kind in ("dma", "cat", "uncat"):
             s = "d%d" % nd[0]
             nd[0] += 1
-            if ar[2]:
+            if kind == "cat":
+                q.dma_start(heads(ar[0]), P(ar[1])).then_inc(T.sem[s], 16)
+            elif kind == "uncat":
+                q.dma_start(P(ar[0]), heads(ar[1])).then_inc(T.sem[s], 16)
+            elif ar[2]:
                 q.dma_start(P(ar[0]), P(ar[1]), accum_op=ALU.add, max_dma_last_dim=4096 if _dt(ar[0]) == BF else 8192).then_inc(T.sem[s], 16)
             else:
                 q.dma_start(P(ar[0]), P(ar[1])).then_inc(T.sem[s], 16)
@@ -792,7 +1179,9 @@ def rank_program(g, core, T, topo):
             else:
                 ins = q.activation(P(ar[0]), P(ar[1]), ar[2], bias=P(ar[3]), scale=P(ar[4]))
         elif kind == "mm":
-            ins = q.matmul(P(ar[0]), P(ar[1]), P(ar[2]), ar[3], ar[4])
+            for out, terms, first, last in ar:
+                for j, (l, r) in enumerate(terms):
+                    ins = q.matmul(P(out), P(l), P(r), first and j == 0, last and j == len(terms) - 1)
         elif kind == "sel":
             ins = q.affine_select(P(ar[0]), P(ar[1]), ar[2], ar[3], ar[4], ar[5], ar[6])
         else:

import math
from concourse.bass import DstId, RemoteDMATransfer
from concourse.mybir import AluOpType as ALU, ActivationFunctionType as ACT

V, H, KV, M = 1024, 256, 3072, 1536
SW = M + 16
SO = SW - V
ZW = KV + 8
RW = 64 + 2 * H
EPS = 2.0 ** -30
SC = [1.0, 8.0, -1 / 64, 1 / 2, 4.0, -1 / 32, 1 / 32, -1 / 8, 1 / 8, 2.0, -1 / 16, 1 / 16, 1 / 4]

F32, BF, I32, U16, F16 = "float32", "bfloat16", "int32", "uint16", "float16"
_SB = {
    "wt": (4 * KV, BF), "yb": (10 * KV, BF), "zz": (2 * ZW, F32), "acc": (KV, F32), "rc": (KV, F32),
    "sp": (9 * SW - 2 * SO, BF), "aa": (9 * V, BF), "zg": (KV, F32), "rg": (V, F32), "rl": (2 * RW, F32),
    "sb": (H, F32), "sg": (2 * H, BF), "sf": (H, BF), "cap": (V, F32), "mm": (2 * V, F16), "qq": (2 * V, BF),
    "dr": (V, BF), "ls": (V, BF), "cn": (V, BF), "one16": (512, BF),
    "ii32": (256, F32), "ii16": (256, BF), "ids": (128 * len(SC), BF), "hf16": (128, F16),
    "h16": (144, BF), "k16": (144, BF), "pd32": (256, F32), "pp16": (256, BF), "pd16": (256, BF),
    "srci": (192, I32), "dlyi": (192, I32), "sndi": (32, I32), "ioi": (192, I32), "cli": (4, I32),
    "clf": (4, F32), "srcf": (192, F32), "fd": (192, F32), "fa": (192, F32), "t1": (192, F32),
    "t2": (192, F32), "la": (192, F32), "lb": (192, F32),
    "swp": (192, BF), "d8": (192, BF), "eag": (192, BF), "x8": (192, BF), "cod": (192, BF),
    "lt1": (192, U16), "lg": (192, U16), "lp": (192, U16), "lsn": (32, U16), "lsp": (32, U16), "lr": (64, U16), "lbs": (192, U16),
    "lba": (384, U16), "lbb": (384, U16), "lb3": (384, U16),
}
_PS = {"pv": 1024, "pk": 1024, "pq": 1024, "px0": 512, "px1": 512}
_HW = {"w": BF, "drive": BF, "loss": BF}
SCRATCH = {k: ("sbuf", [128, n], d) for k, (n, d) in _SB.items()}
SCRATCH.update({k: ("psum", [128, n], F32) for k, n in _PS.items()})
NDMA, NREM = 90, 20
SEMAPHORES = ["cv", "ca", "cp", "cg"] + ["d%d" % i for i in range(NDMA)] + ["ar%d" % i for i in range(NREM)] + ["lo%d" % i for i in range(NREM)]

COST = dict(cyc=0.83, gat=1.56, sca=3.5, pe=0.42, vfix=60, afix=90, pfix=25, wake=120, same=50, c16=1.0,
            dissue=900, hissue=60, dlat=2000, dbw=550.0, rissue=400, rlat=2400)
VARIANTS = [dict(cyc=0.9, gat=1.4, sca=3.0, pe=0.45, rlat=2800, wake=150), dict(cyc=1.2, gat=2.0, sca=5.5, pe=0.6, dbw=450.0)]
OPT = dict(seed=0, tries=4, steps=22000, more=40000, heat=0.0015, pull=0.3, aim=[0, 1], passes=1,
           tail="vaa", own="ppv", spike=["vvvv", "aaaa", "aaav"], wt_eng="vadd", vote=["bssm", "ssss"],
           ysplit=[[0] * 4] * 3, afix="vvv", sc_eng="aaaaaaa", ids="g", xhalf=True, fin="m", whole=[False, False, False],
           gaps=2, g4=8.0, sat=7.0, mat=5.3, big="a", late=[1, 2], cend=1, rps=False, rpos=3, cpos=[2, 5], fpos=[2, 2], wsplit=[True, True, True], fill=True, defer=True, rb={2: [0, 1, 2]}, parts=[1, 1, 2],
           beat=[10.3, 14.7, 11.5], zbeat=[0, 13.5, 13.5],
           send=[5.4, 6.4, 5.4], rat=[6.2, 5.0], x4=[(8.0, 13.1, 13.0), (8.0, 13.1, 13.0), (7.0, 12.0, 0)], xat=[10.3, 11.3, 13.2],
           vat=[[(7.0, 8.0, 9.0), (5.3, 6.2, 7.1)], [(12.8, 13.7, 14.0), (5.3, 6.2, 7.1)]],
           gam=[(-1.7, -0.8, 3.6), (2.4, 2.5, 2.6)], fat=[7.0, 12.9, 13.8], bat=[(1.6, 3.0, 1.6, 3.5, 0), (0.6, 1.7, 0.9, 1.7, 1.0)])


def A(name, lo=0, hi=None, step=1):
    if hi is None:
        hi = _SB[name][0] if name in _SB else _PS[name]
    return (name, lo, hi, step)


def IND(win, off):
    return ("@", win, off)


def _n(a):
    if a[0] == "@":
        return 16 * _n(a[2])
    return (a[2] - a[1] + a[3] - 1) // a[3]


def _dt(a):
    if a[0] == "@":
        return _dt(a[1])
    return _SB[a[0]][1] if a[0] in _SB else _HW.get(a[0], F32)


def _isap(a):
    return isinstance(a, tuple)


def _parts(a):
    return [a[1], a[2]] if a[0] == "@" else [a]


def _ap(T, a):
    if not _isap(a):
        return a
    if a[0] == "@":
        return _ap(T, a[1]).indirect(_ap(T, a[2]))
    return T[a[0]][:, a[1]:a[2]] if a[3] == 1 else T[a[0]][:, a[1]:a[2]:a[3]]


def build_ops(C, O):
    ops, clock = [], [0.0]

    def add(eng, kind, args, outs, ins, dur, lat=0.0, dby=0.0):
        rd, wr = [], []
        for a in ins:
            if _isap(a):
                rd += _parts(a)
        for a in outs:
            if a[0] == "@":
                wr.append(a[1]); rd.append(a[2])
            else:
                wr.append(a)
        clock[0] += 0.001
        ops.append(dict(eng=eng, kind=kind, args=args, rd=rd, wr=wr, dur=dur, lat=lat, dby=dby, at=clock[0]))

    def at(x):
        clock[0] = x

    def vdur(out, ins, two):
        n = _n(out)
        if out[0] == "@":
            return C["vfix"] + n * C["sca"] * C["cyc"]
        if any(a[0] == "@" for a in ins):
            return C["vfix"] + n * C["gat"] * C["cyc"]
        narrow = all(_dt(a) in (BF, F16, U16) for a in [out] + ins)
        f = (2.0 if two and all(a[0] in _SB for a in ins) else 1.0) * (0.5 if narrow else 1.0)
        if two and narrow:
            f = C["c16"]
        return C["vfix"] + max(64, n * f) * C["cyc"]

    def tt(out, a, b, op):
        add("v", "tt", (out, a, b, op), [out], [a, b], vdur(out, [a, b], True))

    def ts(out, a, s1, op0, s2=None, op1=None):
        add("v", "ts", (out, a, s1, s2, op0, op1), [out], [a, s1, s2], vdur(out, [a], False))

    def cp(out, a):
        add("v", "cp", (out, a), [out], [a], vdur(out, [a], False))

    def ms(out, c):
        add("v", "ms", (out, c), [out], [], vdur(out, [], False))

    def act(out, a, func, bias=0.0, scale=1.0, extra=0.0):
        n = _n(out)
        f = C["sca"] if out[0] == "@" else C["gat"] if a[0] == "@" else 1.0
        add("a", "act", (out, a, func, bias, scale), [out], [a, bias, scale], C["afix"] + max(64, n * f) * C["cyc"] + extra)

    def gat(eng, out, win, off):
        if eng == "a":
            act(out, IND(win, off), ACT.Copy)
        else:
            cp(out, IND(win, off))

    def group(out, terms, first=True, last=True):
        dur = sum(C["pfix"] + max(64, _n(r)) * (4 if _dt(r) == F32 else 1) * C["pe"] for _, r in terms)
        add("p", "mm", [(out, terms, first, last)], [out], [a for t in terms for a in t], dur)

    def both(bank, terms, first=True, last=True):
        for h in range(2):
            group(half(bank, 0, h), [(l, half(n, b, h if n != "one16" else 0)) for l, n, b in terms], first, last)
        o = ops.pop()
        for k in ("args", "rd", "wr", "dur"):
            ops[-1][k] += o[k]

    def mm(out, lhs, rhs, start=True, stop=True):
        group(out, [(lhs, rhs)], start, stop)

    def dma(eng, out, a, acc=False):
        by = _n(out) * 128 * (2 if _dt(out) == BF else 4)
        add(eng, "dma", (out, a, acc), [out], [a, out] if acc else [a], C["dissue"] if eng == "g" else C["hissue"],
            C["dlat"], by * (2 if acc else 1) / C["dbw"])

    def cat(kind, out, a):
        add("s", kind, (out, a), [out], [a], C["hissue"], C["dlat"], 1000.0 if _dt(a) == F32 else 600.0)

    def rem(tr):
        add("g", "rem", tr, [t[2] for t in tr], [s for t in tr for s in t[1]], C["rissue"], C["rlat"] - 600.0, 600.0)

    def gp(kind, out, ins, args):
        add("g", kind, args, [out], ins, 170 + 2 * _n(out) * C["cyc"])

    def sel(out, a, pattern, op, base, cm, other=0.0):
        gp("sel", out, [a], (out, a, pattern, op, other, base, cm))

    def iota(out, pattern, base, cm):
        gp("iota", out, [], (out, pattern, base, cm))

    def fill(out, c):
        iota(out, [[0, _n(out)]], c, 0)

    def ID(s):
        i = SC.index(s)
        return A("ids", 128 * i, 128 * i + 128)

    def half(name, base, h):
        return A(name, base + 512 * h, base + 512 * h + 512)

    def third(name, base, k):
        return A(name, base + V * k, base + V * k + V)

    spos = lambda e, s: max(0, (4 + s if e % 2 == 0 else 4 - s) * SW - SO)
    apos = lambda e, t: (0 if t == 0 else 4 * (e % 2) + t) * V
    YB = [[0, 1, 2, 3], [4, 5, 6, 7], [2, 1, 0, 8]]
    PB = [[4, 5, 6, 7], [3, 2, 8, 9]]
    ypos = lambda e, t: YB[e][t - 1] * KV
    mpos = lambda t: V if t else 0
    I32F, SH32 = A("ii32", 0, 128), A("ii32", 16, 144)
    SH16 = A("ii16", 112, 240)
    p0 = spos(0, 0)

    def wrap(out, hbuf, src, base, n=KV):
        group(out, [(A(hbuf, 15 - i, 143 - i), A(src, base + i, base + n, 16)) for i in range(16)])
        ops[-1]["rd"] = [A(hbuf), A(src, base, base + n)]

    def rowwise(out, idx, width, more, tmp):
        lo, hi = A("ioi", 0, _n(idx)), A("dlyi", 0, _n(idx))
        ts(lo, idx, 15, ALU.bitwise_and)
        ts(hi, idx, 4, ALU.logical_shift_right)
        ts(tmp, lo, float(width), ALU.mult)
        tt(tmp, tmp, hi, ALU.add)
        if more:
            tt(tmp, tmp, more, ALU.add)
        cp(out, tmp)

    def send_spikes(e, s, T):
        p = spos(e, s)
        at(T)
        gat("a", A("sg", 0, H), A("sp", p, p + V), A("lsn", 0, 16))
        gat("a", A("sg", H, 2 * H), A("sp", p, p + V), A("lsn", 16, 32))
        mm(A("px0", 0, H), SH16, A("sg", 0, H))
        act(A("sf"), A("px0", 0, H), ACT.Copy)
        rem([(1, [A("sf")], A("sp", p + V, p + V + H)), (-1, [A("sg", H, 2 * H)], A("sp", p + V + H, p + M))])

    def weights(t):
        o, a, s = (t - 1) * KV, 3 * KV, 2.0 ** (t - 4)
        if O["wt_eng"][t - 1] == "d":
            dma("s", A("wt", o, o + KV), A("wt", o - KV, o))
            dma("g", A("wt", o, o + KV), A("wt", o - KV, o), True)
            return
        for k in range(3):
            if O["wt_eng"][t - 1] == "v":
                ts(third("wt", o, k), third("wt", a, k), EPS, ALU.max, s, ALU.mult)
            else:
                act(third("wt", o, k), third("wt", a, k), ACT.Identity, EPS * s, s)

    def scaled(some):
        for s in some:
            if O["ids"] == "g":
                sel(ID(s), A("k16", 0, 128), [[-1, 128]], ALU.not_equal, 0, 1, s)
            else:
                act(ID(s), A("ii32", 0, 128), ACT.Identity, 0.0, s)

    def start():
        dma("s", A("dr"), A("drive", 0, V)); dma("a", A("sndi"), A("snd", 0, 32))
        dma("s", A("srci"), A("src", 0, 192)); dma("a", A("dlyi"), A("dly", 0, 192))
        for k in range(3):
            dma("s", third("wt", 3 * KV, k), third("w", 0, k))
        dma("a", A("ls"), A("loss", 0, V))
        ms(A("pd32"), 1.0)
        sel(A("ii32"), A("pd32"), [[0, 2], [-1, 128]], ALU.is_equal, 0, 1)
        cp(A("ii16"), A("ii32"))
        fill(A("k16"), 0)
        fill(A("sp", p0 + M, p0 + SW), 0)
        cp(A("lsn"), A("sndi"))
        ts(A("sp", p0, p0 + V), A("dr"), 1.0, ALU.is_ge, 32.0, ALU.mult)
        send_spikes(0, 0, 1.0)
        scaled(SC[:4])
        ts(A("t1"), A("srci"), 1536.0, ALU.is_ge, -1536.0, ALU.mult)
        tt(A("srcf"), A("srci"), A("t1"), ALU.add)
        ts(A("t2"), A("dlyi"), 1.0, ALU.subtract, float(SW), ALU.mult)
        tt(A("fd"), A("srcf"), A("t2"), ALU.add)
        ts(A("lt1"), A("fd"), float(M), ALU.min)
        weights(1)
        ts(A("hf16"), A("ii16", 0, 128), 0.5, ALU.mult)
        ts(third("mm", 0, 0), A("dr"), 1.0, ALU.min)
        iota(A("cli", 0, 1), [[0, 1]], 0, 1)
        for b in (5, 6, 7, 3, 2, 1):
            fill(A("sp", b * SW + M - SO, b * SW + SW - SO), 0)

    def more_lists():
        tt(A("fa"), A("srcf"), A("t2"), ALU.subtract)
        ts(A("lg"), A("fa"), float(SW), ALU.add)
        ts(A("cli", 1, 2), A("cli", 0, 1), 15, ALU.bitwise_and)
        ts(A("clf", 0, 1), A("cli", 1, 2), 128.0, ALU.subtract)
        ts(A("x8"), A("dlyi"), 128.0, ALU.mult, A("clf", 0, 1), ALU.add)
        ts(A("la"), A("dlyi"), 1.0, ALU.subtract, float(ZW), ALU.mult)
        rowwise(A("lp"), A("srci"), 192, A("la"), A("px1", 0, 192))
        rowwise(A("lsp"), A("sndi"), 64, None, A("px1", 256, 288))

    def constants():
        fill(A("one16"), 1)
        fill(A("h16"), 0)
        sel(A("h16", 15, 144, 16), A("one16", 0, 9), [[-16, 9]], ALU.is_ge, 0, 1)
        sel(A("h16", 15, 144, 16), A("h16", 15, 144, 16), [[16, 9]], ALU.is_ge, 15, -1)
        sel(A("k16", 15, 144, 16), A("one16", 0, 9), [[-16, 9]], ALU.is_equal, 0, 1)
        sel(A("pd32", 0, 128), A("pd32", 0, 128), [[-2, 64], [1, 2]], ALU.is_equal, -1, 1)
        sel(A("pd32", 128, 256), A("pd32", 128, 256), [[-4, 32], [2, 2], [-1, 2]], ALU.is_equal, -2, 1)
        tt(A("pp16"), A("pd32"), A("ii32"), ALU.add)
        tt(A("pd32"), A("pd32"), A("ii32"), ALU.subtract)
        cp(A("pd16"), A("pd32"))
        fill(A("rl", 0, 64), 0); fill(A("rl", RW, RW + 64), 0)

    def f_open(e, t, T):
        at(T - 1.5)
        both("pv", [(ID(1.0), "dr", 0), (ID(-2.0 ** (t - 7)), "sp", spos(e, t - 1)), (A("hf16"), "mm", mpos(t - 1))], True, False)

    def f_gather(e, t, T):
        s, y, w = 2.0 ** (4 - t), ypos(e, t), (t - 1) * KV
        if t == 1:
            win, lst = A("sp", p0, p0 + SW), "lt1"
        else:
            lo = min(spos(e, t - 1), spos(e, t - 2))
            win, lst = A("sp", lo, lo + 2 * SW), "lg"
        for k in range(3):
            yk, wk, lk = third("yb", y, k), third("wt", w, k), A(lst, 64 * k, 64 * k + 64)
            at(T + 1.4 * k)
            if k < O["ysplit"][e][t - 1]:
                gat("a", yk, win, lk)
                at(T + 3.0)
                tt(yk, yk, wk, ALU.min)
            else:
                tt(yk, IND(win, lk), wk, ALU.min)
            at(T + 1.4 * k + 1.5)
            both("pv", [(ID(s), "yb", y + k * V)], False, k == 2)

    def smode(e, t):
        return "v" if O["spike"][e][t - 1] == "m" and t == 4 else O["spike"][e][t - 1]

    def f_spike(e, t, T):
        s, p, mode = 2.0 ** (4 - t), spos(e, t), smode(e, t)
        at(T + 4.35)
        for h in range(2):
            if mode == "v":
                ts(half("sp", p, h), half("pv", 0, h), 1.0, ALU.is_ge, 2.0 * s, ALU.mult)
            elif mode == "m":
                ts(half("mm", mpos(t), h), half("pv", 0, h), 1.0, ALU.min)
                ts(half("sp", p, h), half("mm", mpos(t), h), 1.0, ALU.is_ge, 2.0 * s, ALU.mult)
            else:
                q = half("qq", t % 2 * V, h)
                act(q, half("pv", 0, h), ACT.Sign, 2.0 ** -12 - 1.0)
                if mode == "x":
                    ts(half("sp", p, h), q, s, ALU.mult, s, ALU.add)
                else:
                    act(half("sp", p, h), q, ACT.Identity, s, s)
        if t < 4:
            send_spikes(e, t, T + O["send"][e])
        if e < 2 and O["vote"][e][t - 1] in "sbc" and mode in "vm":
            act(third("qq", 0, t % 2), A("pv"), ACT.Sign, 2.0 ** -12 - 1.0)

    def f_keep(e, t, T):
        at(T + 5.3)
        if t < 4 and smode(e, t) != "m":
            ts(third("mm", mpos(t), 0), A("pv"), 1.0, ALU.min)

    def f_slope(e, t, T, T2):
        s, y, a = 2.0 ** (4 - t), ypos(e, t), third("aa", apos(e, t), 0)
        late = e == 2 and t < 4 and t in O["late"]
        small = t == 4 and e < 2 or late
        for h in range(2):
            at(T + h)
            bank = A("px%d" % (0 if late else h))
            terms = [(ID(1.0), half("dr", 0, h))] + [(ID(s), half("yb", y + k * V, h)) for k in range(3)]
            if t == 4:
                at(T - 1.4 + 0.1 * h)
                group(bank if small else half("pq", 0, h), terms[:3], True, False)
                at(T - 0.05 + 0.1 * h)
                group(bank if small else half("pq", 0, h), terms[3:], False, True)
            else:
                group(bank if small else half("pq", 0, h), terms + [(ID(4.0 / s), half("sp", spos(e, t), h))])
            if small:
                act(half("aa", a[1], h), bank, ACT.Identity, s * ((211 if t < 4 else 195) - 1 / 64), -2.0 * s)
        at(T + 2.5)
        if not small:
            act(a, A("pq"), ACT.Identity, s * ((211 if t < 4 else 195) - 1 / 64), -2.0 * s)
        at(T2)
        if O["afix"][e] == "v":
            ts(a, a, 192.0 * s, ALU.subtract, 0.5 * s, ALU.max)
        else:
            act(a, a, ACT.Relu, -192.5 * s)
            act(a, a, ACT.Identity, 0.5 * s)

    def f_vote(e, t, Ts):
        y, p, b, vote = ypos(e, t), spos(e, t), PB[e][t - 1] * KV, O["vote"][e][t - 1]
        for k in range(3):
            at(Ts[k])
            o, yk = third("yb", b, k), third("yb", y, k)
            if vote == "s" or (vote == "b" and k > 0) or (vote == "c" and k > 1):
                tt(o, yk, third("qq", 0, t % 2), ALU.mult)
            elif vote == "m":
                tt(o, yk, A("sp", p, p + V), ALU.min)
            else:
                bank = "pk" if e == 0 else "pq"
                both(bank, [(ID(1 / 8), "yb", y + k * V), (ID(-1 / 8), "sp", p)])
                act(o, A(bank), ACT.Relu, 0.0, 2.0 ** (7 - t))

    def diffs(e, bank):
        mm(A(bank, 0, 192), A("pd32", 128 * e, 128 * e + 128), A("srcf"))
        mm(A(bank, 256, 448), A("pd16", 128 * e, 128 * e + 128), A("x8"))
        act(A("t1"), A(bank, 0, 192), ACT.Copy)
        act(A("d8"), A(bank, 256, 448), ACT.Copy)

    def exchange(e, T):
        vb = 8 * KV
        for k in range(3):
            bank = ("pq", "pk", "pv")[k]
            for h in range(2):
                terms = []
                for t in range(1, 5):
                    if t == 4:
                        at(T + (0.2, 3.1, 6.5)[k] + 0.1 * h)
                        group(half(bank, 0, h), terms, True, False)
                        at(T + O["vat"][e][1][k] + 1.0 + 0.1 * h)
                        terms = []
                    b, y = half("yb", PB[e][t - 1] * KV + k * V, h), half("yb", ypos(e, t) + k * V, h)
                    vote = O["vote"][e][t - 1]
                    if vote == "s" or (vote == "b" and k > 0) or (vote == "c" and k > 1):
                        terms += [(ID(2.0 ** -t), b)]
                    elif vote == "m":
                        terms += [(ID(-2.0 ** -t), y), (ID(2.0 ** (1 - t)), b)]
                    else:
                        terms += [(ID(2.0 ** -t), y), (ID(-1 / 8), b)]
                group(half(bank, 0, h), terms, False, True)
                if O["xhalf"]:
                    act(half("yb", vb + k * V, h), half(bank, 0, h), ACT.Sign, -EPS / 32)
            if not O["xhalf"]:
                act(third("yb", vb, k), A(bank), ACT.Sign, -EPS / 32)
            at(T + O["vat"][e][1][k] + 2.3)
            wrap(A("px0", 64 * k, 64 * k + 64), "h16", "yb", vb + k * V, V)
        X0, X1 = A("px0", 0, 192), A("px0", 256, 448)
        at(T + O["xat"][0])
        ts(A("eag"), X0, 1.0, ALU.is_ge)
        mm(X1, A("pp16", 128 * e, 128 * e + 128), A("eag"))
        at(T + O["xat"][1])
        ts(X1, X1, 1.5, ALU.is_ge)
        tt(X0, X1, A("t1"), ALU.mult)
        tt(A("fd"), X0, A("fd"), ALU.add)
        ts(A("lt1"), A("fd"), float(M), ALU.min)
        at(T + O["xat"][2])
        tt(A("cod"), X1, A("d8"), ALU.mult)
        tt(A("fa"), X0, A("fa"), ALU.add)
        if e == 0:
            tt(A("srcf"), X0, A("srcf"), ALU.add)
            act(A("swp"), X1, ACT.Copy)
            cp(A("lg"), A("fd"))
        else:
            ts(A("lg"), A("fa"), float(SW), ALU.add)

    def back_lists(e):
        o = 192 * (e % 2)
        ts(A("lb3", o, o + 192), A("la"), float(KV), ALU.min)
        cp(A("lba", o, o + 192), A("la"))
        cp(A("lbb", o, o + 192), A("lb"))

    def invert_in():
        fill(A("rg"), 0)
        for c in range(6):
            dma("s", third("zz", 0, c), A("rg"))
        fill(A("zz", 6 * V, 2 * ZW), 0)
        for c in range(6):
            iota(half("zg", 0, c), [[1, 512]], 64 + 512 * c, 0)

    def scatter(some):
        for c in some:
            dst = IND(A("zz"), A("lp", 32 * c, 32 * c + 32)) if c < 6 else IND(A("rg"), A("lsp"))
            if O["sc_eng"][c] == "a":
                act(dst, half("zg", 0, c % 6), ACT.Silu, extra=1300 if "a" not in O["sc_eng"][:c] else 0)
            else:
                cp(dst, half("zg", 0, c % 6))

    def invert_out():
        P0 = A("px1", 0, 192)
        cat("uncat", A("la"), A("zz", 0, KV))
        cat("uncat", A("lb"), A("zz", ZW, ZW + KV))
        cat("uncat", A("t2", 0, 64), A("rg"))
        act(P0, A("lb"), ACT.Identity, -64.0)
        tt(P0, P0, A("la"), ALU.add)
        cp(A("srci"), P0)
        ts(P0, A("lb"), 8.0, ALU.is_ge, float(ZW), ALU.mult)
        tt(A("la"), P0, A("srci"), ALU.add)
        ts(P0, A("lb"), 8.0, ALU.is_lt, float(ZW), ALU.mult)
        tt(A("lb"), P0, A("srci"), ALU.add)
        back_lists(0)
        cp(A("ioi", 0, 64), A("t2", 0, 64))
        cp(A("lr"), A("ioi", 0, 64))
        rowwise(A("lbs"), A("srci"), 192, None, P0)
        dma("s", A("yb", 9 * KV, 10 * KV), A("w", 0, KV))

    def follow_a(e, T, Ts):
        ab, gb = 9 * KV, (8 if e == 0 else 3) * KV
        at(T)
        if e == 1:
            mm(A("pq", 0, 192), A("pd16", 0, 128), A("cod"))
            tt(A("swp"), A("pq", 0, 192), A("swp"), ALU.mult)
            tt(A("cod"), A("cod"), A("swp"), ALU.add)
        cat("cat", A("yb", ab, ab + KV), A("cod"))
        for k in range(3):
            at(Ts[k])
            gat("a", third("yb", gb, k), A("yb", ab, ab + KV), A("lbs", 64 * k, 64 * k + 64))

    def follow_b(e, T):
        bank, gb = "pq", (8 if e == 0 else 3) * KV
        P0, P1 = A(bank, 0, 192), A(bank, 256, 448)
        at(T - 2.0)
        wrap(P0, "k16", "yb", gb)
        at(T)
        act(A("eag"), P0, ACT.Identity, 3072.0)
        tt(A("la"), P0, A("la"), ALU.add)
        tt(A("lb"), P0, A("lb"), ALU.add)
        for n, c in (("la", ZW / 128 - 1), ("lb", -ZW / 128 - 1)):
            act(P1, A("eag"), ACT.Identity, -3072.0 * c, c)
            tt(A(n), P1, A(n), ALU.add)
        back_lists(e + 1)
        if e == 0:
            diffs(1, bank)

    def count(e, bank="pq"):
        for h in range(2):
            terms = [(ID(2.0 ** (s - 5)), half("sp", spos(x, s), h)) for x in ([1, 2] if e == 2 and O["cpos"][1] > 4 else [e]) for s in range(5)]
            group(half(bank, 0, h if bank == "pq" else 0), terms + ([(ID(1.0), half("cn", 0, h))] if e else []))
            if bank != "pq":
                act(half("cn", 0, h), A(bank), ACT.Copy)
        if bank == "pq":
            act(A("cn"), A("pq"), ACT.Copy)
        if e == 2:
            dma("g", A("cnt", 0, V), A("cn"))

    def recip_a():
        for k in range(3):
            act(third("rc", 0, k), third("wt", 3 * KV, k), ACT.Ln, extra=0 if k else 1500)
            ops[-1]["rd"].append(A("lr"))
        for k in range(3):
            act(third("rc", 0, k), third("rc", 0, k), ACT.Exp, 0.0, -1.0, extra=0 if k else 1500)
            if k == 0:
                ops[-1]["rd"].append(A("rc"))

    def recip_b(k, bank):
        r = third("rc", 0, k)
        both(bank, [(ID(1.0), "wt", 3 * KV + k * V)])
        tt(A(bank), A(bank), r, ALU.mult)
        act(A(bank), A(bank), ACT.Identity, 2.0, -1.0)
        tt(r, A(bank), r, ALU.mult)

    lbuf = lambda e, t: "pk" if e < 2 else ("pv", "pq")[t % 2]
    land = lambda e, t: ((3 * e + 3 - t) % 2) * RW

    def finish(z, add_z, Z):
        for k in range(3):
            a, bank = third("acc", 0, k), "pk"
            if add_z == "d":
                at(Z + O["gam"][1][k])
                dma("g", a, third("zz", z, k), True)
            at(Z + O["fat"][k] - 2.0)
            if O["rps"]:
                act(A(bank), third("rc", 0, k), ACT.Copy)
            else:
                for h in range(2):
                    mm(half(bank, 0, h), I32F, half("acc", k * V, h))
            at(Z + O["fat"][k])
            tt(a, A(bank), a if O["rps"] else third("rc", 0, k), ALU.mult)
            dma("s", third("gam", 0, k), a)

    def b_z(e, t, Z):
        z, y = (t % 2) * ZW, ypos(e, t)
        for k in range(3):
            at(Z - 2.7 + 0.9 * k)
            tt(third("zz", z, k), third("yb", y, k), A(lbuf(e, t)), ALU.mult)

    def b_gamma(e, t, Z):
        z, y, fin = (t % 2) * ZW, ypos(e, t), O["fin"]
        if e == 2 and t == 1 and fin == "m":
            b = 9 * KV
            at(Z - 8.0)
            for k in range(3):
                if O["big"] == "v":
                    ts(third("yb", b, k), third("yb", y, k), 2.0 ** 40, ALU.mult)
                else:
                    act(third("yb", b, k), third("yb", y, k), ACT.Identity, 0.0, 2.0 ** 40)
            at(Z + 0.05)
            act(A("pk"), A(lbuf(e, t)), ACT.Identity, 0.0, 2.0 ** (t - 4))
            at(Z + 1.5)
            for k in range(3):
                tt(third("rc", 0, k), third("yb", b, k), A("pk"), ALU.min)
                dma("g", third("gam", 0, k), third("rc", 0, k), True)
        elif e == 0 and t == 4:
            at(Z + 3.6)
            dma("s", A("acc"), A("zz", z, z + KV))
        elif e == 2 and t == (2 if fin == "m" else 1):
            finish(z, "d" if fin == "m" else fin, Z)
        else:
            for k in range(3):
                at(Z + O["gam"][e == 2][k])
                dma("g", third("acc", 0, k), third("zz", z, k), True)

    def b_first(e, Z):
        x = lbuf(e, 4)
        at(Z - 6.0)
        both(x, [(ID(1.0), "ls", 0)])
        at(Z - 4.5)
        tt(A(x), A(x), third("aa", apos(e, 4), 0), ALU.mult)
        tt(A(x), A(x), third("sp", spos(e, 4), 0), ALU.min)
        b_z(e, 4, Z)

    def b_lists(e, t):
        o = 192 * (e % 2)
        lst = "lb3" if t == 3 else "lbb" if t % 2 == 0 else "lba"
        return (A("zz", 0, ZW) if t == 3 else A("zz")), lambda c0, c1: A(lst, o + c0, o + c1)

    def b_wires(e, t, Z):
        (win, L), r, ew = b_lists(e, t), land(e, t), O["tail"][0] if e == 2 else "a"
        at(Z + 0.1)
        if O["wsplit"][e]:
            gat("a", A("zg", V, V + H), win, L(64, 80))
            gat(ew, A("zg", M + V, M + V + H), win, L(160, 176))
            gat("a", A("zg", V + H, M), win, L(80, 96))
            gat(ew, A("zg", M + V + H, KV), win, L(176, 192))
        else:
            gat("a", A("zg", V, M), win, L(64, 96))
            gat("a", A("zg", M + V, KV), win, L(160, 192))
        at(Z + O["bat"][e == 2][0])
        mm(A("px1", 0, H), SH32, A("zg", V, V + H), True, False)
        mm(A("px1", 0, H), SH32, A("zg", M + V, M + V + H), False, True)
        at(Z + O["bat"][e == 2][1])
        act(A("sb"), A("px1", 0, H), ACT.Copy)
        rem([(-1, [A("sb")], A("rl", r + 64, r + 64 + H)),
             (1, [A("zg", V + H, M), A("zg", M + V + H, KV)], A("rl", r + 64 + H, r + RW))])
        ops[-1]["rd"].append(A("rg"))

    def b_cap(e, t, Z):
        at(Z + (0.5 if e < 2 else 4.5))
        cap = A("cap") if e < 2 else A(lbuf(e, t + 1))
        tt(cap, A(lbuf(e, t + 1)), third("sp", spos(e, t), 0), ALU.max)
        if t == 0:
            act(cap, cap, ACT.Identity, 0.0, 1 / 16)

    def b_own(e, t, Z):
        (win, L), own, b, x = b_lists(e, t), O["own"][e], O["bat"][e == 2], lbuf(e, t)
        at(Z + b[0] + 0.1)
        lift = [(ID(2.0), "one16", 0), (ID(-2.0 ** (t - 4)), "sp", spos(e, t))] if t == 0 else []
        both(x, lift + [(ID(1.0), "ls", 0)], True, False)
        n = O["parts"][e]
        for c in range(n):
            w = V // n
            a0, a1 = A("zg", c * w, c * w + w), A("zg", M + c * w, M + c * w + w)
            at(Z + b[2] + c * b[4])
            gat("a", a0, win, L(c * w // 16, (c * w + w) // 16))
            at(Z + b[3] + c * b[4])
            l1 = L(96 + c * w // 16, 96 + (c * w + w) // 16)
            if own == "v":
                tt(a1, IND(win, l1), a0, ALU.add)
            else:
                gat(O["tail"][1] if e == 2 else "a", a1, win, l1)
        if own == "d":
            dma("g", A("zg", M, M + V), A("zg", 0, V), True)
        if own == "p":
            at(Z + b[2] + 1.5)
            for h in range(2):
                mm(half(x, 0, h), I32F, half("zg", 0, h), False, False)
        at(Z + b[3] + 1.5)
        for h in range(2):
            mm(half(x, 0, h), I32F, half("zg", M, h), False, False)

    def b_back(e, t, R):
        r = land(e, t)
        for h in range(2):
            both = e == 2 and O["tail"][2] == "v"
            at(R + (0 if both else 0.8 * h))
            gat("v" if both and h else "a", half("rg", 0, h), A("rl", r, r + RW), A("lr", 32 * h, 32 * h + 32))
            at(R + 0.95 + 0.9 * h)
            mm(half(lbuf(e, t), 0, h), I32F, half("rg", 0, h), False, True)

    def b_lam(e, t, Z):
        a = apos(e, t)
        at(Z - 4.6)
        if e < 2 and O["whole"][e]:
            tt(A("pk"), A("pk"), third("aa", a, 0), ALU.mult)
            tt(A("pk"), A("pk"), A("cap"), ALU.min)
        elif e < 2:
            for h in range(2):
                tt(half("pk", 0, h), half("pk", 0, h), half("aa", a, h), ALU.mult)
                tt(half("pk", 0, h), half("pk", 0, h), half("cap", 0, h), ALU.min)
        else:
            for h in range(2):
                tt(half("rg", 0, h), half(lbuf(e, t), 0, h), half("aa", a, h), ALU.mult)
                tt(half(lbuf(e, t) if t else "cap", 0, h), half(lbuf(e, t + 1), 0, h), half("rg", 0, h), ALU.min)
                if t == 0:
                    dma("s", half("lam", 0, h), half("cap", 0, h))
        if t > 0:
            b_z(e, t, Z)

    def b_next(e, t, Z):
        if t > (0 if e == 2 else 1):
            b_wires(e, t - 1, Z)
        if (e, t) == (2, 4) and O["defer"]:
            b_lam(1, 1, Z + 5.6)
            b_gamma(1, 1, Z + 5.6)
            Z += O["g4"]
        b_gamma(e, t, Z)
        if (e, t) == (2, 4) and O["defer"]:
            Z -= O["g4"]
        if t > (0 if e == 2 else 1):
            b_cap(e, t - 1, Z)
            b_own(e, t - 1, Z)

    def slope0():
        act(A("aa", 0, V), A("dr"), ACT.Identity, 195 - 1 / 64, -2.0)
        ts(A("aa", 0, V), A("aa", 0, V), 192.0, ALU.subtract, 0.5, ALU.max)

    start()
    at(2.0)
    scaled(SC[4:])
    invert_in()
    extras = {1: [(O["mat"], more_lists), (6.4, lambda: weights(2)), (7.8, constants)] + [(O["sat"] + 1.6 * c, lambda c=c: scatter([c])) for c in range(7)],
              2: [(6.3, lambda: weights(3)), (11.0, lambda: diffs(0, "px1"))],
              3: [(6.3, lambda: weights(4)), (6.4, invert_out)]}
    T, Z = 8.0, 0.0
    for e in range(3):
        for t in range(1, 5):
            u, beat = 4 - t if e and t < 4 else 0, O["beat"][e]
            f_open(e, t, T)
            if u:
                b_back(e - 1, u, Z + O["rat"][0])
                Z += O["zbeat"][e]
            f_gather(e, t, T)
            if t == 4:
                f_slope(e, t, T + 4.4, T + O["x4"][e][0])
            f_spike(e, t, T)
            f_keep(e, t, T)
            if e and t == O["fpos"][e - 1]:
                follow_b(e - 1, T + 6.2)
            if t < 4 and not (e == 2 and t in O["late"]):
                f_slope(e, t, T + 7.5, T + beat + 6.05)
            if u and not (e == 2 and u == 1 and O["defer"]):
                b_lam(e - 1, u, Z)
                b_next(e - 1, u, Z)
            if e and t == O["fpos"][e - 1] - 1:
                follow_a(e - 1, T + 5.5, [T + 8.5, T + 10.1, T + 10.2])
            for x, f in extras.get(t, []) if e == 0 else []:
                at(T + x)
                f()
            if e < 2:
                f_vote(e, t, [T + x for x in O["vat"][e][t == 4]])
            if e and t == O["cpos"][e - 1]:
                at(T + 11.0)
                count(e - 1)
            if 4 * e + t == O["rpos"] + 8:
                at(T + 8.0)
                recip_a()
            for k in O["rb"].get(10 + t, []) if e == 2 else []:
                at(T + 6.4)
                recip_b(k, "pq")
            if e == 2 and t == 1:
                at(T + 6.3)
                slope0()
            if t < 4:
                T += beat
        if e < 2:
            exchange(e, T)
        Z = T + O["x4"][e][1]
        b_first(e, Z)
        b_next(e, 4, Z)
        T += O["x4"][e][2]
    for t in (3, 2, 1, 0):
        if t in O["late"]:
            f_slope(2, t, Z - 5.0, Z + 4.0)
        if t == O["cend"]:
            at(Z + 3.0)
            count(2, "px0")
        for k in O["rb"].get(t, []):
            at(Z + 2.5 + k)
            recip_b(k, "pk")
        b_back(2, t, Z + O["rat"][1])
        Z += 12.0
        b_lam(2, t, Z)
        if t:
            b_next(2, t, Z)
    return ops


def link(ops):
    hist = {}
    for i, op in enumerate(ops):
        dep = {}
        acc = [(a, False) for a in op["rd"]] + [(a, True) for a in op["wr"]]
        for a, w in acc:
            ps = a[0] in _PS
            lo, hi = (a[1] // 512 * 512, (a[2] + 511) // 512 * 512) if ps else (a[1], a[2])
            for (j, l2, h2, w2, s2, o2) in hist.get(a[0], []):
                if l2 >= hi or h2 <= lo:
                    continue
                if a[3] > 1 and s2 == a[3] and (o2 - a[1]) % s2 and not ps:
                    continue
                landing = op["kind"] == "rem" and w
                if landing:
                    continue
                if w or w2 or (ps and ops[j]["eng"] != op["eng"]):
                    kind = "lo" if (ops[j]["kind"] == "rem" and not w2) else "ar"
                    dep.setdefault(j, set()).add(kind)
        op["dep"] = dep
        for a, w in acc:
            ps = a[0] in _PS
            lo, hi = (a[1] // 512 * 512, (a[2] + 511) // 512 * 512) if ps else (a[1], a[2])
            hl = hist.setdefault(a[0], [])
            if (w or ps) and (a[3] == 1 or ps) and op["kind"] != "rem":
                hl[:] = [x for x in hl if not (x[1] >= lo and x[2] <= hi and w and x[0] != i)]
            if w and op["kind"] == "rem":
                hl[:] = [x for x in hl if not (x[1] >= lo and x[2] <= hi)]
            hl.append((i, lo, hi, w, a[3], a[1]))


def graph(ops, C):
    n = len(ops)
    succ, pred, above = [[] for _ in ops], [[] for _ in ops], [0] * n
    for i, op in enumerate(ops):
        for j in sorted(op["dep"], reverse=True):
            if not above[i] >> j & 1:
                same = ops[j]["eng"] == op["eng"] and not ops[j]["lat"]
                x = C["wake"] if not same else 0.0 if op["eng"] == "p" else C["same"]
                succ[j].append((i, x)); pred[i].append((j, x))
                above[i] |= above[j] | 1 << j
    return (["vapgs".index(o["eng"]) for o in ops], [o["dur"] for o in ops], [o["lat"] for o in ops], [o["dby"] for o in ops], succ, pred)


def nodes(G):
    eng, dur, lat, dby, succ, _ = G
    eng, dur, fw, tail = list(eng), list(dur), [], [0.0] * len(eng)
    extra, seq = [], []
    for i in range(len(succ)):
        seq.append(i)
        if dby[i]:
            seq.append(len(eng))
            fw.append([(len(eng), 500.0)])
            extra.append([(k, x + lat[i] - 500.0) for k, x in succ[i]])
            eng.append(5); dur.append(dby[i]); tail.append(lat[i] - 500.0)
        else:
            fw.append(succ[i])
    fw += extra
    bw = [[] for _ in fw]
    for i, s in enumerate(fw):
        for k, x in s:
            bw[k].append((i, x))
    return eng, dur, fw, bw, tail, seq


def place(eng, dur, succ, seq, head):
    rdy = list(head)
    end = [0.0] * len(eng)
    st, en = [[] for _ in range(6)], [[] for _ in range(6)]
    for i in seq:
        s, e, t, d = st[eng[i]], en[eng[i]], rdy[i], dur[i]
        lo = len(e)
        while lo and e[lo - 1] > t:
            lo -= 1
        while lo < len(e) and s[lo] < t + d:
            t = e[lo]
            lo += 1
        f = end[i] = t + d
        s.insert(lo, t); e.insert(lo, f)
        for k, x in succ[i]:
            if f + x > rdy[k]:
                rdy[k] = f + x
    return end


def rerun(G, order, p, end, fin, why):
    eng, dur, lat, dby, _, pred = G
    free, who, left, q = [0.0] * 6, [-1] * 6, 6, p - 1
    while left and q >= 0:
        i = order[q]
        q -= 1
        if who[eng[i]] < 0:
            free[eng[i]], who[eng[i]] = end[i], i
            left -= 1
        if dby[i] and who[5] < 0:
            free[5], who[5] = fin[i] - lat[i] + 500.0, i
            left -= 1
    for q in range(p, len(order)):
        i = order[q]
        e = eng[i]
        t, w = free[e], who[e]
        for j, x in pred[i]:
            if fin[j] + x > t:
                t, w = fin[j] + x, j
        f = end[i] = free[e] = t + dur[i]
        who[e] = i
        if dby[i]:
            f += 500.0
            if free[5] > f:
                f, w = free[5], who[5]
            free[5] = f = f + dby[i]
            who[5] = i
            f += lat[i] - 500.0
        fin[i], why[i] = f, w
    return max(fin)


def behind(G, order, top, p, tail, moved):
    eng, dur, lat, dby, succ, _ = G
    nxt, td, left = [0.0] * 5, 0.0, set(range(6))
    for i in order[top:]:
        if eng[i] in left:
            nxt[eng[i]] = dur[i] + tail[i]
            left.discard(eng[i])
        if dby[i] and 5 in left:
            td = moved[i]
            left.discard(5)
        if not left:
            break
    for q in range(top - 1, p - 1, -1):
        i = order[q]
        t = 0.0
        for k, x in succ[i]:
            if x + dur[k] + tail[k] > t:
                t = x + dur[k] + tail[k]
        if dby[i]:
            td = moved[i] = dby[i] + max(lat[i] - 500.0 + t, td)
            t = 500.0 + td
        if nxt[eng[i]] > t:
            t = nxt[eng[i]]
        tail[i] = t
        nxt[eng[i]] = dur[i] + t


def retry(G, order, p, hi, s, tail, limit, undo, last):
    eng, dur, lat, dby, _, pred = G
    end, fin, why = s
    free, who, left, q = [0.0] * 6, [-1] * 6, 6, p - 1
    while left and q >= 0:
        i = order[q]
        q -= 1
        if who[eng[i]] < 0:
            free[eng[i]], who[eng[i]] = end[i], i
            left -= 1
        if dby[i] and who[5] < 0:
            free[5], who[5] = fin[i] - lat[i] + 500.0, i
            left -= 1
    reach, open_ = hi, set(eng[i] for i in order[p:hi + 1]) | {5}
    for q in range(p, len(order)):
        i = order[q]
        e = eng[i]
        t, w = free[e], who[e]
        for j, x in pred[i]:
            if fin[j] + x > t:
                t, w = fin[j] + x, j
        t = f = free[e] = t + dur[i]
        who[e] = i
        if dby[i]:
            f += 500.0
            if free[5] > f:
                f, w = free[5], who[5]
            free[5] = f = f + dby[i]
            who[5] = i
            f += lat[i] - 500.0
            if q > hi:
                if f == fin[i]:
                    open_.discard(5)
                else:
                    open_.add(5)
        if t != end[i] or f != fin[i]:
            if q > hi and t + tail[i] > limit:
                return None
            open_.add(e)
            if last[i] > reach:
                reach = last[i]
        elif q > hi:
            open_.discard(e)
        undo.append((i, end[i], fin[i], why[i]))
        end[i], fin[i], why[i] = t, f, w
        if q >= reach and not open_ - {4}:
            break
    return max(fin)


def polish(gs, order, steps, temp, rnd, marks, pull, gaps):
    n = len(order)
    up, down = [set(j for j, _ in p) for p in gs[0][5]], [set(k for k, _ in s) for s in gs[0][4]]
    st = [([0.0] * n, [0.0] * n, [-1] * n) for _ in gs]
    base = [rerun(G, order, 0, *s) for G, s in zip(gs, st)]

    tails = [([0.0] * n, [0.0] * n) for _ in gs]
    value = lambda ends, w: sum((x + w * sum([s[1][i] for i in marks])) / b for x, s, b in zip(ends, st, base)) / len(gs)
    cur, best, keep = 9.0, 1.0, list(order)
    arcs, took, good = None, -1, n
    for it in range(steps):
        if arcs is None:
            took += 1
            if took % 24 == 0:
                end, dur = st[0][0], gs[0][1]
                order = sorted(order, key=lambda i: end[i] - dur[i])
                w = pull / len(marks) * (1 - it / steps)
                ends = [rerun(G, order, 0, *s) for G, s in zip(gs, st)]
                cur, good, pos = value(ends, w), n, [0] * n
                for q, i in enumerate(order):
                    pos[i] = q
                far_ = [max([pos[k] for k in d] + [0]) for d in down]
            arcs = []
            for end, fin, why in st:
                for i in (fin.index(max(fin)), marks[rnd(len(marks))]):
                    while why[i] >= 0:
                        if why[i] not in up[i]:
                            arcs.append((why[i], i))
                        i = why[i]
        u, v = arcs[rnd(len(arcs))]
        far = rnd([0, 0, 3, 10, 40][rnd(5)] + 1)
        side = rnd(2)
        if rnd(3) < gaps:
            (end, fin, _), G = st[it % len(gs)], gs[it % len(gs)]
            one, holes = (v, []) if side else (u, [])
            e, nb = G[0][one], u if side else v
            stop = max([pos[j] for j in up[v]] + [-1]) if side else min([pos[k] for k in down[u]] + [n])
            for q in (range(pos[u] - 1, stop - 8, -1) if side else range(pos[v] + 1, min(n, stop + 8))):
                i = order[q]
                if q >= 0 and G[0][i] == e:
                    a, b = (i, nb) if side else (nb, i)
                    if end[b] - G[1][b] - end[a] > 0.3 * G[1][one]:
                        holes.append(pos[u] - pos[b] if side else pos[a] - pos[v])
                    nb = i
            if holes:
                far = holes[rnd(len(holes))]
        if side:
            lo, hi = max(0, pos[u] - far), pos[v]
            mark = {v}
            for q in range(hi - 1, lo - 1, -1):
                if not mark.isdisjoint(down[order[q]]):
                    mark.add(order[q])
            seg = order[lo:hi + 1]
            seg = [i for i in seg if i in mark] + [i for i in seg if i not in mark]
        else:
            lo, hi = pos[u], min(n - 1, pos[v] + far)
            mark = {u}
            for q in range(lo + 1, hi + 1):
                if not mark.isdisjoint(up[order[q]]):
                    mark.add(order[q])
            seg = order[lo:hi + 1]
            seg = [i for i in seg if i not in mark] + [i for i in seg if i in mark]
        was = order[lo:hi + 1]
        if seg == was:
            continue
        if good > hi + 1:
            for G, tl in zip(gs, tails):
                behind(G, order, good, hi + 1, *tl)
            good = hi + 1
        room = temp * (1 - it / steps) * rnd(1000) / 500
        order[lo:hi + 1] = seg
        new, undo = [], []
        for G, s, tl, x, b in zip(gs, st, tails, ends, base):
            undo.append([])
            new.append(retry(G, order, lo, hi, s, tl[0], x + (room * len(gs) + 0.002) * b, undo[-1], far_))
            if new[-1] is None:
                break
        x = value(new, w) if new[-1] else 9.0
        if x <= cur + room:
            cur, ends, arcs, good = x, new, None, max(good, hi + 1)
            for q in range(lo, hi + 1):
                pos[order[q]] = q
                for j in up[order[q]]:
                    if far_[j] < q:
                        far_[j] = q
            last = sum(x / b for x, b in zip(ends, base)) / len(gs)
            if last < best:
                best, keep = last, list(order)
        else:
            order[lo:hi + 1] = was
            for (end, fin, why), log in zip(st, undo):
                for i, a, b, c in log:
                    end[i], fin[i], why[i] = a, b, c
    return keep


_PLAN = {}


def plan():
    if not _PLAN:
        gs = []
        for v in VARIANTS:
            C = dict(COST, **v)
            ops = build_ops(C, OPT)
            link(ops)
            gs.append(graph(ops, C))
        n = len(ops)
        state = [OPT["seed"] * 7919 + 12345]

        def rnd(m):
            state[0] = (state[0] * 6364136223846793005 + 1442695040888963407) % (1 << 64)
            return (state[0] >> 33) % m

        eng, dur, fw, bw, tail, seq = nodes(gs[OPT["aim"][0]])
        zero = [0.0] * len(eng)
        key = [o["at"] for o in ops] + [0.0] * (len(eng) - n)
        for i in seq:
            for k, _ in fw[i]:
                key[k] = max(key[k], key[i] + 1e-6)
        seq = sorted(seq, key=lambda i: key[i])
        end = place(eng, dur, fw, seq, zero)
        if not OPT["fill"]:
            end = [key[i] + dur[i] for i in range(n)]
        for _ in range(OPT["passes"] - 1):
            back = place(eng, dur, bw, sorted(seq, key=lambda i: -end[i]), tail)
            end = place(eng, dur, fw, sorted(seq, key=lambda i: -back[i]), zero)
        order = sorted(range(n), key=lambda i: end[i] - dur[i])
        aim, marks = [gs[k] for k in OPT["aim"]], [i for i in range(n) if ops[i]["kind"] == "rem"]
        time = lambda o: math.prod(rerun(G, o, 0, [0.0] * n, [0.0] * n, [-1] * n) for G in aim)
        order = min([polish(aim, order, OPT["steps"], OPT["heat"], rnd, marks, OPT["pull"], OPT["gaps"]) for _ in range(OPT["tries"])], key=time)
        order = polish(aim, order, OPT["more"], OPT["heat"] / 2, rnd, marks, OPT["pull"] / 2, OPT["gaps"])
        _PLAN["ops"], _PLAN["order"], _PLAN["gs"] = ops, order, gs
    return _PLAN["ops"], _PLAN["order"]


def _masks(core, nxt, prv, topo):
    en, ep = topo.engines(core, nxt), topo.engines(core, prv)
    first, second = (nxt, prv) if len(en) <= len(ep) else (prv, nxt)
    e1, e2 = topo.engines(core, first), topo.engines(core, second)
    k = len(set(e1) | set(e2)) // 2
    k = 1 << int(math.log2(min(k, len(e1))))
    s1 = e1[:k]
    s2 = [x for x in e2 if x not in s1][:k]
    return {first: s1, second: s2}


def rank_program(g, core, T, topo):
    rank = T.rank_of(core)
    if rank is None:
        return
    cores = list(T.cores)
    n = len(cores)
    nb = {1: cores[(rank + 1) % n], -1: cores[(rank - 1) % n]}
    eng_out = _masks(core, nb[1], nb[-1], topo)
    arrive = len(_masks(nb[1], cores[(rank + 2) % n], core, topo)[core]) + len(_masks(nb[-1], core, cores[(rank - 2) % n], topo)[core])
    leave = len(eng_out[nb[1]]) + len(eng_out[nb[-1]])
    ops, order = plan()
    Q = {"v": g.vector, "a": g.scalar, "p": g.tensor, "g": g, "s": g.sync}
    cnt = {"cv": 0, "ca": 0, "cp": 0, "cg": 0}
    done, seen, total = {}, {}, {}
    nd, nr = [0], [0]
    P = lambda a: _ap(T, a)
    heads = lambda a: T[a[0]][0:128:16, a[1]:a[2]]
    for i in order:
        op = ops[i]
        eng, kind, ar = op["eng"], op["kind"], op["args"]
        q = Q[eng]
        need = {}
        for j, kinds in op["dep"].items():
            if eng == "p" and ops[j]["eng"] == "p":
                continue
            for kd in kinds:
                s, c = done[j][kd]
                need[s] = max(need.get(s, 0), c)
        for s, c in need.items():
            if seen.get((eng, s), 0) < c:
                q.wait_ge(T.sem[s], c)
                seen[(eng, s)] = c
        if kind == "rem":
            sa, sl = "ar%d" % nr[0], "lo%d" % nr[0]
            nr[0] += 1
            trs = []
            for to, srcs, dst in ar:
                rid, pid, _ = topo.addr(nb[to])
                mask = sum(1 << x for x in eng_out[nb[to]])
                trs.append(RemoteDMATransfer(dst_ids=[DstId(rid=rid, pnc=pid)], dma_engine_mask=mask, remote_sem=T.sem[sa],
                                             srcs=[P(s) for s in srcs], dsts=[P(dst)], alu_op=1 if len(srcs) > 1 else 0))
            g.remote_dma_fused(trs, local_sem=T.sem[sl])
            done[i] = {"ar": (sa, arrive), "lo": (sl, leave)}
            total[sa], total[sl] = arrive, leave
            continue
        if kind in ("dma", "cat", "uncat"):
            s = "d%d" % nd[0]
            nd[0] += 1
            if kind == "cat":
                q.dma_start(heads(ar[0]), P(ar[1])).then_inc(T.sem[s], 16)
            elif kind == "uncat":
                q.dma_start(P(ar[0]), heads(ar[1])).then_inc(T.sem[s], 16)
            elif ar[2]:
                q.dma_start(P(ar[0]), P(ar[1]), accum_op=ALU.add, max_dma_last_dim=4096 if _dt(ar[0]) == BF else 8192).then_inc(T.sem[s], 16)
            else:
                q.dma_start(P(ar[0]), P(ar[1])).then_inc(T.sem[s], 16)
            done[i] = {"ar": (s, 16)}
            total[s] = 16
            continue
        if kind == "tt":
            ins = q.tensor_tensor(P(ar[0]), P(ar[1]), P(ar[2]), ar[3])
        elif kind == "ts":
            if ar[5] is None:
                ins = q.tensor_scalar(P(ar[0]), P(ar[1]), P(ar[2]), None, ar[4])
            else:
                ins = q.tensor_scalar(P(ar[0]), P(ar[1]), P(ar[2]), P(ar[3]), ar[4], ar[5])
        elif kind == "cp":
            ins = q.tensor_copy(P(ar[0]), P(ar[1]))
        elif kind == "ms":
            ins = q.memset(P(ar[0]), ar[1])
        elif kind == "act":
            if ar[3] == 0.0 and ar[4] == 1.0:
                ins = q.activation(P(ar[0]), P(ar[1]), ar[2])
            else:
                ins = q.activation(P(ar[0]), P(ar[1]), ar[2], bias=P(ar[3]), scale=P(ar[4]))
        elif kind == "mm":
            for out, terms, first, last in ar:
                for j, (l, r) in enumerate(terms):
                    ins = q.matmul(P(out), P(l), P(r), first and j == 0, last and j == len(terms) - 1)
        elif kind == "sel":
            ins = q.affine_select(P(ar[0]), P(ar[1]), ar[2], ar[3], ar[4], ar[5], ar[6])
        else:
            ins = q.iota(P(ar[0]), ar[1], ar[2], ar[3], allow_small_or_imprecise_dtypes=_dt(ar[0]) != I32)
        s = "c" + eng
        cnt[s] += 1
        ins.then_inc(T.sem[s], 1)
        done[i] = {"ar": (s, cnt[s])}
        total[s] = cnt[s]
    for s, c in total.items():
        if max(seen.get((e, s), 0) for e in Q) < c:
            g.sync.wait_ge(T.sem[s], c)
